import numpy as np, ml_dtypes
CORES = [48,51,52,55]
N = 4
BF = ml_dtypes.bfloat16
def gentries(a):
    return np.ascontiguousarray(a.reshape(8, 16, -1).transpose(0, 2, 1)).reshape(8, -1)
def gtable(e):
    e = np.asarray(e); return np.ascontiguousarray(e.reshape(8, -1, 16).transpose(0, 2, 1)).reshape(128, -1).astype(np.int32)
NW, E, EP, C, U = 4096, 256, 3, 4, 2
def at(a, d):
    return np.roll(a, -1, axis=0) if d == 2 else a
def pick(a, ix):
    return np.take_along_axis(a, ix.reshape(8, 1, -1), 2).reshape(8, 16, E, 16)
def children(L, last, st, b):
    n = np.where(st, np.minimum(C, 15 - last), 0); end = np.add.accumulate(n, axis=-1); m = np.arange(16)
    k = np.add.reduce((end[..., None, :] <= m[:, None]).astype(np.int64), axis=-1)
    real = k < 16; k = np.minimum(k, 15)
    bb = np.where(real, np.take_along_axis(last, k, 2) + 1 + m - np.take_along_axis(end - n, k, 2), 15)
    Lk = np.take_along_axis(L, k, 2); Bb = np.take_along_axis(b, bb, 2)
    return np.where(real, (((Lk * Bb) >> 5) + Lk + 37 * Bb) & (NW - 1), NW - 1), bb, k
def grow(w, tau, b):
    names, par, votes = [[], [], []], [[], [], []], []
    for r in range(N):
        L = b[r]; last = np.zeros((8, E, 16), np.int64) + np.arange(16); p = np.zeros((8, E, 16), np.int64); c = np.zeros((8, E), np.int64)
        for d in range(3):
            q = (r + d) % N
            st = np.count_nonzero(pick(at(w[q], d), L) >= at(tau[q], d)[:, :, None, d:d + 1], axis=1) >= 9
            c = c + np.count_nonzero(st, axis=-1); names[d].append(L); par[d].append(p)
            if d < 2: L, last, p = children(L, last, st, b[r])
        votes.append(c)
    return names, par, np.stack(votes)
def winnow(w, names, fp, fn):
    new = []
    for q in range(N):
        bad = np.zeros((8, NW), bool); miss = np.zeros((8, NW), bool)
        for d in range(3):
            r = (q - d) % N; ix = names[d][r][:, :, :U]
            h = np.zeros(ix.shape, np.int64) + ((np.arange(8) + (d == 2)) % 8)[:, None, None]
            for flag, hit in ((fp, bad), (fn, miss)):
                on = np.zeros(ix.shape, bool) | flag[r][:, :, None]
                hit[h[on], ix[on]] = True
        fac = np.where(miss, 2.0, np.where(bad, 0.5, 1.0)).astype(np.float32)
        v = np.minimum(np.maximum(w[q] * fac[:, None, :], np.float32(0.25)), np.float32(4.0)); v[:, :, NW - 1] = 0
        new.append(v)
    return np.stack(new)
def bf(a):
    return np.asarray(a).astype(BF).astype(np.float32)
def parts(rng, off=0.8):
    f = 0.5 + 0.75 * rng.random((128, NW))
    t0 = bf(np.exp2(0.8 * rng.random((N, 8, 16, 3)) - 0.4)); up = rng.integers(0, 4, t0.shape)
    tau = np.where(up < 2, t0, np.where(up == 2, t0 * np.float32(1.0 + 2.0 ** -12), np.nextafter(t0, np.float32(8.0)))).astype(np.float32)
    z = off * (2.0 * rng.random((N, 8, 1, 1), dtype=np.float32) - 1.0) + 3.2 * rng.random((N, 8, 1, NW), dtype=np.float32) - 1.6 + 1.2 * rng.random((N, 8, 16, NW), dtype=np.float32) - 0.6
    w = np.where(rng.random((N, 8, 16, NW), dtype=np.float32) < 0.1, np.take_along_axis(t0, rng.integers(0, 3, (N, 8, 1, NW)), 3), np.exp2(z))
    w = bf(np.minimum(np.maximum(w, 0.25), 4.0)); w[..., NW - 1] = 0
    b = rng.integers(0, NW - 1, (EP, N, 8, E, 16))
    x = 0.5 + 0.5 * rng.random((N, 128, EP * E))
    return f, w, b, x, tau
def tune(rng, w, tau, b, codes, share):
    lab, ask = [], []; codes = np.broadcast_to(codes, (EP - 1, N, 8, E))
    for t in range(EP - 1):
        names, par, c = grow(w, tau, b[t]); code = codes[t]
        near = c + rng.integers(0, 2, c.shape)
        loose = np.where(rng.random(c.shape) < 0.7, c + rng.integers(-2, 4, c.shape), rng.integers(1, 49, c.shape))
        ends = np.where(rng.random(c.shape) < 0.7, rng.choice(np.array([1, 48]), c.shape), near)
        a = np.where(code == 0, loose, np.where(code == 1, c, np.where(code == 2, c + 1, np.where(code == 3, near, ends))))
        a = np.minimum(np.maximum(a, 1), 48)
        y = np.where((code == 1) | (code == 3), 0, np.where(code == 2, 1, (rng.random(c.shape) < share).astype(np.int64)))
        lab.append(y); ask.append(a)
        if t < EP - 2: w = winnow(w, names, (c >= a) & (y == 0), (c < a) & (y == 1))
    return np.stack(lab), np.stack(ask)
def pack(rng, f, w, b, x, tau, code, share):
    lab, ask = tune(rng, w, tau, b, code, share)
    f = np.array(f); f[:, NW - 1] = 0
    flat = lambda a: np.ascontiguousarray(a.transpose(1, 2, 0, 3).reshape(N, 8, -1)).astype(np.int32)
    return {"ft": np.stack([f.astype(BF)] * N), "wt": np.ascontiguousarray(w.reshape(N, 128, NW)).astype(BF),
            "bn": np.stack([gtable(b[:, r].transpose(1, 0, 2, 3).reshape(8, -1)) for r in range(N)]), "xv": x.astype(BF),
            "tau": np.ascontiguousarray(tau.reshape(N, 128, 3)).astype(np.float32), "lab": flat(lab), "ask": flat(ask)}
def setup_inputs(rng):
    f, w, b, x, tau = parts(rng)
    return pack(rng, f, w, b, x, tau, np.zeros((N, 8, E), np.int64), rng.choice(np.array([0.15, 0.3, 0.5]), (N, 8, 1)))
def setup_inputs_spread(rng):
    f, w, b, x, tau = parts(rng)
    x = x * np.exp2(rng.integers(-1, 2, (N, 1, EP * E)))
    b = np.minimum(((NW - 1) * rng.random(b.shape) ** 3).astype(np.int64), NW - 2)
    w = bf(np.exp2(4.0 * rng.random(w.shape, dtype=np.float32) - 2.0)); w[..., NW - 1] = 0
    return pack(rng, f, w, b, x, tau, np.zeros((N, 8, E), np.int64), rng.choice(np.array([0.05, 0.3, 0.6]), (N, 8, 1)))
def setup_inputs_ends(rng):
    f, w, b, x, tau = parts(rng)
    f = np.where(rng.random(f.shape) < 0.5, 0.5, 1.25); x = np.where(rng.random(x.shape) < 0.5, 0.25, 2.0)
    w = np.where(rng.random(w.shape) < rng.choice(np.array([0.0, 0.5, 1.0]), (N, 8, 1, NW)), 4.0, 0.25).astype(np.float32)
    w[:, 1, :, 0] = 0.25; w[:, 1, :, NW - 2] = 0.25; w[:, 6, :, 0] = 0.25; w[:, 6, :, NW - 2] = 0.25; w[..., NW - 1] = 0
    low = np.array([9, 0, 5, 6, 7, 8, 6, 16])[None, :, None, None]
    tau = np.where(np.argsort(rng.random((N, 8, 16, 3)), axis=2) < low, 0.25, 4.0).astype(np.float32)
    two = rng.choice(np.array([0, NW - 2]), b.shape); m = rng.random(b.shape) < 0.7; m[:, :, 1, ::2] = True; m[:, :, 6, ::2] = True
    b = np.where(m, two, b)
    return pack(rng, f, w, b, x, tau, np.full((N, 8, E), 4), np.array([0.5, 0.03, 0.97, 0.3, 0.5, 0.1, 0.9, 0.3])[None, :, None])
def pattern(T):
    on = np.zeros(16, bool)
    for k in range(15):
        n = min(C, 15 - k)
        if n <= T: on[k] = True; T = T - n
    return on
def setup_inputs_corners(rng):
    f, w, b, x, tau = parts(rng); tau[:, 1:] = 0.375; slot = np.arange(16); e = np.arange(E)[:, None]
    size = (0, NW - 1, NW - 2, NW - 2, 64, 64, 64, NW >> 1)
    pats = np.stack([pattern(T) for T in (0, 1, C, 15, 16, 17, 40)] + [slot >= 0, slot == 15])
    for r in range(N):
        for g in range(1, 8):
            o = rng.permutation(NW - 1); H = size[g]; m = np.zeros(NW, bool); m[o[:H]] = True
            w[r, g] = bf(np.where(m, 3.0 + rng.random((16, NW)), 0.25 + 0.05 * rng.random((16, NW))))
            for t in range(EP):
                if g == 1: want = np.ones((E, 16), bool)
                elif g < 4: want = (slot < 15) | ((e + t) % 2 == 0)
                elif g < 7: want = slot >= 16 - ((e + t + r) & 3)
                else: want = pats[(np.arange(E) + t) % len(pats)]
                b[t, r, g] = o[np.where(want, rng.integers(0, H, (E, 16)), rng.integers(min(H, NW - 2), NW - 1, (E, 16)))]
    w[..., NW - 1] = 0
    code = np.zeros((N, 8, E), np.int64); code[:, 0] = 2; code[:, 1:7] = 3
    return pack(rng, f, w, b, x, tau, code, np.full((N, 8, 1), 0.4))
def setup_inputs_crowd(rng):
    f, w, b, x, tau = parts(rng)
    b[:, :, :5] = 0
    for t in range(EP):
        for r in range(N): b[t, r, 4, int(rng.integers(0, E)), int(rng.integers(0, U))] = int(rng.integers(1, NW - 1))
    b[:, :, 5] = rng.choice(rng.integers(0, NW - 1, 3), (EP, N, E, 16)); b[:, :, 6] = int(rng.integers(1, NW - 1))
    w[:, :5, :, 0] = 1.0; tau[..., :2] = 0.3; tau[..., 2] = 3.0
    other = rng.integers(1, NW - 1, (EP, N)); w[:, 2:4, :, other.reshape(-1)] = 1.0
    code = np.zeros((N, 8, E), np.int64); code[:, :5] = 1; code[:, 6] = 2
    for r in range(N):
        e = int(rng.integers(0, E)); code[r, 2, e] = 2; b[:, r, 2, e, 0] = other[:, r]
        code[r, 4, int(rng.integers(0, E))] = 2
    return pack(rng, f, w, b, x, tau, code, np.full((N, 8, 1), 0.3))
def setup_inputs_full(rng):
    f, w, b, x, tau = parts(rng, 0.0); tau = np.nextafter(bf(tau), np.float32(8.0))
    b[..., :U] = np.argsort(rng.random((EP, N, 8, NW - 1)), axis=-1)[..., :E * U].reshape(EP, N, 8, E, U)
    return pack(rng, f, w, b, x, tau, np.where(np.arange(EP - 1) % 2 == 0, 2, 1)[:, None, None, None], np.full((N, 8, 1), 0.5))
def check_ranges(d):
    bad = []
    for k, lo, hi in (("bn", 0, NW - 2), ("lab", 0, 1), ("ask", 1, 48), ("tau", 0.25, 4)):
        v = np.asarray(d[k])
        if not np.all((v >= lo) & (v <= hi)): bad.append("range of " + k)
    for k, lo, hi in (("ft", 0.5, 1.25), ("wt", 0.25, 4)):
        v = np.asarray(d[k]).astype(np.float32)
        if not np.all((v[..., :NW - 1] >= lo) & (v[..., :NW - 1] <= hi)): bad.append("range of " + k)
        if not np.all(v[..., NW - 1] == 0): bad.append("last column of " + k)
    v = np.asarray(d["ft"]).astype(np.float32)
    if not np.all(v == v[:1]): bad.append("ft is not alike on all ranks")
    v = np.asarray(d["xv"]).astype(np.float32)
    if not np.all((v >= 0.25) & (v <= 2)): bad.append("range of xv")
    return bad
def reference(ft, wt, bn, xv, tau, lab, ask):
    f = np.asarray(ft).astype(np.float64).reshape(N, 8, 16, NW); w = np.asarray(wt).astype(np.float32).reshape(N, 8, 16, NW); ta = np.asarray(tau).astype(np.float32).reshape(N, 8, 16, 3)
    b = np.stack([gentries(a) for a in bn]).astype(np.int64).reshape(N, 8, EP, E, 16)
    la = np.asarray(lab).reshape(N, 8, EP - 1, E); need = np.asarray(ask).reshape(N, 8, EP - 1, E); ys, cs = [], []
    for t in range(EP):
        names, par, c = grow(w, ta, b[:, :, t]); s = np.zeros((N, 8, 16, E))
        for r in range(N):
            for d in range(3):
                q = (r + d) % N; L = names[d][r]; fl = pick(at(f[q], d), L)
                v = fl if d == 0 else np.take_along_axis(v, par[d][r][:, None], 3) * fl
                s[r] += np.add.reduce(v * pick(at(w[q], d), L), axis=3)
        ys.append(s); cs.append(c)
        if t < EP - 1:
            yes = c >= need[:, :, t]
            w = winnow(w, names, yes & (la[:, :, t] == 0), ~yes & (la[:, :, t] == 1))
    y = np.stack(ys).transpose(1, 2, 3, 0, 4).reshape(N, 128, EP * E) * np.asarray(xv).astype(np.float64)
    return {"y": y.astype(np.float32), "cv": np.stack(cs).transpose(1, 2, 0, 3).reshape(N, 8, EP * E).astype(np.float32)}

def check_inputs(d):
    bad = list(check_ranges(d))
    if not bad:
        for name, y in reference(**d).items():
            for q in range(N):
                v = np.abs(np.asarray(y[q], np.float64)); s = np.sqrt(np.mean(v * v))
                if v.max() > 8 * s or s < 2.0 ** 3: bad.append('%s of rank %d is uneven or too small' % (name, q))
    return bad

@@ -1,0 +1,623 @@
+from concourse.bass import DstId, RemoteDMATransfer
+from concourse.mybir import AluOpType as OP, ActivationFunctionType as AF
+
+NW, E, EP, H = 4096, 256, 3, 128
+BF, F32, I32, U16 = "bfloat16", "float32", "int32", "uint16"
+QG, QV = 1024, 512
+
+
+def _sb(cols, d):
+    return ("sbuf", [128, cols], d)
+
+
+SCRATCH = {
+    "w1": _sb(NW, BF), "w20": _sb(NW, BF), "w21": _sb(NW, BF), "w3": _sb(NW, BF), "fa": _sb(NW, BF), "fw1": _sb(NW, F32), "fw3": _sb(NW, F32),
+    "fd": ("dram", [6, 128, NW // 2], F32),
+    "wd": ("dram", [6, 128, NW // 2], BF), "thd": ("dram", [128, 8], F32),
+    "bni": _sb(768, I32), "bh": _sb(768, BF), "bl": _sb(768, BF), "l1u": _sb(768, U16),
+    "bw": _sb(18 * 256, BF), "dw0": _sb(17 * H, BF), "dw1": _sb(17 * H, BF),
+    "ge": _sb(4096, BF), "cw": _sb(16400, BF), "i4k": _sb(384, BF), "bd": ("dram", [2, 144, 768], BF),
+    "v1p": _sb(2048, BF), "v20": _sb(2064, F32), "v21": _sb(2064, F32),
+    "t1": _sb(1024, F32), "t2": _sb(4096, F32), "t3": _sb(1024, F32), "idf": _sb(128, F32),
+    "xs0": ("sbuf", [128, 3, 512], BF), "xs1": ("sbuf", [128, 3, 512], BF),
+    "st": _sb(768, BF), "nb": _sb(256, BF), "endb": _sb(256, BF), "kb": _sb(256, BF), "eq": _sb(768, BF),
+    "o1": _sb(256, U16), "o2": _sb(256, U16), "par": _sb(512, U16), "lu": _sb(512, U16),
+    "ls": _sb(256, F32), "uu": _sb(256, F32), "ti": _sb(256, I32), "tj": _sb(256, I32), "li": _sb(256, I32),
+    "di": _sb(512, I32), "dh": _sb(512, BF), "dl": _sb(512, BF), "l2": _sb(256, BF), "cap": _sb(256, BF),
+    "capt": _sb(256, F32), "lot": _sb(96, F32), "fl": _sb(48, F32), "fab": _sb(64, F32),
+    "labb": _sb(512, BF), "askb": _sb(512, BF),
+    "cs": _sb(1024, F32), "cin": _sb(1024, F32), "s1": _sb(256, F32), "s2": _sb(256, F32),
+    "fna": _sb(256, BF), "fnb": _sb(256, BF), "fct": _sb(256, BF),
+    "xvs": _sb(768, BF), "ys": _sb(256, F32),
+    "cvs": _sb(256, F32), "taus": _sb(4, F32), "tw": _sb(16, F32), "tb": _sb(8, BF), "th": _sb(8, F32),
+    "th2": _sb(8, F32), "th3": _sb(8, F32),
+    "dif": _sb(128, F32), "q144": _sb(144, F32), "gq": _sb(128, F32), "pc": _sb(8, I32), "col": _sb(32, F32),
+    "km": _sb(16, F32), "idn": _sb(128, BF), "i256": _sb(512, BF), "blk": _sb(128, BF), "tri": _sb(256, BF),
+    "shf": _sb(384, BF), "tmpm": _sb(128, BF), "big": _sb(5 * 144, BF), "sel": _sb(2048, BF), "g8": _sb(8, BF),
+    "ni8": _sb(8, BF), "selu": _sb(16, BF), "rep": _sb(512, BF), "nio": _sb(512, BF),
+    "one": _sb(128, BF), "eio": _sb(256, BF), "es1": _sb(256, BF), "es2": _sb(128, BF), "e16": _sb(128, BF),
+}
+for _b in ("X0", "Y0", "Z0", "X1", "Y1", "Z1", "S0", "S1"):
+    SCRATCH["P" + _b] = ("psum", [128, 512], F32)
+SEMAPHORES = ["cV", "cA", "cP", "cG"] + ["s%d" % i for i in range(140)]
+
+OV, LEANS, PASSES, STAG, VAL = 30.0, (4000.0, 5000.0, 6000.0), 5, 0.0, 0.0
+CY, PCY, GA, HOP = 1.0, 0.5, 1.6, 120.0
+
+
+def build(g, core, T, topo):
+    rank = T.rank_of(core)
+    n = len(T.cores)
+    ops, acc, nsem, lead = [], {}, [0], [0.0]
+
+    def A(name, a=0, b=None, s=1, p0=0, p1=128, ps=1):
+        if b is None:
+            b = SCRATCH[name][1][1]
+        if name in ("ohw", "g1o"):
+            a, b = (a, b) if name == "ohw" else (a + 12288, b + 12288)
+            name = "cw"
+        return (T[name][p0:p1:ps, a:b:s], (name, a, b))
+
+    def add(eng, fn, rd, wr, occ, lat=None, kind="c", after=()):
+        i = len(ops)
+        deps = dict((j, True) for j in after)
+        for regs, w in ((rd, False), (wr, True)):
+            for nm, a, b in regs:
+                for j, c, d, w2 in acc.setdefault(nm, []):
+                    if j == i:
+                        continue
+                    if a < d and c < b and (w or w2):
+                        deps[j] = True
+                if w:
+                    acc[nm] = [x for x in acc[nm] if not (a <= x[1] and x[2] <= b)]
+                acc[nm].append((i, a, b, w))
+        ops.append(dict(eng=eng, fn=fn, deps=deps, occ=occ, lat=occ if lat is None else lat, kind=kind, lead=lead[0],
+                        banks=sorted(set(x[0] for x in list(rd) + list(wr) if x[0][0] == "P"))))
+        return i
+
+    def sem():
+        nsem[0] += 1
+        return "s%d" % (nsem[0] - 1)
+
+    def wid(x):
+        return int(x[0].shape[-1]) * (3 if len(x[0].shape) == 3 else 1)
+
+    def two(*xs):
+        return all(SCRATCH[x[1][0]][2] in (BF, U16) for x in xs)
+
+    def cost(*xs):
+        return OV + CY * max(64, wid(xs[0]) * (0.5 if two(*xs) else 1))
+
+    def ts(o, i, s1, s2, op0, op1=None, after=()):
+        rd = [i[1]] + [s[1] for s in (s1, s2) if isinstance(s, tuple)]
+        v1 = s1[0] if isinstance(s1, tuple) else s1
+        v2 = s2[0] if isinstance(s2, tuple) else s2
+        if op1 is None:
+            fn = lambda q, e: [q.tensor_scalar(o[0], i[0], v1, None, op0)]
+        else:
+            fn = lambda q, e: [q.tensor_scalar(o[0], i[0], v1, v2, op0, op1)]
+        return add("V", fn, rd, [o[1]], cost(o, i), after=after)
+
+    def tt(o, a, b, op):
+        k = 1 if "P" in (a[1][0][0], b[1][0][0]) else 2
+        return add("V", lambda q, e: [q.tensor_tensor(o[0], a[0], b[0], op)], [a[1], b[1]], [o[1]], OV + CY * max(64, k * wid(o)))
+
+    def cp(o, i):
+        return add("V", lambda q, e: [q.tensor_copy(o[0], i[0])], [i[1]], [o[1]], cost(o, i))
+
+    def ev(o, i, scale=1.0, bias=0.0):
+        def fn(q, e):
+            if e == "A":
+                return [q.activation(o[0], i[0], AF.Identity, bias=bias, scale=scale)]
+            return [q.tensor_scalar(o[0], i[0], scale, bias, OP.mult, OP.add)]
+        return add("AV", fn, [i[1]], [o[1]], OV + CY * max(64, wid(o)))
+
+    def ms(o, v):
+        return add("V", lambda q, e: [q.memset(o[0], v)], [], [o[1]], cost(o))
+
+    def iota(o, pat, base, cm):
+        if SCRATCH[o[1][0]][2] == I32:
+            fn = lambda q, e: [q.iota(o[0], pat, base, cm)]
+        else:
+            fn = lambda q, e: [q.iota(o[0], pat, base, cm, allow_small_or_imprecise_dtypes=True)]
+        return add("G", fn, [], [o[1]], 150 + 2 * CY * wid(o))
+
+    def mm(o, pairs):
+        def fn(q, e):
+            return [q.matmul(o[0], l[0], r[0], k == 0, k == len(pairs) - 1) for k, (l, r) in enumerate(pairs)]
+        return add("P", fn, [x[1] for pr in pairs for x in pr], [o[1]],
+                   60 + len(pairs) * (10 + PCY * max(64, wid(o)) * (4 if pairs[0][0][1][0] == "idf" else 1)))
+
+    def gat(o, win, off, eng="AV"):
+        def fn(q, e):
+            src = win[0].indirect(off[0])
+            return [q.activation(o[0], src, AF.Copy) if e == "A" else q.tensor_copy(o[0], src)]
+        return add(eng, fn, [win[1], off[1]], [o[1]], 65 + GA * wid(o))
+
+    def gge(o, win, off, thr, d):
+        pos, neg = A(thr, d, d + 1), A(thr, 4 + d, 5 + d)
+        def fn(q, e):
+            src = win[0].indirect(off[0])
+            if e == "A":
+                return [q.activation(o[0], src, AF.Sign, bias=neg[0])]
+            return [q.tensor_scalar(o[0], src, pos[0], 0.5, OP.is_ge, OP.subtract)]
+        return add("AV", fn, [win[1], off[1], (thr, 0, 8)], [o[1]], 65 + GA * wid(o))
+
+    def gmul(o, win, off, b, op=OP.mult):
+        return add("V", lambda q, e: [q.tensor_tensor(o[0], win[0].indirect(off[0]), b[0], op)],
+                   [win[1], off[1], b[1]], [o[1]], 55 + GA * wid(o))
+
+    def dma(o, i, rd, wr, lat, eng="S", twin=None):
+        if twin is None:
+            k = add(eng, lambda q, e: [q.dma_start(o, i)], rd, wr, 100, lat, kind="d")
+            ops[k]["sem"] = [sem(), 16]
+        else:
+            k = add(eng, lambda q, e: [q.dma_start(o, i)], rd, [], 100, lat, kind="d", after=list(ops[twin]["deps"]))
+            for nm, a, b in wr:
+                acc[nm].append((k, a, b, True))
+            ops[k]["sem"] = ops[twin]["sem"]
+            ops[k]["sem"][1] += 16
+        return k
+
+    def send(parts, lat, wr=()):
+        ls, rs = sem(), [sem() for _ in parts]
+        trs, cnt = [], []
+        for k, (ahead, src, dst) in enumerate(parts):
+            to = T.cores[(rank + ahead) % n]
+            en = topo.engines(core, to)
+            m = len(en) // len(parts)
+            rid, pid = topo.addr(to)[:2]
+            trs.append(RemoteDMATransfer(dst_ids=[DstId(rid=rid, pnc=pid)], dma_engine_mask=sum(1 << x for x in en[k * m:(k + 1) * m]),
+                                         remote_sem=T.sem[rs[k]], src=src[0], dst=dst[0]))
+            cnt.append(m)
+        i = add("G", lambda q, e: [q.remote_dma_fused(trs, local_sem=T.sem[ls])], [p[1][1] for p in parts], list(wr), 400, lat, kind="r")
+        ops[i]["tok"] = (ls, sum(cnt))
+        for k, p in enumerate(parts):
+            j = add("", None, [], [p[2][1]], 0, 300, kind="a", after=[i])
+            ops[j]["tok"] = (rs[k], cnt[k])
+
+    for k in range(2):
+        dma(T.w1[:, k * 2048:(k + 1) * 2048], T.wt[:, k * 2048:(k + 1) * 2048], [], [("w1", k * 2048, (k + 1) * 2048)], 3200, "SA"[k])
+    dma(T.bni[:], T.bn[:], [], [("bni", 0, 768)], 2600, "A")
+    dma(T.taus[:, 0:3], T.tau[:], [], [("taus", 0, 4)], 2200)
+    dma(T.fa[:], T.ft[:], [], [("fa", 0, NW)], 5000)
+    dma(T.di[0:8, :], T.lab[:], [], [("di", 0, 512)], 2500)
+    dma(T.xvs[:], T.xv[:], [], [("xvs", 0, 768)], 2500)
+
+    def send_w(v, k):
+        half = A("w1", k * 2048, (k + 1) * 2048)
+        send([(-1, half, A("w2%d" % (v % 2), k * 2048, (k + 1) * 2048))], 3500)
+
+    def send_w3(v, k):
+        half = A("w1", k * 2048, (k + 1) * 2048)
+        slot = 2 * v + k
+        send([(-2, half, (T.wd[slot], ("wd", slot, slot + 1)))], 4000)
+        c = slice(k * 2048, (k + 1) * 2048)
+        j = dma(T.w3[0:112, c], T.wd[slot, 16:128, :], [("wd", slot, slot + 1)], [("w3", k * 2048, (k + 1) * 2048)], 3000)
+        dma(T.w3[112:128, c], T.wd[slot, 0:16, :], [("wd", slot, slot + 1)], [("w3", k * 2048, (k + 1) * 2048)], 3000, twin=j)
+
+    ta = A("taus", 0, 3)
+    cp(A("tb", 0, 3), ta)
+    tt(A("tw", 0, 3), A("tb", 0, 3), ta, OP.is_ge)
+    ts(A("tw", 4, 7), A("tw", 0, 3), -2.0 ** -9, 1 + 2.0 ** -10, OP.mult, OP.add)
+    tt(A("tw", 8, 11), A("tw", 4, 7), A("tb", 0, 3), OP.mult)
+    ts(A("tw", 12, 15), ta, 0.25, None, OP.is_gt)
+    ms(A("th"), 0.0)
+    tt(A("tw", 0, 3), A("tw", 8, 11), A("tw", 12, 15), OP.mult)
+    ts(A("th", 0, 3), A("tw", 0, 3), 0.01, None, OP.max)
+    ts(A("th", 4, 7), A("tw", 0, 3), -1.0, -0.01, OP.mult, OP.min)
+    send_w(0, 0)
+    send_w(0, 1)
+    send([(-1, A("th"), A("th2")), (-2, A("th"), (T.thd[:], ("thd", 0, 8)))], 2500)
+    send_w3(0, 0)
+    send_w3(0, 1)
+    dma(T.th3[0:112, :], T.thd[16:128, :], [("thd", 0, 8)], [("th3", 0, 4)], 2200)
+    dma(T.th3[112:128, :], T.thd[0:16, :], [("thd", 0, 8)], [("th3", 4, 8)], 2200)
+
+    C = lambda j: A("col", j, j + 1)
+    iota(A("pc", 0, 1), [[0, 1]], 0, 1)
+    iota(A("q144"), [[1, 144]], 0, 0)
+    iota(A("dif"), [[1, 128]], 0, -1)
+    iota(A("gq"), [[1, 8], [0, 16]], 0, 0)
+    iota(A("eio"), [[1, 256]], 0, 0)
+    iota(A("cs", 0, 512), [[16, 8], [1, 2], [0, 32]], 0, -1)
+    iota(A("cs", 512, 528), [[16, 8], [1, 2]], 0, -1)
+    iota(A("nio"), [[0, 16], [-1, 32]], 16, 0)
+    ts(A("pc", 2, 3), A("pc", 0, 1), 4, None, OP.arith_shift_right)
+    ts(A("pc", 4, 5), A("pc", 0, 1), 15, None, OP.bitwise_and)
+    cp(C(0), A("pc", 2, 3))
+    cp(C(1), A("pc", 4, 5))
+    ts(C(2), C(0), 16.0, 15.0, OP.mult, OP.add)
+    ts(A("km"), A("q144", 0, 16), C(1), None, OP.is_equal)
+    K = lambda j: A("km", j, j + 1)
+    ROWS = ((0, 4), (8, 12), (1, 5))
+    BIG = lambda j, m: A("big", 144 * j + 15 - m, 144 * j + 143 - m)
+    ts(A("big", 0, 144), A("q144"), C(2), None, OP.is_equal)
+    for t in range(EP):
+        ts(C(3 + t), K(ROWS[t][0]), 128.0, K(ROWS[t][1]), OP.mult, OP.add)
+        ts(A("big", 144 * (1 + t), 144 * (2 + t)), A("q144"), C(2), C(3 + t), OP.is_equal, OP.mult)
+    ts(C(6), K(8), 256.0, None, OP.mult)
+    ts(A("big", 576, 720), A("q144"), C(2), C(6), OP.is_equal, OP.mult)
+    ts(A("idn"), A("dif"), 0.0, None, OP.is_equal)
+    ts(A("blk"), A("gq"), C(0), None, OP.is_equal)
+    ts(A("tmpm"), A("dif"), 0.0, None, OP.is_ge)
+    tt(A("tri", 128, 256), A("tmpm"), A("blk"), OP.mult)
+    ts(C(7), C(1), -1.0, 15.0, OP.mult, OP.add)
+    ts(C(8), C(7), 4.0, None, OP.min)
+    ts(A("tri", 0, 128), A("tri", 128, 256), C(8), None, OP.mult)
+    for j in range(4):
+        ts(C(9 + j), C(1), float(j), 256.0, OP.is_ge, OP.mult)
+        ts(A("i256", 128 * j, 128 * j + 128), A("dif"), 0.0, C(9 + j), OP.is_equal, OP.mult)
+    for j in range(1, 4):
+        o = A("shf", 128 * j - 128, 128 * j)
+        ts(A("tmpm"), A("dif"), float(j), None, OP.is_equal)
+        tt(o, A("tmpm"), A("blk"), OP.mult)
+        tt(o, A("idn"), o, OP.subtract)
+    ts(A("es1"), A("eio"), 1.0 / 256, None, OP.mult)
+    ts(A("es2"), A("eio", 0, 128), 1.0 / 128, None, OP.mult)
+    ts(A("e16"), A("eio", 0, 128), 16.0, None, OP.mult)
+    cp(A("l1u", 0, 256), A("bni", 0, 256))
+    cp(A("l1u", 256, 768), A("bni", 256, 768))
+    ms(A("bw", 0, 4096), 0.0)
+    for a in range(0, 768, 256):
+        ts(A("ti"), A("bni", a, a + 256), 7, None, OP.arith_shift_right)
+        ts(A("bh", a, a + 256), A("ti"), -16.0, None, OP.add)
+        ts(A("tj"), A("bni", a, a + 256), 127, None, OP.bitwise_and)
+        cp(A("bl", a, a + 256), A("tj"))
+    tt(C(13), K(0), K(8), OP.add)
+    tt(C(13), C(13), K(1), OP.add)
+    ts(C(14), C(13), -112.0, 127.0, OP.mult, OP.add)
+    ts(C(15), C(13), -16.0, None, OP.mult)
+    ts(A("bw", 4096, 4352), A("eio"), 0.0, C(14), OP.mult, OP.add)
+    ts(A("bw", 4352, 4608), A("eio"), 0.0, C(15), OP.mult, OP.add)
+    for t in range(EP):
+        for k, nm in enumerate(("bh", "bl")):
+            j = 2 * t + k
+            dma(T.bw[ROWS[t][k]:128:16, 0:4096], T[nm][:, 256 * t:256 * t + 256], [(nm, 256 * t, 256 * t + 256), ("bw", 6, 4096)], [("bw", j, j + 1)], 2600)
+    for j, nm in enumerate(("bh", "bl")):
+        dma(T.bd[j, 0:128, :], T[nm][:], [(nm, 0, 768)], [("bd", 2 * j, 2 * j + 1)], 2600)
+        dma(T.bd[j, 128:144, :], T[nm][0:16, :], [(nm, 0, 768)], [("bd", 2 * j + 1, 2 * j + 2)], 2600)
+    ts(C(17), K(4), 127.0, None, OP.mult)
+    ts(C(18), K(8), -16.0, C(17), OP.mult, OP.add)
+    ts(C(19), K(0), 15.0, C(18), OP.mult, OP.add)
+    ts(A("cw", 16384, 16400), A("eio", 0, 16), 0.0, C(19), OP.mult, OP.add)
+    ts(A("i4k"), A("i256", 128, 512), 16.0, None, OP.mult)
+    tt(C(16), C(14), K(8), OP.add)
+    for h in range(2):
+        for a in range(0, 2048, 512):
+            iota(A("dw%d" % h, a, a + 512), [[0, 512]], 0, 0)
+        ts(A("dw%d" % h, 2048, 2176), A("eio", 0, 128), 0.0, C(16), OP.mult, OP.add)
+        ms(A("v2%d" % h, 2048, 2064), 0.0)
+    ts(A("g8"), A("q144", 0, 8), C(0), None, OP.is_equal)
+    ts(A("ni8"), A("dif", 0, 8), 0.0, -1.0, OP.is_equal, OP.mult)
+    ts(A("rep"), A("cs", 0, 512), 0.0, None, OP.is_equal)
+    ts(A("selu"), A("cs", 512, 528), 0.0, None, OP.is_equal)
+    ms(A("one"), 1.0)
+    ts(A("idf"), A("dif"), 0.0, None, OP.is_equal)
+    for k in range(16):
+        ts(A("sel", 128 * k, 128 * k + 128), A("blk"), K(k), None, OP.mult)
+    cp(A("labb", p1=8), A("di", p1=8))
+    dma(T.di[0:8, :], T.ask[:], [], [("di", 0, 512)], 2500)
+    cp(A("askb", p1=8), A("di", p1=8))
+    for j in range(4):
+        mm(A("PS0", 8 * j, 8 * j + 8), [(A("labb", 128 * j, 128 * j + 128, p1=8), A("idn", 0, 8, p1=8))])
+    ev(A("fab", 0, 32), A("PS0", 0, 32), -2049.0, 1.0)
+    ev(A("fab", 32, 64), A("PS0", 0, 32), 2048.0, 0.0)
+
+    def wide(nm, h, k):
+        return A(nm, 2048 * h + k, 2048 * h + 2048, 16)
+
+    def strong(h, d, win, thr, lst, a):
+        for s in range(0, 2048, QG):
+            gge(A("ge", 2048 * h + s, 2048 * h + s + QG), A(win), A(lst, a + s // 16, a + (s + QG) // 16), thr, d)
+        x = A("PX%d" % h, 0, 128)
+        mm(x, [(BIG(0, k), wide("ge", h, k)) for k in range(16)])
+        ts(A("st", 384 * h + 128 * d, 384 * h + 128 * d + 128), x, 0.0, None, OP.is_gt)
+
+    def children(t, h, d):
+        X, Y, Z = "PX%d" % h, "PY%d" % h, "PZ%d" % h
+        c = lambda nm, j=0, w=1: A(nm, 128 * (w * h + j), 128 * (w * h + j) + 128)
+        st = c("st", d, 3)
+        if d == 0:
+            mm(A(X, 128, 256), [(A("tri", 0, 128), st)])
+        else:
+            tt(c("nb"), st, c("cap"), OP.mult)
+            mm(A(X, 128, 256), [(A("tri", 128, 256), c("nb"))])
+        ev(c("endb"), A(X, 128, 256))
+        cm = lambda m: A("ge", 2048 * h + 128 * m, 2048 * h + 128 * m + 128)
+        for m in range(16):
+            ts(cm(m), c("endb"), float(m), None, OP.is_le)
+        es = c("es1") if d == 0 else A("es2")
+        kp = A(X, 256, 384)
+        mm(kp, [(BIG(0, m), cm(m)) for m in range(16)] + [(A("idn"), es)])
+        one = d == 0 and t > 0
+        if not one:
+            ts(c("o1"), kp, 256.0 if d == 0 else 128.0, None, OP.mult)
+        tt(c("kb"), kp, es, OP.subtract)
+        for s in range(0, 0 if one else 2048, QG):
+            gat(A("g1o", 2048 * h + s, 2048 * h + s + QG), A("bw" if d == 0 else "dw%d" % h), A("o1", 128 * h + s // 16, 128 * h + (s + QG) // 16))
+        for j in range(3):
+            mm(A(Y, 128 * j, 128 * j + 128), [(A("shf", 128 * j, 128 * j + 128), c("kb"))])
+        ts(A("eq", 384 * h, 384 * h + 384), A(Y, 0, 384), 0.0, None, OP.is_equal)
+        cs = [(A("i256", 128 * j + 128, 128 * j + 256), c("eq", j, 3)) for j in range(3)]
+        ls = [(A("i256", 0, 128), c("kb"))] if d == 0 else [(BIG(4, k), wide("g1o", h, k)) for k in range(16)]
+        if one:
+            ts(c("nb"), c("kb"), 16.0, 64.0, OP.is_equal, OP.mult)
+            mm(A(X, 0, 128), [(A("i4k", 128 * j, 128 * j + 128), c("eq", j, 3)) for j in range(3)]
+               + [(A("idn"), c("eio")), (A("i256", 0, 128), c("nb"))] + ls)
+            ts(c("o2"), A(X, 0, 128), 16384.0, None, OP.min)
+        else:
+            mm(A(X, 0, 128), cs + [(A("idn"), c("eio"))] + ls)
+            ts(c("o2"), A(X, 0, 128), 256.0, 4607.0, OP.add, OP.min)
+        for s in range(0, 2048, QG):
+            gat(A("ge", 2048 * h + s, 2048 * h + s + QG), A("cw" if one else "bw"), A("o2", 128 * h + s // 16, 128 * h + (s + QG) // 16))
+        if d == 1:
+            mm(A(Y, 384, 512), [(A("idn"), c("kb")), (A("idn"), A("e16"))])
+            cp(c("par", 1, 2), A(Y, 384, 512))
+        if d == 0:
+            mm(A(Z, 128, 256), cs + ls)
+            ev(c("l2"), A(Z, 128, 256), 1.0 / 256, 1.0)
+            ev(c("capt"), A(Z, 128, 256), -1.0 / 256, 14.0)
+            ts(c("cap"), c("capt"), 4.0, None, OP.min)
+        mm(A(Y, 0, 128), [(BIG(1, k), wide("ge" if one else "g1o", h, k)) for k in range(16)])
+        ev(c("ls"), A(Y, 0, 128), 1.0, 3232.0)
+        if d == 0:
+            ts(c("par", 0, 2), c("ls"), -1184.0, None, OP.add)
+        ev(c("uu"), c("ls"), 65.0, 75776.0 - 65 * 1184 + 409600)
+        mm(A(Z, 0, 128), [(BIG(2 if one else 1 + t, k), wide("ge", h, k)) for k in range(16)])
+        tt(c("ti"), c("ls"), A(Z, 0, 128), OP.mult)
+        ts(c("tj"), c("ti"), 5, None, OP.arith_shift_right)
+        tt(c("ti"), c("tj"), c("uu"), OP.add)
+        ts(c("li"), c("ti"), NW - 1, None, OP.bitwise_and)
+        cp(c("lu", d, 2), c("li"))
+        if d == 0 or t < EP - 1:
+            ts(c("di", 0, 2), c("li"), 7, None, OP.arith_shift_right)
+            ts(c("dh", d, 2), c("di", 0, 2), -16.0, None, OP.add)
+            ts(c("di", 1, 2), c("li"), 127, None, OP.bitwise_and)
+            cp(c("dl", d, 2), c("di", 1, 2))
+        if d == 0:
+            w = "dw%d" % h
+            k = None
+            for j, src in ((2, c("l2")), (0, c("dh", 0, 2)), (1, c("dl", 0, 2))):
+                z = dma(T[w][4 * j:128:16, 0:2048], src[0], [src[1]], [(w, 0, 2048)], 2300, twin=k)
+                k = z if k is None else k
+
+    def marks(h, d, hi, lo):
+        Z, S = "PZ%d" % h, "PS%d" % h
+        mm(A(Z, 256, 272), [(lo, A("selu"))])
+        a = 48 * h + 16 * d
+        ev(A("lot", a, a + 16), A(Z, 256, 272))
+        for j in range(16):
+            ts(A("ohw", 128 * (a + j), 128 * (a + j) + 128), A("eio", 0, 128), A("lot", a + j, a + j + 1), None, OP.is_equal)
+        mm(A(S), [(hi, A("rep")), (A("one", p1=1), A("nio", p1=1))])
+        ev((T["xs%d" % h][:, d, :], ("xs%d" % h, 8 * d, 8 * d + 8)), A(S))
+
+    def values12(t, h):
+        for s in range(0, 2048, QV):
+            a, b = s // 16, (s + QV) // 16
+            l1 = A("l1u", 256 * t + 128 * h + a, 256 * t + 128 * h + b)
+            l2 = A("lu", 256 * h + a, 256 * h + b)
+            vp = A("v1p", s, s + QV)
+            gat(vp, A("fa"), A("par", 256 * h + a, 256 * h + b))
+            gmul(A("v2%d" % h, s, s + QV), A("fa"), l2, vp)
+            gmul(A("t2", 2048 * h + s, 2048 * h + s + QV), A("w2%d" % (t % 2)), l2, A("v2%d" % h, s, s + QV))
+            gat(A("t1", s % 1024, s % 1024 + QV), A("fw1"), l1)
+            if (s + QV) % 1024 == 0:
+                plus(2048 * h + s + QV - 1024, "t1")
+
+    def plus(r, nm):
+        o, x = A("t2", r, r + 1024), A(nm)
+        k = add("G", lambda q, e: [q.dma_start(o[0], x[0], accum_op=OP.add)], [x[1], o[1]], [o[1]], 1000, 3500, kind="d")
+        ops[k]["sem"] = [sem(), 16]
+
+    def values3(t, h):
+        for s in range(0, 2048, QV):
+            a, b = s // 16, (s + QV) // 16
+            l3 = A("lu", 256 * h + 128 + a, 256 * h + 128 + b)
+            x = A("t3", s % 1024, s % 1024 + QV)
+            gat(x, A("v2%d" % h), A("par", 256 * h + 128 + a, 256 * h + 128 + b))
+            gmul(x, A("fw3"), l3, x)
+            if (s + QV) % 1024 == 0:
+                r = s + QV - 1024
+                sums = [(A("idf"), A("t2", 2048 * h + r + k, 2048 * h + r + 1024, 16)) for k in range(16)]
+                if t == EP - 1 and h == 1:
+                    sums += [(A("idf"), A("t3", k, 1024, 16)) for k in range(16)]
+                else:
+                    plus(2048 * h + r, "t3")
+                mm(A("PZ%d" % h, 384 + r // 16, 448 + r // 16), sums)
+        e0, ys = 256 * t + 128 * h, A("ys", 128 * h, 128 * h + 128)
+        tt(ys, A("xvs", e0, e0 + 128), A("PZ%d" % h, 384, 512), OP.mult)
+        dma(T.y[:, e0:e0 + 128], ys[0], [ys[1]], [], 2200)
+
+    def products(v):
+        for j in range(8):
+            P, c = ("PS0", "PS1")[j % 2], (512 * j, 512 * j + 512)
+            mm(A(P), [(A("idn"), A("fa", *c))])
+            tt(A("fw1", *c), A("w1", *c), A(P), OP.mult)
+        for k in range(2):
+            a, slot = 2048 * k, 2 * v + k
+            send([(-2, A("fw1", a, a + 2048), (T.fd[slot], ("fd", slot, slot + 1)))], 6000)
+            j = dma(T.fw3[0:112, a:a + 2048], T.fd[slot, 16:128, :], [("fd", slot, slot + 1)], [("fw3", a, a + 2048)], 4500)
+            dma(T.fw3[112:128, a:a + 2048], T.fd[slot, 0:16, :], [("fd", slot, slot + 1)], [("fw3", a, a + 2048)], 4500, twin=j)
+
+    products(0)
+    for t in range(EP):
+        last = t == EP - 1
+        for h in range(2):
+            strong(h, 0, "w3" if t else "w1", "th", "l1u", 256 * t + 128 * h)
+        if t:
+            k = None
+            for cc in range(4):
+                for j, nm in enumerate(("bh", "bl")):
+                    for row, src, rd in ((4 * j, T[nm][:, 256 * t:256 * t + 256], (nm, 256 * t, 256 * t + 256)),
+                                         (8 + 4 * j, T.bd[j, cc + 1:cc + 129, 256 * t:256 * t + 256], ("bd", 0, 4))):
+                        z = dma(T.cw[row:128:16, 4096 * cc:4096 * cc + 4096], src, [rd], [("cw", 0, 16384)], 5000, twin=k)
+                        k = z if k is None else k
+            send_w3(t, 0)
+            send_w3(t, 1)
+        for h in range(2):
+            children(t, h, 0)
+        for h in range(2):
+            e0 = 256 * t + 128 * h
+            if not last:
+                marks(h, 0, A("bh", e0, e0 + 128), A("bl", e0, e0 + 128))
+            strong(h, 1, "w2%d" % (t % 2), "th2", "lu", 256 * h)
+            if not last:
+                marks(h, 1, A("dh", 256 * h, 256 * h + 128), A("dl", 256 * h, 256 * h + 128))
+            children(t, h, 1)
+            if not last:
+                marks(h, 2, A("dh", 256 * h + 128, 256 * h + 256), A("dl", 256 * h + 128, 256 * h + 256))
+            strong(h, 2, "w3", "th3", "lu", 256 * h + 128)
+            sts = [A("st", 384 * h + 128 * d, 384 * h + 128 * d + 128) for d in range(3)]
+            if not last:
+                x = A("PX%d" % h, 0, 8)
+                mm(x, [(s, A("g8")) for s in sts] + [(A("askb", e0, e0 + 128, p1=8), A("ni8", p1=8))])
+                j = 8 * (2 * t + h)
+                f = lambda k: A("fl", 24 * h + 8 * k, 24 * h + 8 * k + 8)
+                ts(f(0), x, 0.0, None, OP.is_ge)
+                tt(f(1), f(0), A("fab", j, j + 8), OP.mult)
+                tt(f(2), f(1), A("fab", 32 + j, 40 + j), OP.add)
+                for gr in range(8):
+                    x, fg = T["xs%d" % h][:, :, 64 * gr:64 * gr + 64], A("fl", 24 * h + 16 + gr, 24 * h + 17 + gr)
+                    reg = [("xs%d" % h, 8 * d + gr, 8 * d + gr + 1) for d in range(3)]
+                    add("V", lambda q, e, x=x, fg=fg: [q.tensor_scalar(x, x, 0.0, fg[0], OP.is_equal, OP.mult)], reg + [fg[1]], reg, OV + 96 * CY)
+            y8 = A("PY%d" % h, 0, 128, p1=8)
+            mm(y8, [(A("g8"), s) for s in sts])
+            ev(A("cvs", 128 * h, 128 * h + 128, p1=8), y8)
+            if h == 1:
+                dma(T.cv[:, 256 * t:256 * t + 256], T.cvs[0:8, :], [("cvs", 0, 256)], [], 2200)
+            lead[0] = VAL
+            values12(t, h)
+            values3(t, h)
+        lead[0] = 0.0
+        if last:
+            break
+        for d in (2, 1, 0):
+            for gr in range(8):
+                b = 32 * ((gr + (d == 2)) % 8) + (256 if d == 0 else 0)
+                prs = [(A("ohw", 128 * (48 * h + 16 * d + 2 * gr + u), 128 * (48 * h + 16 * d + 2 * gr + u + 1)),
+                        (T["xs%d" % h][:, d, 64 * gr + 32 * u:64 * gr + 32 * u + 32], ("xs%d" % h, 8 * d + gr, 8 * d + gr + 1)))
+                       for h in range(2) for u in range(2)]
+                mm(A("PS0" if d == 1 else "PS1", b, b + 32), prs)
+            if d > 0:
+                o = 512 * t + 256 * (d - 1)
+                ev(A("cs", o, o + 256), A("PS0" if d == 1 else "PS1", 0, 256))
+        o = 512 * t
+        send([(1, A("cs", o, o + 256), A("cin", o, o + 256)), (2, A("cs", o + 256, o + 512), A("cin", o + 256, o + 512))],
+             2500, wr=[("w2%d" % ((t + 1) % 2), 0, NW)])
+        tt(A("s1"), A("cin", o + 256, o + 512), A("PS1", 256, 512), OP.add)
+        tt(A("s2"), A("s1"), A("cin", o, o + 256), OP.add)
+        ts(A("fna"), A("s2"), 0.5, -0.5, OP.is_gt, OP.mult)
+        ts(A("fnb"), A("s2"), 2047.5, 1.5, OP.is_gt, OP.mult)
+        for b in range(2):
+            mm(A("PX0", 128 * b, 128 * b + 128), [(A(nm, b, 256, 2), A("idn")) for nm in ("fna", "fnb")])
+        ev(A("fct"), A("PX0", 0, 256), 1.0, 1.0)
+        for j in range(8):
+            P = ("PY0", "PS0", "PY1", "PS1")[j % 4]
+            for b in range(2):
+                mm(A(P, 256 * b, 256 * b + 256), [(A("sel", 128 * (2 * j + b), 128 * (2 * j + b + 1)), A("fct"))])
+            tt(A("w3", 512 * j, 512 * j + 512), A("w1", 512 * j, 512 * j + 512), A(P), OP.mult)
+            if j % 2 == 1:
+                z = (512 * j - 512, min(512 * j + 512, NW - 1))
+                ts(A("w1", *z), A("w3", *z), 0.25, 4.0, OP.max, OP.min)
+            if j % 4 == 3:
+                send_w(t + 1, j // 4)
+        products(t + 1)
+    return ops
+
+
+def place(ops, order, before, back, lean):
+    busy, at = {}, {}
+    for i in order:
+        o = ops[i]
+        best = None
+        off = o["lat"] - o["occ"] if back else 0.0
+        t0 = max([at[j][0] + ops[j]["lat"] + HOP for j in before[i]] + [0.0]) + off
+        for e in o["eng"] or " ":
+            t = t0
+            res = [] if e == " " else [(e, o["occ"])] + [(b, o["occ"] + 60) for b in o["banks"]]
+            moved = True
+            while moved:
+                moved = False
+                for r, d in res:
+                    for a, b in busy.setdefault(r, []):
+                        if a >= t + d:
+                            break
+                        if b > t:
+                            t, moved = b, True
+            if best is None or t + lean < best[0]:
+                best = (t, e, res)
+        at[i] = (best[0] - off, best[1])
+        for r, d in best[2]:
+            busy[r].append((best[0], best[0] + d))
+            busy[r].sort()
+    return at, max(at[i][0] + ops[i]["lat"] for i in at)
+
+
+def plan(ops):
+    n = len(ops)
+    pred = [list(o["deps"]) for o in ops]
+    succ = [[] for _ in ops]
+    up = [0.0] * n
+    for i in range(n - 1, -1, -1):
+        up[i] += ops[i]["lat"]
+        for j in pred[i]:
+            up[j] = max(up[j], up[i] + HOP)
+            succ[j].append(i)
+    best = None
+    for lean in LEANS:
+        at, end = place(ops, sorted(range(n), key=lambda i: (-up[i] - ops[i]["lead"], i)), pred, False, lean)
+        for k in range(PASSES):
+            bk, _ = place(ops, sorted(range(n), key=lambda i: (-at[i][0] - ops[i]["lat"], -i)), succ, True, lean)
+            at, end = place(ops, sorted(range(n), key=lambda i: (-bk[i][0] - ops[i]["lat"], i)), pred, False, lean)
+            if best is None or end < best[0]:
+                best = (end, at)
+    for i in range(n):
+        ops[i]["t"], ops[i]["e"] = best[1][i]
+        ops[i]["end"] = ops[i]["t"] + ops[i]["lat"]
+    order = sorted(range(n), key=lambda i: (ops[i]["t"], i))
+    prev = {}
+    for i in order:
+        for b in ops[i]["banks"]:
+            if b in prev:
+                ops[i]["deps"].setdefault(prev[b], False)
+            prev[b] = i
+    return order
+
+
+def rank_program(g, core, T, topo):
+    if T.rank_of(core) is None:
+        return
+    ops = build(g, core, T, topo)
+    order = plan(ops)
+    Q = {"V": g.vector, "A": g.scalar, "P": g.tensor, "G": g, "S": g.sync}
+    cnt = dict((e, 0) for e in "VAPG")
+    seen = dict((e, {}) for e in Q)
+    total = {}
+    for i in order:
+        o = ops[i]
+        e = o["e"]
+        if o["kind"] != "a":
+            need = {}
+            for j, hard in o["deps"].items():
+                if hard or ops[j]["e"] != e:
+                    s, v = ops[j]["tok"]
+                    need[s] = max(need.get(s, 0), v)
+            for s, v in need.items():
+                if seen[e].get(s, 0) < v:
+                    Q[e].wait_ge(T.sem[s], v)
+                    seen[e][s] = v
+            ins = o["fn"](Q[e], e)
+            if o["kind"] == "c":
+                for x in ins:
+                    x.then_inc(T.sem["c" + e], 1)
+                cnt[e] += len(ins)
+                o["tok"] = ("c" + e, cnt[e])
+            elif o["kind"] == "d":
+                ins[0].then_inc(T.sem[o["sem"][0]], 16)
+                o["tok"] = tuple(o["sem"])
+        s, v = o["tok"]
+        total[s] = max(total.get(s, 0), v)
+    for s, v in total.items():
+        if not any(seen[e].get(s, 0) >= v for e in seen):
+            g.sync.wait_ge(T.sem[s], v)

@@ -11,54 +11,55 @@ def _sb(cols, d):
 
 
 SCRATCH = {
-    "w1": _sb(NW, BF), "w20": _sb(NW, BF), "w21": _sb(NW, BF), "w3": _sb(NW, BF), "fa": _sb(NW, BF), "fw1": _sb(NW, F32), "fw3": _sb(NW, F32),
-    "fd": ("dram", [6, 128, NW // 2], F32),
-    "wd": ("dram", [6, 128, NW // 2], BF), "thd": ("dram", [128, 8], F32),
-    "bni": _sb(768, I32), "bh": _sb(768, BF), "bl": _sb(768, BF), "l1u": _sb(768, U16),
-    "bw": _sb(18 * 256, BF), "dw0": _sb(17 * H, BF), "dw1": _sb(17 * H, BF),
-    "ge": _sb(4096, BF), "cw": _sb(16400, BF), "i4k": _sb(384, BF), "bd": ("dram", [2, 144, 768], BF),
-    "v1p": _sb(2048, BF), "v20": _sb(2064, F32), "v21": _sb(2064, F32),
+    "w1": _sb(NW, BF), "w20": _sb(NW, BF), "w21": _sb(NW, BF), "w3": _sb(NW, BF), "fa": _sb(NW, BF),
+    "fw1": _sb(NW, F32), "fw3": _sb(NW, F32),
+    "fd": ("dram", [6, 128, NW // 2], F32), "wd": ("dram", [6, 128, NW // 2], BF), "thd": ("dram", [128, 8], F32),
+    "bd": ("dram", [8, 19, 1536], BF),
+    "bni": _sb(768, I32), "bdg": _sb(1536, BF), "l1u": _sb(768, U16),
+    "bw0": _sb(17 * 256, BF), "bw1": _sb(17 * 256, BF), "dw0": _sb(17 * H, BF), "dw1": _sb(17 * H, BF),
+    "ge": _sb(4096, BF), "g1o": _sb(4096, BF), "ohw": _sb(12288, BF),
+    "v1p": _sb(1024, BF), "v20": _sb(2064, F32), "v21": _sb(2064, F32),
     "t1": _sb(1024, F32), "t2": _sb(4096, F32), "t3": _sb(1024, F32), "idf": _sb(128, F32),
     "xs0": ("sbuf", [128, 3, 512], BF), "xs1": ("sbuf", [128, 3, 512], BF),
     "st": _sb(768, BF), "nb": _sb(256, BF), "endb": _sb(256, BF), "kb": _sb(256, BF), "eq": _sb(768, BF),
     "o1": _sb(256, U16), "o2": _sb(256, U16), "par": _sb(512, U16), "lu": _sb(512, U16),
-    "ls": _sb(256, F32), "uu": _sb(256, F32), "ti": _sb(256, I32), "tj": _sb(256, I32), "li": _sb(256, I32),
-    "di": _sb(512, I32), "dh": _sb(512, BF), "dl": _sb(512, BF), "l2": _sb(256, BF), "cap": _sb(256, BF),
-    "capt": _sb(256, F32), "lot": _sb(96, F32), "fl": _sb(48, F32), "fab": _sb(64, F32),
-    "labb": _sb(512, BF), "askb": _sb(512, BF),
-    "cs": _sb(1024, F32), "cin": _sb(1024, F32), "s1": _sb(256, F32), "s2": _sb(256, F32),
-    "fna": _sb(256, BF), "fnb": _sb(256, BF), "fct": _sb(256, BF),
+    "ls": _sb(256, F32), "uu": _sb(256, F32), "ti": _sb(256, I32), "li": _sb(256, I32),
+    "di": _sb(512, I32), "dh": _sb(512, BF), "dl": _sb(512, BF), "l2": _sb(256, BF),
+    "lot": _sb(96, BF), "fl": _sb(16, BF), "fab": _sb(32, BF),
+    "labx": _sb(512, BF), "askb": _sb(512, BF), "rx": _sb(512, BF),
+    "cs": _sb(1024, BF), "cin": _sb(1024, BF), "c0": _sb(256, BF), "fct": _sb(256, BF),
     "xvs": _sb(768, BF), "ys": _sb(256, F32),
     "cvs": _sb(256, F32), "taus": _sb(4, F32), "tw": _sb(16, F32), "tb": _sb(8, BF), "th": _sb(8, F32),
     "th2": _sb(8, F32), "th3": _sb(8, F32),
     "dif": _sb(128, F32), "q144": _sb(144, F32), "gq": _sb(128, F32), "pc": _sb(8, I32), "col": _sb(32, F32),
-    "km": _sb(16, F32), "idn": _sb(128, BF), "i256": _sb(512, BF), "blk": _sb(128, BF), "tri": _sb(256, BF),
+    "km": _sb(16, F32), "idn": _sb(128, BF), "i256": _sb(128, BF), "blk": _sb(128, BF), "tri": _sb(256, BF),
     "shf": _sb(384, BF), "tmpm": _sb(128, BF), "big": _sb(5 * 144, BF), "sel": _sb(2048, BF), "g8": _sb(8, BF),
-    "ni8": _sb(8, BF), "selu": _sb(16, BF), "rep": _sb(512, BF), "nio": _sb(512, BF),
-    "one": _sb(128, BF), "eio": _sb(256, BF), "es1": _sb(256, BF), "es2": _sb(128, BF), "e16": _sb(128, BF),
+    "ni8": _sb(8, BF), "selu": _sb(16, BF), "rep": _sb(512, BF), "one": _sb(128, BF), "nil": _sb(128, BF),
+    "eio": _sb(256, BF), "es2": _sb(128, BF), "e16": _sb(128, BF), "eo": _sb(80, BF),
+    "ma": ("sbuf", [128, 4, 144], BF), "mb": ("sbuf", [128, 4, 128], BF), "mc": ("sbuf", [128, 4, 128], BF),
+    "mw": ("sbuf", [128, 4, 8], F32),
 }
-for _b in ("X0", "Y0", "Z0", "X1", "Y1", "Z1", "S0", "S1"):
+for _b in ("X0", "Y0", "X1", "Y1", "Z", "T", "S0", "S1"):
     SCRATCH["P" + _b] = ("psum", [128, 512], F32)
-SEMAPHORES = ["cV", "cA", "cP", "cG"] + ["s%d" % i for i in range(140)]
+SEMAPHORES = ["cV", "cA", "cP", "cG"] + ["s%d" % i for i in range(146)]
 
-OV, LEANS, PASSES, STAG, VAL = 30.0, (4000.0, 5000.0, 6000.0), 5, 0.0, 0.0
-CY, PCY, GA, HOP = 1.0, 0.5, 1.6, 120.0
+OV, CY, PCY, GA, HOP, DM, DB = 40.0, 0.9, 0.45, 1.25, 100.0, 2000.0, 0.24
+LEANS, PASSES, NEAR, FAR = (0.5, 1.0, 2.0), 4, 300.0, 4000.0
 
 
 def build(g, core, T, topo):
     rank = T.rank_of(core)
     n = len(T.cores)
-    ops, acc, nsem, lead = [], {}, [0], [0.0]
+    ops, acc, nsem = [], {}, [0]
 
     def A(name, a=0, b=None, s=1, p0=0, p1=128, ps=1):
         if b is None:
-            b = SCRATCH[name][1][1]
-        if name in ("ohw", "g1o"):
-            a, b = (a, b) if name == "ohw" else (a + 12288, b + 12288)
-            name = "cw"
+            b = NW if name == "wu" else SCRATCH[name][1][1]
+        if name == "wu":
+            name, a, b = "ohw", a + 8192, b + 8192
         return (T[name][p0:p1:ps, a:b:s], (name, a, b))
 
-    def add(eng, fn, rd, wr, occ, lat=None, kind="c", after=()):
+    def add(eng, fn, rd, wr, occ, lag=0.0, kind="c", after=(), lean=NEAR, big=0.0):
         i = len(ops)
         deps = dict((j, True) for j in after)
         for regs, w in ((rd, False), (wr, True)):
@@ -71,7 +72,9 @@ def build(g, core, T, topo):
                 if w:
                     acc[nm] = [x for x in acc[nm] if not (a <= x[1] and x[2] <= b)]
                 acc[nm].append((i, a, b, w))
-        ops.append(dict(eng=eng, fn=fn, deps=deps, occ=occ, lat=occ if lat is None else lat, kind=kind, lead=lead[0],
+        if not isinstance(occ, dict):
+            occ = dict((e, occ) for e in eng or " ")
+        ops.append(dict(eng=eng, fn=fn, deps=deps, occ=occ, lag=lag, kind=kind, lean=lean, big=big,
                         banks=sorted(set(x[0] for x in list(rd) + list(wr) if x[0][0] == "P"))))
         return i
 
@@ -80,15 +83,19 @@ def build(g, core, T, topo):
         return "s%d" % (nsem[0] - 1)
 
     def wid(x):
-        return int(x[0].shape[-1]) * (3 if len(x[0].shape) == 3 else 1)
-
-    def two(*xs):
-        return all(SCRATCH[x[1][0]][2] in (BF, U16) for x in xs)
+        k = 1
+        for z in x[0].shape[1:]:
+            k *= int(z)
+        return k
 
     def cost(*xs):
-        return OV + CY * max(64, wid(xs[0]) * (0.5 if two(*xs) else 1))
+        two = all(SCRATCH[x[1][0]][2] in (BF, U16) for x in xs)
+        return OV + CY * max(64, wid(xs[0]) * (0.5 if two else 1))
 
-    def ts(o, i, s1, s2, op0, op1=None, after=()):
+    def both(o, i):
+        return {"A": OV + CY * max(64, wid(o)), "V": cost(o, i)}
+
+    def ts(o, i, s1, s2, op0, op1=None):
         rd = [i[1]] + [s[1] for s in (s1, s2) if isinstance(s, tuple)]
         v1 = s1[0] if isinstance(s1, tuple) else s1
         v2 = s2[0] if isinstance(s2, tuple) else s2
@@ -96,7 +103,7 @@ def build(g, core, T, topo):
             fn = lambda q, e: [q.tensor_scalar(o[0], i[0], v1, None, op0)]
         else:
             fn = lambda q, e: [q.tensor_scalar(o[0], i[0], v1, v2, op0, op1)]
-        return add("V", fn, rd, [o[1]], cost(o, i), after=after)
+        return add("V", fn, rd, [o[1]], cost(o, i))
 
     def tt(o, a, b, op):
         k = 1 if "P" in (a[1][0][0], b[1][0][0]) else 2
@@ -105,12 +112,22 @@ def build(g, core, T, topo):
     def cp(o, i):
         return add("V", lambda q, e: [q.tensor_copy(o[0], i[0])], [i[1]], [o[1]], cost(o, i))
 
-    def ev(o, i, scale=1.0, bias=0.0):
+    def ev(o, i, scale=1.0, bias=0.0, relu=False, lean=NEAR):
         def fn(q, e):
             if e == "A":
-                return [q.activation(o[0], i[0], AF.Identity, bias=bias, scale=scale)]
+                return [q.activation(o[0], i[0], AF.Relu if relu else AF.Identity, bias=bias, scale=scale)]
+            if relu:
+                return [q.tensor_scalar(o[0], i[0], bias, 0.0, OP.add, OP.max)]
             return [q.tensor_scalar(o[0], i[0], scale, bias, OP.mult, OP.add)]
-        return add("AV", fn, [i[1]], [o[1]], OV + CY * max(64, wid(o)))
+        return add("AV", fn, [i[1]], [o[1]], both(o, i), lean=lean)
+
+    def gt(o, i, c, up=True, eng="VA"):
+        k = 512.0 if up else -512.0
+        def fn(q, e):
+            if e == "A":
+                return [q.activation(o[0], i[0], AF.Sigmoid, bias=-k * c, scale=k)]
+            return [q.tensor_scalar(o[0], i[0], c, None, OP.is_gt if up else OP.is_lt)]
+        return add(eng, fn, [i[1]], [o[1]], both(o, i), lean=50.0)
 
     def ms(o, v):
         return add("V", lambda q, e: [q.memset(o[0], v)], [], [o[1]], cost(o))
@@ -122,17 +139,21 @@ def build(g, core, T, topo):
             fn = lambda q, e: [q.iota(o[0], pat, base, cm, allow_small_or_imprecise_dtypes=True)]
         return add("G", fn, [], [o[1]], 150 + 2 * CY * wid(o))
 
-    def mm(o, pairs):
+    def mm(o, pairs, first=True, final=True, left=None, wr=()):
         def fn(q, e):
-            return [q.matmul(o[0], l[0], r[0], k == 0, k == len(pairs) - 1) for k, (l, r) in enumerate(pairs)]
-        return add("P", fn, [x[1] for pr in pairs for x in pr], [o[1]],
-                   60 + len(pairs) * (10 + PCY * max(64, wid(o)) * (4 if pairs[0][0][1][0] == "idf" else 1)))
+            stop = final
+            if left is not None:
+                left[0] -= 1
+                stop = left[0] == 0
+            return [q.matmul(o[0], l[0], r[0], first and k == 0, stop and k == len(pairs) - 1) for k, (l, r) in enumerate(pairs)]
+        return add("P", fn, [x[1] for pr in pairs for x in pr] + ([] if first else [o[1]]), [o[1]] + list(wr),
+                   len(pairs) * (10 + PCY * max(64, wid(o)) * (4 if pairs[0][0][1][0] == "idf" else 1)), 60)
 
-    def gat(o, win, off, eng="AV"):
+    def gat(o, win, off, lean=NEAR):
         def fn(q, e):
             src = win[0].indirect(off[0])
             return [q.activation(o[0], src, AF.Copy) if e == "A" else q.tensor_copy(o[0], src)]
-        return add(eng, fn, [win[1], off[1]], [o[1]], 65 + GA * wid(o))
+        return add("AV", fn, [win[1], off[1]], [o[1]], 60 + GA * wid(o), lean=lean)
 
     def gge(o, win, off, thr, d):
         pos, neg = A(thr, d, d + 1), A(thr, 4 + d, 5 + d)
@@ -141,25 +162,26 @@ def build(g, core, T, topo):
             if e == "A":
                 return [q.activation(o[0], src, AF.Sign, bias=neg[0])]
             return [q.tensor_scalar(o[0], src, pos[0], 0.5, OP.is_ge, OP.subtract)]
-        return add("AV", fn, [win[1], off[1], (thr, 0, 8)], [o[1]], 65 + GA * wid(o))
+        return add("AV", fn, [win[1], off[1], (thr, 0, 8)], [o[1]], 60 + GA * wid(o))
 
-    def gmul(o, win, off, b, op=OP.mult):
-        return add("V", lambda q, e: [q.tensor_tensor(o[0], win[0].indirect(off[0]), b[0], op)],
+    def gmul(o, win, off, b):
+        return add("V", lambda q, e: [q.tensor_tensor(o[0], win[0].indirect(off[0]), b[0], OP.mult)],
                    [win[1], off[1], b[1]], [o[1]], 55 + GA * wid(o))
 
-    def dma(o, i, rd, wr, lat, eng="S", twin=None):
+    def dma(o, i, rd, wr, nb=0, eng="S", twin=None):
+        fn = lambda q, e: [q.dma_start(o, i)]
         if twin is None:
-            k = add(eng, lambda q, e: [q.dma_start(o, i)], rd, wr, 100, lat, kind="d")
+            k = add(eng, fn, rd, wr, 80, DM + DB * nb, kind="d", big=DB * nb)
             ops[k]["sem"] = [sem(), 16]
         else:
-            k = add(eng, lambda q, e: [q.dma_start(o, i)], rd, [], 100, lat, kind="d", after=list(ops[twin]["deps"]))
+            k = add(eng, fn, rd, [], 80, DM + DB * nb, kind="d", after=list(ops[twin]["deps"]), big=DB * nb)
             for nm, a, b in wr:
                 acc[nm].append((k, a, b, True))
             ops[k]["sem"] = ops[twin]["sem"]
             ops[k]["sem"][1] += 16
         return k
 
-    def send(parts, lat, wr=()):
+    def send(parts, nb, wr=()):
         ls, rs = sem(), [sem() for _ in parts]
         trs, cnt = [], []
         for k, (ahead, src, dst) in enumerate(parts):
@@ -170,31 +192,29 @@ def build(g, core, T, topo):
             trs.append(RemoteDMATransfer(dst_ids=[DstId(rid=rid, pnc=pid)], dma_engine_mask=sum(1 << x for x in en[k * m:(k + 1) * m]),
                                          remote_sem=T.sem[rs[k]], src=src[0], dst=dst[0]))
             cnt.append(m)
-        i = add("G", lambda q, e: [q.remote_dma_fused(trs, local_sem=T.sem[ls])], [p[1][1] for p in parts], list(wr), 400, lat, kind="r")
+        i = add("G", lambda q, e: [q.remote_dma_fused(trs, local_sem=T.sem[ls])], [p[1][1] for p in parts], list(wr),
+                400, DM + 2 * DB * nb, kind="r", big=2 * DB * nb)
         ops[i]["tok"] = (ls, sum(cnt))
         for k, p in enumerate(parts):
             j = add("", None, [], [p[2][1]], 0, 300, kind="a", after=[i])
             ops[j]["tok"] = (rs[k], cnt[k])
 
     for k in range(2):
-        dma(T.w1[:, k * 2048:(k + 1) * 2048], T.wt[:, k * 2048:(k + 1) * 2048], [], [("w1", k * 2048, (k + 1) * 2048)], 3200, "SA"[k])
-    dma(T.bni[:], T.bn[:], [], [("bni", 0, 768)], 2600, "A")
-    dma(T.taus[:, 0:3], T.tau[:], [], [("taus", 0, 4)], 2200)
-    dma(T.fa[:], T.ft[:], [], [("fa", 0, NW)], 5000)
-    dma(T.di[0:8, :], T.lab[:], [], [("di", 0, 512)], 2500)
-    dma(T.xvs[:], T.xv[:], [], [("xvs", 0, 768)], 2500)
+        dma(T.w1[:, k * 2048:(k + 1) * 2048], T.wt[:, k * 2048:(k + 1) * 2048], [], [("w1", k * 2048, (k + 1) * 2048)], 4096, "SA"[k])
+    dma(T.bni[:, 0:256], T.bn[:, 0:256], [], [("bni", 0, 256)], 1024, "A")
+    dma(T.taus[:, 0:3], T.tau[:], [], [("taus", 0, 4)])
+    dma(T.bni[:, 256:768], T.bn[:, 256:768], [], [("bni", 256, 768)], 2048)
+    dma(T.fa[:], T.ft[:], [], [("fa", 0, NW)], 8192)
+    dma(T.di[0:8, :], T.lab[:], [], [("di", 0, 512)])
+    dma(T.xvs[:], T.xv[:], [], [("xvs", 0, 768)], 1536)
 
     def send_w(v, k):
         half = A("w1", k * 2048, (k + 1) * 2048)
-        send([(-1, half, A("w2%d" % (v % 2), k * 2048, (k + 1) * 2048))], 3500)
-
-    def send_w3(v, k):
-        half = A("w1", k * 2048, (k + 1) * 2048)
         slot = 2 * v + k
-        send([(-2, half, (T.wd[slot], ("wd", slot, slot + 1)))], 4000)
+        send([(-1, half, A("w2%d" % (v % 2), k * 2048, (k + 1) * 2048)), (-2, half, (T.wd[slot], ("wd", slot, slot + 1)))], 8192)
         c = slice(k * 2048, (k + 1) * 2048)
-        j = dma(T.w3[0:112, c], T.wd[slot, 16:128, :], [("wd", slot, slot + 1)], [("w3", k * 2048, (k + 1) * 2048)], 3000)
-        dma(T.w3[112:128, c], T.wd[slot, 0:16, :], [("wd", slot, slot + 1)], [("w3", k * 2048, (k + 1) * 2048)], 3000, twin=j)
+        j = dma(T.w3[0:112, c], T.wd[slot, 16:128, :], [("wd", slot, slot + 1)], [("w3", k * 2048, (k + 1) * 2048)], 4096)
+        dma(T.w3[112:128, c], T.wd[slot, 0:16, :], [("wd", slot, slot + 1)], [("w3", k * 2048, (k + 1) * 2048)], twin=j)
 
     ta = A("taus", 0, 3)
     cp(A("tb", 0, 3), ta)
@@ -208,11 +228,9 @@ def build(g, core, T, topo):
     ts(A("th", 4, 7), A("tw", 0, 3), -1.0, -0.01, OP.mult, OP.min)
     send_w(0, 0)
     send_w(0, 1)
-    send([(-1, A("th"), A("th2")), (-2, A("th"), (T.thd[:], ("thd", 0, 8)))], 2500)
-    send_w3(0, 0)
-    send_w3(0, 1)
-    dma(T.th3[0:112, :], T.thd[16:128, :], [("thd", 0, 8)], [("th3", 0, 4)], 2200)
-    dma(T.th3[112:128, :], T.thd[0:16, :], [("thd", 0, 8)], [("th3", 4, 8)], 2200)
+    send([(-1, A("th"), A("th2")), (-2, A("th"), (T.thd[:], ("thd", 0, 8)))], 0)
+    j = dma(T.th3[0:112, :], T.thd[16:128, :], [("thd", 0, 8)], [("th3", 0, 8)])
+    dma(T.th3[112:128, :], T.thd[0:16, :], [("thd", 0, 8)], [("th3", 0, 8)], twin=j)
 
     C = lambda j: A("col", j, j + 1)
     iota(A("pc", 0, 1), [[0, 1]], 0, 1)
@@ -220,9 +238,11 @@ def build(g, core, T, topo):
     iota(A("dif"), [[1, 128]], 0, -1)
     iota(A("gq"), [[1, 8], [0, 16]], 0, 0)
     iota(A("eio"), [[1, 256]], 0, 0)
-    iota(A("cs", 0, 512), [[16, 8], [1, 2], [0, 32]], 0, -1)
-    iota(A("cs", 512, 528), [[16, 8], [1, 2]], 0, -1)
-    iota(A("nio"), [[0, 16], [-1, 32]], 16, 0)
+    iota(A("eo"), [[128, 2], [0, 5], [16, 8]], 0, 0)
+    iota(A("t1", 0, 512), [[16, 8], [1, 2], [0, 32]], 0, -1)
+    iota(A("t1", 512, 528), [[16, 8], [1, 2]], 0, -1)
+    iota(A("t3", 0, 512, p1=32), [[0, 16], [-1, 32]], 16, 0)
+    iota(A("t3", 512, 1024, p1=32), [[1, 8], [0, 64]], 0, -1)
     ts(A("pc", 2, 3), A("pc", 0, 1), 4, None, OP.arith_shift_right)
     ts(A("pc", 4, 5), A("pc", 0, 1), 15, None, OP.bitwise_and)
     cp(C(0), A("pc", 2, 3))
@@ -230,184 +250,230 @@ def build(g, core, T, topo):
     ts(C(2), C(0), 16.0, 15.0, OP.mult, OP.add)
     ts(A("km"), A("q144", 0, 16), C(1), None, OP.is_equal)
     K = lambda j: A("km", j, j + 1)
-    ROWS = ((0, 4), (8, 12), (1, 5))
     BIG = lambda j, m: A("big", 144 * j + 15 - m, 144 * j + 143 - m)
+    ts(C(3), K(0), 128.0, K(4), OP.mult, OP.add)
+    ts(C(4), K(15), -20480.0, C(3), OP.mult, OP.add)
+    ts(C(5), K(8), 256.0, None, OP.mult)
+    ts(C(6), K(15), -256.0, 256.0, OP.mult, OP.add)
     ts(A("big", 0, 144), A("q144"), C(2), None, OP.is_equal)
-    for t in range(EP):
-        ts(C(3 + t), K(ROWS[t][0]), 128.0, K(ROWS[t][1]), OP.mult, OP.add)
-        ts(A("big", 144 * (1 + t), 144 * (2 + t)), A("q144"), C(2), C(3 + t), OP.is_equal, OP.mult)
-    ts(C(6), K(8), 256.0, None, OP.mult)
-    ts(A("big", 576, 720), A("q144"), C(2), C(6), OP.is_equal, OP.mult)
+    for j in range(1, 5):
+        ts(A("big", 144 * j, 144 * j + 144), A("q144"), C(2), C(2 + j), OP.is_equal, OP.mult)
     ts(A("idn"), A("dif"), 0.0, None, OP.is_equal)
     ts(A("blk"), A("gq"), C(0), None, OP.is_equal)
-    ts(A("tmpm"), A("dif"), 0.0, None, OP.is_ge)
+    gt(A("tmpm"), A("dif"), -0.5, eng="A")
     tt(A("tri", 128, 256), A("tmpm"), A("blk"), OP.mult)
-    ts(C(7), C(1), -1.0, 15.0, OP.mult, OP.add)
-    ts(C(8), C(7), 4.0, None, OP.min)
+    ts(C(7), C(1), 11.5, -1.0, OP.is_gt, OP.mult)
+    ts(C(8), C(7), 4.0, None, OP.add)
     ts(A("tri", 0, 128), A("tri", 128, 256), C(8), None, OP.mult)
-    for j in range(4):
-        ts(C(9 + j), C(1), float(j), 256.0, OP.is_ge, OP.mult)
-        ts(A("i256", 128 * j, 128 * j + 128), A("dif"), 0.0, C(9 + j), OP.is_equal, OP.mult)
+    ms(A("tri", 15, 128, 16), 0.0)
+    ts(A("i256"), A("idn"), 256.0, None, OP.mult)
     for j in range(1, 4):
         o = A("shf", 128 * j - 128, 128 * j)
         ts(A("tmpm"), A("dif"), float(j), None, OP.is_equal)
         tt(o, A("tmpm"), A("blk"), OP.mult)
         tt(o, A("idn"), o, OP.subtract)
-    ts(A("es1"), A("eio"), 1.0 / 256, None, OP.mult)
-    ts(A("es2"), A("eio", 0, 128), 1.0 / 128, None, OP.mult)
-    ts(A("e16"), A("eio", 0, 128), 16.0, None, OP.mult)
+    ev(A("es2"), A("eio", 0, 128), 1.0 / 128)
+    ev(A("e16"), A("eio", 0, 128), 16.0)
+    ts(A("eo"), A("eo"), C(1), None, OP.add)
+    ts(A("g8"), A("q144", 0, 8), C(0), None, OP.is_equal)
+    MW = lambda m, a, b: (T.mw[:, m, a:b], ("mw", 8 * m + a, 8 * m + b))
+    ts(MW(0, 0, 5), A("q144", 0, 5), 0.0, C(3), OP.mult, OP.add)
+    ts(A("col", 24, 28), A("km", 1, 16, 4), 128.0, None, OP.mult)
+    tt(MW(1, 0, 4), A("col", 24, 28), A("km", 2, 16, 4), OP.add)
+    cp(MW(1, 4, 5), MW(1, 3, 4))
+    ts(A("col", 28, 32), A("q144", 0, 4), C(1), None, OP.add)
+    ts(MW(2, 0, 4), A("col", 28, 32), 14.0, -8192.0, OP.is_equal, OP.mult)
+    ts(MW(2, 4, 5), K(14), -8192.0, None, OP.mult)
+    ts(MW(3, 0, 4), A("q144", 0, 4), K(15), 1.0, OP.mult, OP.add)
+    tt(C(9), K(15), K(11), OP.subtract)
+    ts(MW(3, 4, 5), C(9), 3.0, 1.0, OP.mult, OP.add)
+    ms((T.ma[:], ("ma", 0, 144)), 0.0)
+    ms((T.mc[:], ("mc", 0, 8)), 0.0)
+    for gr in range(8):
+        ts((T.ma[:, :, 16 * gr + 12:16 * gr + 16], ("ma", 16 * gr + 12, 16 * gr + 16)), (T.mw[:, :, 0:4], ("mw", 0, 32)),
+           A("g8", gr, gr + 1), None, OP.mult)
+    cp((T.mb[:], ("mb", 0, 8)), (T.ma[:, :, 0:128], ("ma", 0, 144)))
+    ms((T.mb[:, :, 15:128:16], ("mb", 0, 8)), 0.0)
+    for m in range(4):
+        ts((T.mc[:, m, 15:128:16], ("mc", m, m + 1)), A("g8"), MW(m, 4, 5), None, OP.mult)
+
+    def MAT(m, j):
+        if j < 3:
+            return (T.ma[:, m, 12 - 4 * j:140 - 4 * j], ("ma", 0, 144))
+        return (T.mb[:, m, :], ("mb", 0, 8)) if j == 3 else (T.mc[:, m, :], ("mc", m, m + 1))
+
     cp(A("l1u", 0, 256), A("bni", 0, 256))
     cp(A("l1u", 256, 768), A("bni", 256, 768))
-    ms(A("bw", 0, 4096), 0.0)
-    for a in range(0, 768, 256):
-        ts(A("ti"), A("bni", a, a + 256), 7, None, OP.arith_shift_right)
-        ts(A("bh", a, a + 256), A("ti"), -16.0, None, OP.add)
-        ts(A("tj"), A("bni", a, a + 256), 127, None, OP.bitwise_and)
-        cp(A("bl", a, a + 256), A("tj"))
-    tt(C(13), K(0), K(8), OP.add)
-    tt(C(13), C(13), K(1), OP.add)
-    ts(C(14), C(13), -112.0, 127.0, OP.mult, OP.add)
-    ts(C(15), C(13), -16.0, None, OP.mult)
-    ts(A("bw", 4096, 4352), A("eio"), 0.0, C(14), OP.mult, OP.add)
-    ts(A("bw", 4352, 4608), A("eio"), 0.0, C(15), OP.mult, OP.add)
+    ms(A("bw0", 0, 4096), 1.0)
+    BD = lambda t, d, a=0, b=256: A("bdg", 512 * t + 256 * d + a, 512 * t + 256 * d + b)
     for t in range(EP):
-        for k, nm in enumerate(("bh", "bl")):
-            j = 2 * t + k
-            dma(T.bw[ROWS[t][k]:128:16, 0:4096], T[nm][:, 256 * t:256 * t + 256], [(nm, 256 * t, 256 * t + 256), ("bw", 6, 4096)], [("bw", j, j + 1)], 2600)
-    for j, nm in enumerate(("bh", "bl")):
-        dma(T.bd[j, 0:128, :], T[nm][:], [(nm, 0, 768)], [("bd", 2 * j, 2 * j + 1)], 2600)
-        dma(T.bd[j, 128:144, :], T[nm][0:16, :], [(nm, 0, 768)], [("bd", 2 * j + 1, 2 * j + 2)], 2600)
-    ts(C(17), K(4), 127.0, None, OP.mult)
-    ts(C(18), K(8), -16.0, C(17), OP.mult, OP.add)
-    ts(C(19), K(0), 15.0, C(18), OP.mult, OP.add)
-    ts(A("cw", 16384, 16400), A("eio", 0, 16), 0.0, C(19), OP.mult, OP.add)
-    ts(A("i4k"), A("i256", 128, 512), 16.0, None, OP.mult)
-    tt(C(16), C(14), K(8), OP.add)
+        a = 256 * t
+        ts(A("ti"), A("bni", a, a + 256), 7, None, OP.arith_shift_right)
+        ts(BD(t, 0), A("ti"), -16.0, None, OP.add)
+        ts(A("li"), A("bni", a, a + 256), 127, None, OP.bitwise_and)
+        cp(BD(t, 1), A("li"))
+    ts(C(10), K(0), -17.0, 1.0, OP.mult, OP.add)
+    tt(C(10), C(10), K(4), OP.subtract)
+    ts(A("bw0", 4096, 4352), A("eio"), 0.0, C(10), OP.mult, OP.add)
+    for a, b in ((0, 512), (512, 1536)):
+        k = dma(T.bd[:, 0:16, a:b], T.bdg[:, a:b], [("bdg", a, b)], [("bd", a, b)])
+        for j in range(3):
+            dma(T.bd[:, 16 + j, a:b], T.bdg[13 + j:128:16, a:b], [("bdg", a, b)], [("bd", a, b)], twin=k)
+
+    def window(t):
+        w, k = "bw%d" % (t % 2), None
+        for r in range(4, -1, -1):
+            for d in range(2):
+                a = 512 * t + 256 * d
+                if r == 0:
+                    o, i, rd = T[w][4 * d:128:16, 0:4096], T.bdg[:, a:a + 256], ("bdg", a, a + 256)
+                else:
+                    m = 15 if r == 4 else 16
+                    o, i, rd = T[w][4 * r - 3 + d:128:16, 0:256 * m], T.bd[:, r:r + m, a:a + 256], ("bd", a, a + 256)
+                z = dma(o, i, [rd], [(w, 0, 4096)], 800, twin=k)
+                k = z if k is None else k
+
+    window(0)
+    dma(T.bw1[:], T.bw0[:], [("bw0", 0, 4352)], [("bw1", 0, 4352)], 8704)
+    window(1)
+    ts(C(11), K(0), 174.0, 1.0, OP.mult, OP.add)
+    ts(C(12), K(4), 126.0, C(11), OP.mult, OP.add)
+    ts(C(13), K(8), 15.0, C(12), OP.mult, OP.add)
     for h in range(2):
-        for a in range(0, 2048, 512):
-            iota(A("dw%d" % h, a, a + 512), [[0, 512]], 0, 0)
-        ts(A("dw%d" % h, 2048, 2176), A("eio", 0, 128), 0.0, C(16), OP.mult, OP.add)
+        dma(T["dw%d" % h][:, 0:2048], T.bw0[:, 0:2048], [("bw0", 0, 2048)], [("dw%d" % h, 0, 2048)], 4096)
+        ts(A("dw%d" % h, 2048, 2176), A("eio", 0, 128), 0.0, C(13), OP.mult, OP.add)
         ms(A("v2%d" % h, 2048, 2064), 0.0)
-    ts(A("g8"), A("q144", 0, 8), C(0), None, OP.is_equal)
     ts(A("ni8"), A("dif", 0, 8), 0.0, -1.0, OP.is_equal, OP.mult)
-    ts(A("rep"), A("cs", 0, 512), 0.0, None, OP.is_equal)
-    ts(A("selu"), A("cs", 512, 528), 0.0, None, OP.is_equal)
+    ts(A("rep"), A("t1", 0, 512), 0.0, None, OP.is_equal)
+    ts(A("selu"), A("t1", 512, 528), 0.0, None, OP.is_equal)
     ms(A("one"), 1.0)
+    ms(A("nil"), 0.0)
     ts(A("idf"), A("dif"), 0.0, None, OP.is_equal)
     for k in range(16):
         ts(A("sel", 128 * k, 128 * k + 128), A("blk"), K(k), None, OP.mult)
-    cp(A("labb", p1=8), A("di", p1=8))
-    dma(T.di[0:8, :], T.ask[:], [], [("di", 0, 512)], 2500)
+    ts(C(14), K(9), -160.0, None, OP.mult)
+    ts(A("t3", 0, 512, p1=32), A("t3", 0, 512, p1=32), A("km", 8, 9, p1=32), A("col", 14, 15, p1=32), OP.mult, OP.add)
+    ts(A("t3", 512, 1024, p1=32), A("t3", 512, 1024, p1=32), 0.0, 64.0, OP.is_equal, OP.mult)
+    tt(A("rx", p1=32), A("t3", 0, 512, p1=32), A("t3", 512, 1024, p1=32), OP.add)
+    ms(A("labx", p1=32), 1.0)
+    ts(A("labx", p1=8), A("di", p1=8), -1.0, 1.0, OP.mult, OP.add)
+    dma(T.di[0:8, :], T.ask[:], [], [("di", 0, 512)])
     cp(A("askb", p1=8), A("di", p1=8))
     for j in range(4):
-        mm(A("PS0", 8 * j, 8 * j + 8), [(A("labb", 128 * j, 128 * j + 128, p1=8), A("idn", 0, 8, p1=8))])
-    ev(A("fab", 0, 32), A("PS0", 0, 32), -2049.0, 1.0)
-    ev(A("fab", 32, 64), A("PS0", 0, 32), 2048.0, 0.0)
+        mm(A("PS0", 8 * j, 8 * j + 8), [(A("labx", 128 * j, 128 * j + 128, p1=8), A("idn", 0, 8, p1=8))])
+    ev(A("fab"), A("PS0", 0, 32), -2049.0, 2048.0)
 
     def wide(nm, h, k):
         return A(nm, 2048 * h + k, 2048 * h + 2048, 16)
+
+    def gather(nm, h, win, lst, a):
+        for s in range(0, 2048, QG):
+            gat(A(nm, 2048 * h + s, 2048 * h + s + QG), A(win), A(lst, a + s // 16, a + (s + QG) // 16))
 
     def strong(h, d, win, thr, lst, a):
         for s in range(0, 2048, QG):
             gge(A("ge", 2048 * h + s, 2048 * h + s + QG), A(win), A(lst, a + s // 16, a + (s + QG) // 16), thr, d)
         x = A("PX%d" % h, 0, 128)
         mm(x, [(BIG(0, k), wide("ge", h, k)) for k in range(16)])
-        ts(A("st", 384 * h + 128 * d, 384 * h + 128 * d + 128), x, 0.0, None, OP.is_gt)
+        gt(A("st", 384 * h + 128 * d, 384 * h + 128 * d + 128), x, 0.5)
 
-    def children(t, h, d):
-        X, Y, Z = "PX%d" % h, "PY%d" % h, "PZ%d" % h
+    def names(t, h, d):
+        Y = "PY%d" % h
         c = lambda nm, j=0, w=1: A(nm, 128 * (w * h + j), 128 * (w * h + j) + 128)
-        st = c("st", d, 3)
-        if d == 0:
-            mm(A(X, 128, 256), [(A("tri", 0, 128), st)])
-        else:
-            tt(c("nb"), st, c("cap"), OP.mult)
-            mm(A(X, 128, 256), [(A("tri", 128, 256), c("nb"))])
+        tt(A(Y, 128, 256), c("ls"), A(Y, 128, 256), OP.mult)
+        tt(c("ti"), c("uu"), A(Y, 128, 256), OP.add)
+        ts(c("li"), c("ti"), 5, NW - 1, OP.arith_shift_right, OP.bitwise_and)
+        cp(c("lu", d, 2), c("li"))
+        if d == 0 or t < EP - 1:
+            ts(c("dh", d, 2), c("lu", d, 2), 1.0 / 128, 143.50390625, OP.mult, OP.add)
+            ts(c("di", d, 2), c("ti"), 5, 127, OP.arith_shift_right, OP.bitwise_and)
+            cp(c("dl", d, 2), c("di", d, 2))
+
+    def second(t, h):
+        X, Y = "PX%d" % h, "PY%d" % h
+        c = lambda nm, j=0, w=1: A(nm, 128 * (w * h + j), 128 * (w * h + j) + 128)
+        mm(A(X, 128, 256), [(A("tri", 0, 128), c("st", 0, 3))])
+        ev(c("endb"), A(X, 128, 256))
+        cm = lambda j: A("ge", 2048 * h + 128 * j, 2048 * h + 128 * j + 128)
+        for j, th in enumerate((0.5, 4.5, 8.5, 12.5, 15.5)):
+            gt(cm(j), c("endb"), th, False)
+        mm(A(X, 0, 40), [(BIG(4, b), A("ge", 2048 * h + b, 2048 * h + 640, 16)) for b in range(16)]
+           + [(A("idn"), A("eo", 40 * h, 40 * h + 40))])
+        o = A("o1", 128 * h, 128 * h + 40)
+        cp(o, A(X, 0, 40))
+        gat(A("g1o", 2048 * h, 2048 * h + 640), A("bw%d" % (t % 2)), o)
+        gp = lambda j: A("g1o", 2048 * h + 128 * j, 2048 * h + 128 * j + 128)
+        mm(A(Y, 256, 384), [(MAT(3, j), cm(j)) for j in range(5)])
+        ev(c("l2"), A(Y, 256, 384))
+        ts(A(Y, 256, 384), A(Y, 256, 384), -15.0, -4.0, OP.add, OP.max)
+        mm(A(Y, 0, 128), [(MAT(2, j), cm(j)) for j in range(5)] + [(MAT(0, j), gp(j)) for j in range(5)])
+        mm(A(Y, 128, 256), [(MAT(1, j), gp(j)) for j in range(5)])
+        ev(c("ls"), A(Y, 0, 128), 1.0, 3232.0, relu=True)
+        ts(c("uu"), A(Y, 0, 128), -4033.0, 2080.0, OP.max, OP.mult)
+        ts(c("par", 0, 2), c("ls"), -1184.0, None, OP.add)
+        names(t, h, 0)
+        w, k = "dw%d" % h, None
+        for j, src in ((2, c("l2")), (0, c("dh", 0, 2)), (1, c("dl", 0, 2))):
+            z = dma(T[w][4 * j:128:16, 0:2048], src[0], [src[1]], [(w, 0, 2048)], 400, twin=k)
+            k = z if k is None else k
+
+    def third(t, h):
+        X, Y = "PX%d" % h, "PY%d" % h
+        c = lambda nm, j=0, w=1: A(nm, 128 * (w * h + j), 128 * (w * h + j) + 128)
+        tt(c("nb"), c("st", 1, 3), A(Y, 256, 384), OP.mult)
+        mm(A(X, 128, 256), [(A("tri", 128, 256), c("nb"))])
         ev(c("endb"), A(X, 128, 256))
         cm = lambda m: A("ge", 2048 * h + 128 * m, 2048 * h + 128 * m + 128)
         for m in range(16):
-            ts(cm(m), c("endb"), float(m), None, OP.is_le)
-        es = c("es1") if d == 0 else A("es2")
-        kp = A(X, 256, 384)
-        mm(kp, [(BIG(0, m), cm(m)) for m in range(16)] + [(A("idn"), es)])
-        one = d == 0 and t > 0
-        if not one:
-            ts(c("o1"), kp, 256.0 if d == 0 else 128.0, None, OP.mult)
-        tt(c("kb"), kp, es, OP.subtract)
-        for s in range(0, 0 if one else 2048, QG):
-            gat(A("g1o", 2048 * h + s, 2048 * h + s + QG), A("bw" if d == 0 else "dw%d" % h), A("o1", 128 * h + s // 16, 128 * h + (s + QG) // 16))
+            gt(cm(m), c("endb"), -m - 0.5)
+        kp = A(X, 0, 128)
+        mm(kp, [(A("idn"), A("es2"))] + [(BIG(0, m), cm(m)) for m in range(8)], final=False)
+        mm(kp, [(BIG(0, m), cm(m)) for m in range(8, 16)], first=False)
+        ts(c("o1"), kp, 128.0, None, OP.mult)
+        ev(c("kb"), kp, 1.0, 143.50390625)
+        gather("g1o", h, "dw%d" % h, "o1", 128 * h)
         for j in range(3):
-            mm(A(Y, 128 * j, 128 * j + 128), [(A("shf", 128 * j, 128 * j + 128), c("kb"))])
-        ts(A("eq", 384 * h, 384 * h + 384), A(Y, 0, 384), 0.0, None, OP.is_equal)
-        cs = [(A("i256", 128 * j + 128, 128 * j + 256), c("eq", j, 3)) for j in range(3)]
-        ls = [(A("i256", 0, 128), c("kb"))] if d == 0 else [(BIG(4, k), wide("g1o", h, k)) for k in range(16)]
-        if one:
-            ts(c("nb"), c("kb"), 16.0, 64.0, OP.is_equal, OP.mult)
-            mm(A(X, 0, 128), [(A("i4k", 128 * j, 128 * j + 128), c("eq", j, 3)) for j in range(3)]
-               + [(A("idn"), c("eio")), (A("i256", 0, 128), c("nb"))] + ls)
-            ts(c("o2"), A(X, 0, 128), 16384.0, None, OP.min)
-        else:
-            mm(A(X, 0, 128), cs + [(A("idn"), c("eio"))] + ls)
-            ts(c("o2"), A(X, 0, 128), 256.0, 4607.0, OP.add, OP.min)
-        for s in range(0, 2048, QG):
-            gat(A("ge", 2048 * h + s, 2048 * h + s + QG), A("cw" if one else "bw"), A("o2", 128 * h + s // 16, 128 * h + (s + QG) // 16))
-        if d == 1:
-            mm(A(Y, 384, 512), [(A("idn"), c("kb")), (A("idn"), A("e16"))])
-            cp(c("par", 1, 2), A(Y, 384, 512))
-        if d == 0:
-            mm(A(Z, 128, 256), cs + ls)
-            ev(c("l2"), A(Z, 128, 256), 1.0 / 256, 1.0)
-            ev(c("capt"), A(Z, 128, 256), -1.0 / 256, 14.0)
-            ts(c("cap"), c("capt"), 4.0, None, OP.min)
-        mm(A(Y, 0, 128), [(BIG(1, k), wide("ge" if one else "g1o", h, k)) for k in range(16)])
+            mm(A(X, 128 * j + 128, 128 * j + 256), [(A("shf", 128 * j, 128 * j + 128), c("kb"))])
+        gt(A("eq", 384 * h, 384 * h + 384), A(X, 128, 512), 0.5, False, "AV")
+        mm(A(X, 128, 256), [(A("i256"), c("eq", j, 3)) for j in range(3)] + [(A("idn"), c("eio"))]
+           + [(BIG(3, k), wide("g1o", h, k)) for k in range(16)])
+        ts(c("o2"), A(X, 128, 256), 256.0, 4351.0, OP.add, OP.min)
+        gather("ge", h, "bw%d" % (t % 2), "o2", 128 * h)
+        mm(A(Y, 384, 512), [(A("idn"), c("kb")), (A("idn"), A("e16"))])
+        ts(c("par", 1, 2), A(Y, 384, 512), -144.0, None, OP.add)
+        mm(A(Y, 0, 128), [(BIG(2, k), wide("g1o", h, k)) for k in range(16)])
         ev(c("ls"), A(Y, 0, 128), 1.0, 3232.0)
-        if d == 0:
-            ts(c("par", 0, 2), c("ls"), -1184.0, None, OP.add)
-        ev(c("uu"), c("ls"), 65.0, 75776.0 - 65 * 1184 + 409600)
-        mm(A(Z, 0, 128), [(BIG(2 if one else 1 + t, k), wide("ge", h, k)) for k in range(16)])
-        tt(c("ti"), c("ls"), A(Z, 0, 128), OP.mult)
-        ts(c("tj"), c("ti"), 5, None, OP.arith_shift_right)
-        tt(c("ti"), c("tj"), c("uu"), OP.add)
-        ts(c("li"), c("ti"), NW - 1, None, OP.bitwise_and)
-        cp(c("lu", d, 2), c("li"))
-        if d == 0 or t < EP - 1:
-            ts(c("di", 0, 2), c("li"), 7, None, OP.arith_shift_right)
-            ts(c("dh", d, 2), c("di", 0, 2), -16.0, None, OP.add)
-            ts(c("di", 1, 2), c("li"), 127, None, OP.bitwise_and)
-            cp(c("dl", d, 2), c("di", 1, 2))
-        if d == 0:
-            w = "dw%d" % h
-            k = None
-            for j, src in ((2, c("l2")), (0, c("dh", 0, 2)), (1, c("dl", 0, 2))):
-                z = dma(T[w][4 * j:128:16, 0:2048], src[0], [src[1]], [(w, 0, 2048)], 2300, twin=k)
-                k = z if k is None else k
+        ev(c("uu"), A(Y, 0, 128), 2080.0)
+        mm(A(Y, 128, 256), [(BIG(1, k), wide("ge", h, k)) for k in range(16)])
+        names(t, h, 1)
 
-    def marks(h, d, hi, lo):
-        Z, S = "PZ%d" % h, "PS%d" % h
-        mm(A(Z, 256, 272), [(lo, A("selu"))])
+    def marks(t, h, d, hi, lo):
+        Y, S = "PY%d" % h, "PS%d" % h
+        mm(A(Y, 384, 400), [(lo, A("selu"))])
         a = 48 * h + 16 * d
-        ev(A("lot", a, a + 16), A(Z, 256, 272))
+        ev(A("lot", a, a + 16), A(Y, 384, 400))
         for j in range(16):
             ts(A("ohw", 128 * (a + j), 128 * (a + j) + 128), A("eio", 0, 128), A("lot", a + j, a + j + 1), None, OP.is_equal)
-        mm(A(S), [(hi, A("rep")), (A("one", p1=1), A("nio", p1=1))])
-        ev((T["xs%d" % h][:, d, :], ("xs%d" % h, 8 * d, 8 * d + 8)), A(S))
+        e0, k = 256 * t + 128 * h, 10 if d else 9
+        mm(A(S), [(hi, A("rep")), (A("labx", e0, e0 + 128, p1=k), A("rx", p1=k))])
+        ev((T["xs%d" % h][:, d, :], ("xs%d" % h, 8 * d, 8 * d + 8)), A(S), lean=FAR)
 
     def values12(t, h):
         for s in range(0, 2048, QV):
             a, b = s // 16, (s + QV) // 16
             l1 = A("l1u", 256 * t + 128 * h + a, 256 * t + 128 * h + b)
             l2 = A("lu", 256 * h + a, 256 * h + b)
-            vp = A("v1p", s, s + QV)
-            gat(vp, A("fa"), A("par", 256 * h + a, 256 * h + b))
+            vp = A("v1p", s % 1024, s % 1024 + QV)
+            gat(vp, A("fa"), A("par", 256 * h + a, 256 * h + b), FAR)
             gmul(A("v2%d" % h, s, s + QV), A("fa"), l2, vp)
             gmul(A("t2", 2048 * h + s, 2048 * h + s + QV), A("w2%d" % (t % 2)), l2, A("v2%d" % h, s, s + QV))
-            gat(A("t1", s % 1024, s % 1024 + QV), A("fw1"), l1)
+            gat(A("t1", s % 1024, s % 1024 + QV), A("fw1"), l1, FAR)
             if (s + QV) % 1024 == 0:
                 plus(2048 * h + s + QV - 1024, "t1")
 
     def plus(r, nm):
         o, x = A("t2", r, r + 1024), A(nm)
-        k = add("G", lambda q, e: [q.dma_start(o[0], x[0], accum_op=OP.add)], [x[1], o[1]], [o[1]], 1000, 3500, kind="d")
+        k = add("G", lambda q, e: [q.dma_start(o[0], x[0], accum_op=OP.add)], [x[1], o[1]], [o[1]], 1000, DM + DB * 8192, kind="d", big=DB * 8192)
         ops[k]["sem"] = [sem(), 16]
 
     def values3(t, h):
@@ -415,7 +481,7 @@ def build(g, core, T, topo):
             a, b = s // 16, (s + QV) // 16
             l3 = A("lu", 256 * h + 128 + a, 256 * h + 128 + b)
             x = A("t3", s % 1024, s % 1024 + QV)
-            gat(x, A("v2%d" % h), A("par", 256 * h + 128 + a, 256 * h + 128 + b))
+            gat(x, A("v2%d" % h), A("par", 256 * h + 128 + a, 256 * h + 128 + b), FAR)
             gmul(x, A("fw3"), l3, x)
             if (s + QV) % 1024 == 0:
                 r = s + QV - 1024
@@ -424,10 +490,11 @@ def build(g, core, T, topo):
                     sums += [(A("idf"), A("t3", k, 1024, 16)) for k in range(16)]
                 else:
                     plus(2048 * h + r, "t3")
-                mm(A("PZ%d" % h, 384 + r // 16, 448 + r // 16), sums)
+                for k in range(0, len(sums), 4):
+                    mm(A("PZ", 128 * h + r // 16, 128 * h + 64 + r // 16), sums[k:k + 4], k == 0, k + 4 == len(sums), wr=[("zt", 0, 1)])
         e0, ys = 256 * t + 128 * h, A("ys", 128 * h, 128 * h + 128)
-        tt(ys, A("xvs", e0, e0 + 128), A("PZ%d" % h, 384, 512), OP.mult)
-        dma(T.y[:, e0:e0 + 128], ys[0], [ys[1]], [], 2200)
+        tt(ys, A("xvs", e0, e0 + 128), A("PZ", 128 * h, 128 * h + 128), OP.mult)
+        dma(T.y[:, e0:e0 + 128], ys[0], [ys[1]], [])
 
     def products(v):
         for j in range(8):
@@ -436,90 +503,80 @@ def build(g, core, T, topo):
             tt(A("fw1", *c), A("w1", *c), A(P), OP.mult)
         for k in range(2):
             a, slot = 2048 * k, 2 * v + k
-            send([(-2, A("fw1", a, a + 2048), (T.fd[slot], ("fd", slot, slot + 1)))], 6000)
-            j = dma(T.fw3[0:112, a:a + 2048], T.fd[slot, 16:128, :], [("fd", slot, slot + 1)], [("fw3", a, a + 2048)], 4500)
-            dma(T.fw3[112:128, a:a + 2048], T.fd[slot, 0:16, :], [("fd", slot, slot + 1)], [("fw3", a, a + 2048)], 4500, twin=j)
+            send([(-2, A("fw1", a, a + 2048), (T.fd[slot], ("fd", slot, slot + 1)))], 8192)
+            j = dma(T.fw3[0:112, a:a + 2048], T.fd[slot, 16:128, :], [("fd", slot, slot + 1)], [("fw3", a, a + 2048)], 8192)
+            dma(T.fw3[112:128, a:a + 2048], T.fd[slot, 0:16, :], [("fd", slot, slot + 1)], [("fw3", a, a + 2048)], twin=j)
+
+    def hot(h, d, gr, u):
+        a = 128 * (48 * h + 16 * d + 2 * gr + u)
+        return (A("ohw", a, a + 128), (T["xs%d" % h][:, d, 64 * gr + 32 * u:64 * gr + 32 * u + 32], ("xs%d" % h, 8 * d + gr, 8 * d + gr + 1)))
 
     products(0)
     for t in range(EP):
         last = t == EP - 1
         for h in range(2):
-            strong(h, 0, "w3" if t else "w1", "th", "l1u", 256 * t + 128 * h)
-        if t:
-            k = None
-            for cc in range(4):
-                for j, nm in enumerate(("bh", "bl")):
-                    for row, src, rd in ((4 * j, T[nm][:, 256 * t:256 * t + 256], (nm, 256 * t, 256 * t + 256)),
-                                         (8 + 4 * j, T.bd[j, cc + 1:cc + 129, 256 * t:256 * t + 256], ("bd", 0, 4))):
-                        z = dma(T.cw[row:128:16, 4096 * cc:4096 * cc + 4096], src, [rd], [("cw", 0, 16384)], 5000, twin=k)
-                        k = z if k is None else k
-            send_w3(t, 0)
-            send_w3(t, 1)
+            strong(h, 0, "wu" if t else "w1", "th", "l1u", 256 * t + 128 * h)
         for h in range(2):
-            children(t, h, 0)
+            second(t, h)
+        if not last:
+            left = [33]
+            mm(A("PT"), [(A("nil", p1=1), A("rep", p1=1))], left=left)
         for h in range(2):
             e0 = 256 * t + 128 * h
             if not last:
-                marks(h, 0, A("bh", e0, e0 + 128), A("bl", e0, e0 + 128))
+                marks(t, h, 0, BD(t, 0, 128 * h, 128 * h + 128), BD(t, 1, 128 * h, 128 * h + 128))
             strong(h, 1, "w2%d" % (t % 2), "th2", "lu", 256 * h)
             if not last:
-                marks(h, 1, A("dh", 256 * h, 256 * h + 128), A("dl", 256 * h, 256 * h + 128))
-            children(t, h, 1)
+                marks(t, h, 1, A("dh", 256 * h, 256 * h + 128), A("dl", 256 * h, 256 * h + 128))
+            third(t, h)
             if not last:
-                marks(h, 2, A("dh", 256 * h + 128, 256 * h + 256), A("dl", 256 * h + 128, 256 * h + 256))
+                marks(t, h, 2, A("dh", 256 * h + 128, 256 * h + 256), A("dl", 256 * h + 128, 256 * h + 256))
             strong(h, 2, "w3", "th3", "lu", 256 * h + 128)
             sts = [A("st", 384 * h + 128 * d, 384 * h + 128 * d + 128) for d in range(3)]
             if not last:
-                x = A("PX%d" % h, 0, 8)
+                x = A("PX%d" % h, 128, 136)
                 mm(x, [(s, A("g8")) for s in sts] + [(A("askb", e0, e0 + 128, p1=8), A("ni8", p1=8))])
-                j = 8 * (2 * t + h)
-                f = lambda k: A("fl", 24 * h + 8 * k, 24 * h + 8 * k + 8)
-                ts(f(0), x, 0.0, None, OP.is_ge)
-                tt(f(1), f(0), A("fab", j, j + 8), OP.mult)
-                tt(f(2), f(1), A("fab", 32 + j, 40 + j), OP.add)
+                ts(A("fl", 8 * h, 8 * h + 8), x, -0.5, 64.0, OP.is_gt, OP.mult)
                 for gr in range(8):
-                    x, fg = T["xs%d" % h][:, :, 64 * gr:64 * gr + 64], A("fl", 24 * h + 16 + gr, 24 * h + 17 + gr)
+                    x = (T["xs%d" % h][:, :, 64 * gr:64 * gr + 64], None)
+                    fg, wt = A("fl", 8 * h + gr, 8 * h + gr + 1), A("fab", 16 * t + 8 * h + gr, 16 * t + 8 * h + gr + 1)
                     reg = [("xs%d" % h, 8 * d + gr, 8 * d + gr + 1) for d in range(3)]
-                    add("V", lambda q, e, x=x, fg=fg: [q.tensor_scalar(x, x, 0.0, fg[0], OP.is_equal, OP.mult)], reg + [fg[1]], reg, OV + 96 * CY)
-            y8 = A("PY%d" % h, 0, 128, p1=8)
+                    add("V", lambda q, e, x=x, fg=fg, wt=wt: [q.tensor_scalar(x[0], x[0], fg[0], wt[0], OP.is_equal, OP.mult)],
+                        reg + [fg[1], wt[1]], reg, OV + 96 * CY)
+                    for d in (1, 2):
+                        b = 256 * (d - 1) + 32 * ((gr + (d == 2)) % 8)
+                        mm(A("PT", b, b + 32), [hot(h, d, gr, u) for u in range(2)], first=False, left=left)
+            y8 = A("PX%d" % h, 256, 384, p1=8)
             mm(y8, [(A("g8"), s) for s in sts])
             ev(A("cvs", 128 * h, 128 * h + 128, p1=8), y8)
             if h == 1:
-                dma(T.cv[:, 256 * t:256 * t + 256], T.cvs[0:8, :], [("cvs", 0, 256)], [], 2200)
-            lead[0] = VAL
+                dma(T.cv[:, 256 * t:256 * t + 256], T.cvs[0:8, :], [("cvs", 0, 256)], [])
             values12(t, h)
             values3(t, h)
-        lead[0] = 0.0
         if last:
             break
-        for d in (2, 1, 0):
-            for gr in range(8):
-                b = 32 * ((gr + (d == 2)) % 8) + (256 if d == 0 else 0)
-                prs = [(A("ohw", 128 * (48 * h + 16 * d + 2 * gr + u), 128 * (48 * h + 16 * d + 2 * gr + u + 1)),
-                        (T["xs%d" % h][:, d, 64 * gr + 32 * u:64 * gr + 32 * u + 32], ("xs%d" % h, 8 * d + gr, 8 * d + gr + 1)))
-                       for h in range(2) for u in range(2)]
-                mm(A("PS0" if d == 1 else "PS1", b, b + 32), prs)
-            if d > 0:
-                o = 512 * t + 256 * (d - 1)
-                ev(A("cs", o, o + 256), A("PS0" if d == 1 else "PS1", 0, 256))
+        if t == 0:
+            window(2)
         o = 512 * t
+        ev(A("cs", o, o + 512), A("PT"))
+        for gr in range(8):
+            mm(A("PS0", 32 * gr, 32 * gr + 32), [hot(h, 0, gr, u) for h in range(2) for u in range(2)])
+        ev(A("c0"), A("PS0", 0, 256))
         send([(1, A("cs", o, o + 256), A("cin", o, o + 256)), (2, A("cs", o + 256, o + 512), A("cin", o + 256, o + 512))],
-             2500, wr=[("w2%d" % ((t + 1) % 2), 0, NW)])
-        tt(A("s1"), A("cin", o + 256, o + 512), A("PS1", 256, 512), OP.add)
-        tt(A("s2"), A("s1"), A("cin", o, o + 256), OP.add)
-        ts(A("fna"), A("s2"), 0.5, -0.5, OP.is_gt, OP.mult)
-        ts(A("fnb"), A("s2"), 2047.5, 1.5, OP.is_gt, OP.mult)
+             0, wr=[("w2%d" % ((t + 1) % 2), 0, NW)])
         for b in range(2):
-            mm(A("PX0", 128 * b, 128 * b + 128), [(A(nm, b, 256, 2), A("idn")) for nm in ("fna", "fnb")])
-        ev(A("fct"), A("PX0", 0, 256), 1.0, 1.0)
+            mm(A("PX0", 128 * b, 128 * b + 128),
+               [(A("one", p1=1), A("one", p1=1)), (A("c0", b, 256, 2), A("idn")),
+                (A("cin", o + b, o + 256, 2), A("idn")), (A("cin", o + 256 + b, o + 512, 2), A("idn"))])
+        ts(A("fct"), A("PX0", 0, 256), 0.5, 2.0, OP.max, OP.min)
         for j in range(8):
             P = ("PY0", "PS0", "PY1", "PS1")[j % 4]
             for b in range(2):
                 mm(A(P, 256 * b, 256 * b + 256), [(A("sel", 128 * (2 * j + b), 128 * (2 * j + b + 1)), A("fct"))])
-            tt(A("w3", 512 * j, 512 * j + 512), A("w1", 512 * j, 512 * j + 512), A(P), OP.mult)
+            tt(A("wu", 512 * j, 512 * j + 512), A("w1", 512 * j, 512 * j + 512), A(P), OP.mult)
             if j % 2 == 1:
                 z = (512 * j - 512, min(512 * j + 512, NW - 1))
-                ts(A("w1", *z), A("w3", *z), 0.25, 4.0, OP.max, OP.min)
+                ts(A("w1", *z), A("wu", *z), 0.25, 4.0, OP.max, OP.min)
             if j % 4 == 3:
                 send_w(t + 1, j // 4)
         products(t + 1)
@@ -531,11 +588,13 @@ def place(ops, order, before, back, lean):
     for i in order:
         o = ops[i]
         best = None
-        off = o["lat"] - o["occ"] if back else 0.0
-        t0 = max([at[j][0] + ops[j]["lat"] + HOP for j in before[i]] + [0.0]) + off
-        for e in o["eng"] or " ":
-            t = t0
-            res = [] if e == " " else [(e, o["occ"])] + [(b, o["occ"] + 60) for b in o["banks"]]
+        off = o["lag"] if back else 0.0
+        t0 = max([at[j][2] + HOP for j in before[i]] + [0.0]) + off
+        for k, e in enumerate(o["eng"] or " "):
+            t, occ = t0, o["occ"][e]
+            res = [] if e == " " else [(e, occ)] + [(b, occ + 60) for b in o["banks"]]
+            if o["big"] > 300:
+                res.append(("D", o["big"]))
             moved = True
             while moved:
                 moved = False
@@ -545,13 +604,13 @@ def place(ops, order, before, back, lean):
                             break
                         if b > t:
                             t, moved = b, True
-            if best is None or t + lean < best[0]:
-                best = (t, e, res)
-        at[i] = (best[0] - off, best[1])
+            if best is None or t + occ + lean * o["lean"] < best[0] + best[3]:
+                best = (t, e, res, occ)
+        at[i] = (best[0] - off, best[1], best[0] - off + best[3] + o["lag"])
         for r, d in best[2]:
             busy[r].append((best[0], best[0] + d))
             busy[r].sort()
-    return at, max(at[i][0] + ops[i]["lat"] for i in at)
+    return at, max(x[2] for x in at.values())
 
 
 def plan(ops):
@@ -560,21 +619,21 @@ def plan(ops):
     succ = [[] for _ in ops]
     up = [0.0] * n
     for i in range(n - 1, -1, -1):
-        up[i] += ops[i]["lat"]
+        up[i] += min(ops[i]["occ"].values()) + ops[i]["lag"]
         for j in pred[i]:
             up[j] = max(up[j], up[i] + HOP)
             succ[j].append(i)
     best = None
     for lean in LEANS:
-        at, end = place(ops, sorted(range(n), key=lambda i: (-up[i] - ops[i]["lead"], i)), pred, False, lean)
-        for k in range(PASSES):
-            bk, _ = place(ops, sorted(range(n), key=lambda i: (-at[i][0] - ops[i]["lat"], -i)), succ, True, lean)
-            at, end = place(ops, sorted(range(n), key=lambda i: (-bk[i][0] - ops[i]["lat"], i)), pred, False, lean)
+        at, end = place(ops, sorted(range(n), key=lambda i: (-up[i], i)), pred, False, lean)
+        for k in range(PASSES + 1):
             if best is None or end < best[0]:
                 best = (end, at)
+            if k < PASSES:
+                bk, _ = place(ops, sorted(range(n), key=lambda i: (-at[i][2], -i)), succ, True, lean)
+                at, end = place(ops, sorted(range(n), key=lambda i: (-bk[i][2], i)), pred, False, lean)
     for i in range(n):
-        ops[i]["t"], ops[i]["e"] = best[1][i]
-        ops[i]["end"] = ops[i]["t"] + ops[i]["lat"]
+        ops[i]["t"], ops[i]["e"], ops[i]["end"] = best[1][i]
     order = sorted(range(n), key=lambda i: (ops[i]["t"], i))
     prev = {}
     for i in order:

@@ -15,25 +15,25 @@ SCRATCH = {
     "fw1": _sb(NW, F32), "fw3": _sb(NW, F32),
     "fd": ("dram", [6, 128, NW // 2], F32), "wd": ("dram", [6, 128, NW // 2], BF), "thd": ("dram", [128, 8], F32),
     "bd": ("dram", [8, 19, 1536], BF),
-    "bni": _sb(768, I32), "bdg": _sb(1536, BF), "l1u": _sb(768, U16),
-    "bw0": _sb(17 * 256, BF), "bw1": _sb(17 * 256, BF), "dw0": _sb(17 * H, BF), "dw1": _sb(17 * H, BF),
+    "bni": _sb(256, I32), "bdg": _sb(1536, BF), "l1u": _sb(768, U16),
+    "bw0": _sb(17 * 256, BF), "dw0": _sb(17 * H, BF), "dw1": _sb(17 * H, BF),
     "ge": _sb(4096, BF), "g1o": _sb(4096, BF), "ohw": _sb(12288, BF),
     "v1p": _sb(1024, BF), "v20": _sb(2064, F32), "v21": _sb(2064, F32),
-    "t1": _sb(1024, F32), "t2": _sb(4096, F32), "t3": _sb(1024, F32), "idf": _sb(128, F32),
+    "t1": _sb(2048, F32), "t2": _sb(4096, F32), "t3": _sb(2048, F32), "idf": _sb(128, F32),
     "xs0": ("sbuf", [128, 3, 512], BF), "xs1": ("sbuf", [128, 3, 512], BF),
     "st": _sb(768, BF), "nb": _sb(256, BF), "endb": _sb(256, BF), "kb": _sb(256, BF), "eq": _sb(768, BF),
-    "o1": _sb(256, U16), "o2": _sb(256, U16), "par": _sb(512, U16), "lu": _sb(512, U16),
+    "o1": _sb(256, U16), "o2": _sb(256, U16), "par0": _sb(512, U16), "par1": _sb(512, U16), "lu0": _sb(512, U16), "lu1": _sb(512, U16),
     "ls": _sb(256, F32), "uu": _sb(256, F32), "ti": _sb(256, I32), "li": _sb(256, I32),
     "di": _sb(512, I32), "dh": _sb(512, BF), "dl": _sb(512, BF), "l2": _sb(256, BF),
     "lot": _sb(96, BF), "fl": _sb(16, BF), "fab": _sb(32, BF),
     "labx": _sb(512, BF), "askb": _sb(512, BF), "rx": _sb(512, BF),
-    "cs": _sb(1024, BF), "cin": _sb(1024, BF), "c0": _sb(256, BF), "fct": _sb(256, BF),
+    "cs": _sb(512, BF), "cin": _sb(512, BF), "c0": _sb(256, F32), "dff": _sb(128, F32), "e512": _sb(128, BF), "fct": _sb(256, BF),
     "xvs": _sb(768, BF), "ys": _sb(256, F32),
     "cvs": _sb(256, F32), "taus": _sb(4, F32), "tw": _sb(16, F32), "tb": _sb(8, BF), "th": _sb(8, F32),
     "th2": _sb(8, F32), "th3": _sb(8, F32),
-    "dif": _sb(128, F32), "q144": _sb(144, F32), "gq": _sb(128, F32), "pc": _sb(8, I32), "col": _sb(32, F32),
+    "q144": _sb(144, F32), "pc": _sb(8, I32), "col": _sb(32, F32),
     "km": _sb(16, F32), "idn": _sb(128, BF), "i256": _sb(128, BF), "blk": _sb(128, BF), "tri": _sb(256, BF),
-    "shf": _sb(384, BF), "tmpm": _sb(128, BF), "big": _sb(5 * 144, BF), "sel": _sb(2048, BF), "g8": _sb(8, BF),
+    "shf": _sb(384, BF), "big": _sb(5 * 144, BF), "sel": _sb(2048, BF), "g8": _sb(8, BF),
     "ni8": _sb(8, BF), "selu": _sb(16, BF), "rep": _sb(512, BF), "one": _sb(128, BF), "nil": _sb(128, BF),
     "eio": _sb(256, BF), "es2": _sb(128, BF), "e16": _sb(128, BF), "eo": _sb(80, BF),
     "ma": ("sbuf", [128, 4, 144], BF), "mb": ("sbuf", [128, 4, 128], BF), "mc": ("sbuf", [128, 4, 128], BF),
@@ -43,14 +43,20 @@ for _b in ("X0", "Y0", "X1", "Y1", "Z", "T", "S0", "S1"):
     SCRATCH["P" + _b] = ("psum", [128, 512], F32)
 SEMAPHORES = ["cV", "cA", "cP", "cG"] + ["s%d" % i for i in range(146)]
 
-OV, CY, PCY, GA, HOP, DM, DB = 40.0, 0.9, 0.45, 1.25, 100.0, 2000.0, 0.24
-LEANS, PASSES, NEAR, FAR = (0.5, 1.0, 2.0), 4, 300.0, 4000.0
+OV, CY, PCY, GA, HOP, DM, DB = 40.0, 0.9, 0.45, 1.4, 100.0, 2000.0, 0.24
+PASSES, SHAKE, NEAR, FAR, GN = 300, 0.4, 300.0, 4000.0, 1500.0
+POV = 20.0
+ON2 = ((0, 0), (0, 0), (1, 1))
+PACES = ((0.67, 0.92, 0.92, 1.0, 0.9), (1.0, 1.0, 1.0, 1.0, 1.05), (0.82, 1.0, 1.3, 1.0, 1.1), (1.32, 1.0, 1.0, 1.0, 1.25))
+SIDE = "AV"
+TILT = (1.0, 1.0, 1.0)
+PE1, PE3 = (0, 0, 0), (0, 0, 1)
 
 
 def build(g, core, T, topo):
     rank = T.rank_of(core)
     n = len(T.cores)
-    ops, acc, nsem = [], {}, [0]
+    ops, acc, nsem, side = [], {}, [0], [0, 0]
 
     def A(name, a=0, b=None, s=1, p0=0, p1=128, ps=1):
         if b is None:
@@ -59,7 +65,7 @@ def build(g, core, T, topo):
             name, a, b = "ohw", a + 8192, b + 8192
         return (T[name][p0:p1:ps, a:b:s], (name, a, b))
 
-    def add(eng, fn, rd, wr, occ, lag=0.0, kind="c", after=(), lean=NEAR, big=0.0):
+    def add(eng, fn, rd, wr, occ, lag=0.0, kind="c", after=(), lean=NEAR, big=0.0, ga=False):
         i = len(ops)
         deps = dict((j, True) for j in after)
         for regs, w in ((rd, False), (wr, True)):
@@ -74,7 +80,7 @@ def build(g, core, T, topo):
                 acc[nm].append((i, a, b, w))
         if not isinstance(occ, dict):
             occ = dict((e, occ) for e in eng or " ")
-        ops.append(dict(eng=eng, fn=fn, deps=deps, occ=occ, lag=lag, kind=kind, lean=lean, big=big,
+        ops.append(dict(eng=eng, fn=fn, deps=deps, occ=occ, lag=lag, kind=kind, lean=lean * TILT[side[1]], big=big, side=side[0], ga=ga,
                         banks=sorted(set(x[0] for x in list(rd) + list(wr) if x[0][0] == "P"))))
         return i
 
@@ -129,6 +135,21 @@ def build(g, core, T, topo):
             return [q.tensor_scalar(o[0], i[0], c, None, OP.is_gt if up else OP.is_lt)]
         return add(eng, fn, [i[1]], [o[1]], both(o, i), lean=50.0)
 
+    def step(o, col, eng):
+        i = A("e512")
+        def fn(q, e):
+            if e == "A":
+                return [q.activation(o[0], i[0], AF.Sigmoid, bias=col[0])]
+            return [q.tensor_scalar(o[0], i[0], col[0], 0.0, OP.add, OP.is_gt)]
+        return add(eng, fn, [i[1], col[1]], [o[1]], both(o, i))
+
+    def sc(o, i, col):
+        def fn(q, e):
+            if e == "A":
+                return [q.activation(o[0], i[0], AF.Identity, scale=col[0])]
+            return [q.tensor_scalar(o[0], i[0], col[0], None, OP.mult)]
+        return add("AV", fn, [i[1], col[1]], [o[1]], both(o, i), lean=FAR)
+
     def ms(o, v):
         return add("V", lambda q, e: [q.memset(o[0], v)], [], [o[1]], cost(o))
 
@@ -139,6 +160,9 @@ def build(g, core, T, topo):
             fn = lambda q, e: [q.iota(o[0], pat, base, cm, allow_small_or_imprecise_dtypes=True)]
         return add("G", fn, [], [o[1]], 150 + 2 * CY * wid(o))
 
+    def keep(o, i, pat, op, fill, base, cm):
+        return add("G", lambda q, e: [q.affine_select(o[0], i[0], pat, op, fill, base, cm)], [i[1]], [o[1]], 190 + 2 * CY * wid(o))
+
     def mm(o, pairs, first=True, final=True, left=None, wr=()):
         def fn(q, e):
             stop = final
@@ -147,13 +171,13 @@ def build(g, core, T, topo):
                 stop = left[0] == 0
             return [q.matmul(o[0], l[0], r[0], first and k == 0, stop and k == len(pairs) - 1) for k, (l, r) in enumerate(pairs)]
         return add("P", fn, [x[1] for pr in pairs for x in pr] + ([] if first else [o[1]]), [o[1]] + list(wr),
-                   len(pairs) * (10 + PCY * max(64, wid(o)) * (4 if pairs[0][0][1][0] == "idf" else 1)), 60)
+                   sum(POV + PCY * max(64, wid(o)) * (4 if SCRATCH[l[1][0]][2] == F32 else 1) for l, r in pairs), 60)
 
     def gat(o, win, off, lean=NEAR):
         def fn(q, e):
             src = win[0].indirect(off[0])
             return [q.activation(o[0], src, AF.Copy) if e == "A" else q.tensor_copy(o[0], src)]
-        return add("AV", fn, [win[1], off[1]], [o[1]], 60 + GA * wid(o), lean=lean)
+        return add("AV", fn, [win[1], off[1]], [o[1]], 60 + GA * wid(o), lean=lean, ga=True)
 
     def gge(o, win, off, thr, d):
         pos, neg = A(thr, d, d + 1), A(thr, 4 + d, 5 + d)
@@ -162,11 +186,11 @@ def build(g, core, T, topo):
             if e == "A":
                 return [q.activation(o[0], src, AF.Sign, bias=neg[0])]
             return [q.tensor_scalar(o[0], src, pos[0], 0.5, OP.is_ge, OP.subtract)]
-        return add("AV", fn, [win[1], off[1], (thr, 0, 8)], [o[1]], 60 + GA * wid(o))
+        return add("AV", fn, [win[1], off[1], (thr, 0, 8)], [o[1]], 60 + GA * wid(o), lean=GN, ga=True)
 
-    def gmul(o, win, off, b):
-        return add("V", lambda q, e: [q.tensor_tensor(o[0], win[0].indirect(off[0]), b[0], OP.mult)],
-                   [win[1], off[1], b[1]], [o[1]], 55 + GA * wid(o))
+    def gmul(o, win, off, b, op=OP.mult):
+        return add("V", lambda q, e: [q.tensor_tensor(o[0], win[0].indirect(off[0]), b[0], op)],
+                   [win[1], off[1], b[1]], [o[1]], 55 + GA * wid(o), ga=True)
 
     def dma(o, i, rd, wr, nb=0, eng="S", twin=None):
         fn = lambda q, e: [q.dma_start(o, i)]
@@ -203,9 +227,8 @@ def build(g, core, T, topo):
         dma(T.w1[:, k * 2048:(k + 1) * 2048], T.wt[:, k * 2048:(k + 1) * 2048], [], [("w1", k * 2048, (k + 1) * 2048)], 4096, "SA"[k])
     dma(T.bni[:, 0:256], T.bn[:, 0:256], [], [("bni", 0, 256)], 1024, "A")
     dma(T.taus[:, 0:3], T.tau[:], [], [("taus", 0, 4)])
-    dma(T.bni[:, 256:768], T.bn[:, 256:768], [], [("bni", 256, 768)], 2048)
+    dma(T.di[:], T.bn[:, 256:768], [], [("di", 0, 512)], 2048)
     dma(T.fa[:], T.ft[:], [], [("fa", 0, NW)], 8192)
-    dma(T.di[0:8, :], T.lab[:], [], [("di", 0, 512)])
     dma(T.xvs[:], T.xv[:], [], [("xvs", 0, 768)], 1536)
 
     def send_w(v, k):
@@ -235,14 +258,31 @@ def build(g, core, T, topo):
     C = lambda j: A("col", j, j + 1)
     iota(A("pc", 0, 1), [[0, 1]], 0, 1)
     iota(A("q144"), [[1, 144]], 0, 0)
-    iota(A("dif"), [[1, 128]], 0, -1)
-    iota(A("gq"), [[1, 8], [0, 16]], 0, 0)
     iota(A("eio"), [[1, 256]], 0, 0)
     iota(A("eo"), [[128, 2], [0, 5], [16, 8]], 0, 0)
-    iota(A("t1", 0, 512), [[16, 8], [1, 2], [0, 32]], 0, -1)
-    iota(A("t1", 512, 528), [[16, 8], [1, 2]], 0, -1)
-    iota(A("t3", 0, 512, p1=32), [[0, 16], [-1, 32]], 16, 0)
-    iota(A("t3", 512, 1024, p1=32), [[1, 8], [0, 64]], 0, -1)
+    iota(A("one"), [[0, 128]], 1, 0)
+    GR = [[-16, 8], [0, 16]]
+    keep(A("idn"), A("one"), [[1, 128]], OP.is_equal, 0.0, 0, -1)
+    keep(A("blk"), A("one"), GR, OP.is_ge, 0.0, 0, 1)
+    keep(A("blk"), A("blk"), [[16, 8], [0, 16]], OP.is_ge, 0.0, 15, -1)
+    keep(A("tri", 128, 256), A("blk"), [[1, 128]], OP.is_ge, 0.0, 0, -1)
+    iota(A("shf"), [[0, 384]], 1, 0)
+    keep(A("shf"), A("shf"), [[0, 3], [1, 128]], OP.is_equal, 0.0, 0, -1)
+    keep(A("shf"), A("shf"), [[-1, 3], [1, 128]], OP.not_equal, -1.0, -1, -1)
+    keep(A("shf"), A("shf"), [[0, 3]] + GR, OP.is_ge, 0.0, 0, 1)
+    iota(A("e16"), [[16, 128]], 0, 0)
+    iota(A("e512"), [[512, 128]], 0, 0)
+    iota(A("nil"), [[0, 128]], 0, 0)
+    iota(A("rep"), [[0, 512]], 1, 0)
+    keep(A("rep"), A("rep"), [[16, 8], [1, 2], [0, 32]], OP.is_equal, 0.0, 0, -1)
+    keep(A("selu"), A("one", 0, 16), [[16, 8], [1, 2]], OP.is_equal, 0.0, 0, -1)
+    keep(A("idf"), A("one"), [[1, 128]], OP.is_equal, 0.0, 0, -1)
+    keep(A("dff"), A("idf"), [[1, 128]], OP.not_equal, -1.0, -1, -1)
+    rx = A("rx", p1=32)
+    iota(rx, [[0, 16], [-1, 32]], 16, 0)
+    keep(rx, rx, [[0, 512]], OP.not_equal, -160.0, -9, 1)
+    keep(rx, rx, [[0, 512]], OP.is_ge, 0.0, -8, 1)
+    keep(rx, rx, [[1, 8], [0, 64]], OP.not_equal, 64.0, 0, -1)
     ts(A("pc", 2, 3), A("pc", 0, 1), 4, None, OP.arith_shift_right)
     ts(A("pc", 4, 5), A("pc", 0, 1), 15, None, OP.bitwise_and)
     cp(C(0), A("pc", 2, 3))
@@ -257,23 +297,14 @@ def build(g, core, T, topo):
     ts(C(6), K(15), -256.0, 256.0, OP.mult, OP.add)
     ts(A("big", 0, 144), A("q144"), C(2), None, OP.is_equal)
     for j in range(1, 5):
-        ts(A("big", 144 * j, 144 * j + 144), A("q144"), C(2), C(2 + j), OP.is_equal, OP.mult)
-    ts(A("idn"), A("dif"), 0.0, None, OP.is_equal)
-    ts(A("blk"), A("gq"), C(0), None, OP.is_equal)
-    gt(A("tmpm"), A("dif"), -0.5, eng="A")
-    tt(A("tri", 128, 256), A("tmpm"), A("blk"), OP.mult)
-    ts(C(7), C(1), 11.5, -1.0, OP.is_gt, OP.mult)
-    ts(C(8), C(7), 4.0, None, OP.add)
-    ts(A("tri", 0, 128), A("tri", 128, 256), C(8), None, OP.mult)
+        sc(A("big", 144 * j, 144 * j + 144), A("big", 0, 144), C(2 + j))
+    gt(A("tb", 4, 5), C(1), 11.5, False, "A")
+    ev(C(8), A("tb", 4, 5), 1.0, 3.0)
+    sc(A("tri", 0, 128), A("tri", 128, 256), C(8))
     ms(A("tri", 15, 128, 16), 0.0)
-    ts(A("i256"), A("idn"), 256.0, None, OP.mult)
-    for j in range(1, 4):
-        o = A("shf", 128 * j - 128, 128 * j)
-        ts(A("tmpm"), A("dif"), float(j), None, OP.is_equal)
-        tt(o, A("tmpm"), A("blk"), OP.mult)
-        tt(o, A("idn"), o, OP.subtract)
-    ev(A("es2"), A("eio", 0, 128), 1.0 / 128)
-    ev(A("e16"), A("eio", 0, 128), 16.0)
+    ev(A("i256"), A("idn"), 256.0, lean=FAR)
+    ev(A("ni8"), A("idn", 0, 8), -1.0, lean=FAR)
+    ev(A("es2"), A("eio", 0, 128), 1.0 / 128, lean=FAR)
     ts(A("eo"), A("eo"), C(1), None, OP.add)
     ts(A("g8"), A("q144", 0, 8), C(0), None, OP.is_equal)
     MW = lambda m, a, b: (T.mw[:, m, a:b], ("mw", 8 * m + a, 8 * m + b))
@@ -303,15 +334,15 @@ def build(g, core, T, topo):
         return (T.mb[:, m, :], ("mb", 0, 8)) if j == 3 else (T.mc[:, m, :], ("mc", m, m + 1))
 
     cp(A("l1u", 0, 256), A("bni", 0, 256))
-    cp(A("l1u", 256, 768), A("bni", 256, 768))
+    cp(A("l1u", 256, 768), A("di"))
     ms(A("bw0", 0, 4096), 1.0)
     BD = lambda t, d, a=0, b=256: A("bdg", 512 * t + 256 * d + a, 512 * t + 256 * d + b)
     for t in range(EP):
-        a = 256 * t
-        ts(A("ti"), A("bni", a, a + 256), 7, None, OP.arith_shift_right)
-        ts(BD(t, 0), A("ti"), -16.0, None, OP.add)
-        ts(A("li"), A("bni", a, a + 256), 127, None, OP.bitwise_and)
-        cp(BD(t, 1), A("li"))
+        x, y = (A("di", 256 * t - 256, 256 * t), A("bni")) if t else (A("bni"), A("ti"))
+        ts(y, x, 7, None, OP.arith_shift_right)
+        ts(BD(t, 0), y, -16.0, None, OP.add)
+        ts(x, x, 127, None, OP.bitwise_and)
+        cp(BD(t, 1), x)
     ts(C(10), K(0), -17.0, 1.0, OP.mult, OP.add)
     tt(C(10), C(10), K(4), OP.subtract)
     ts(A("bw0", 4096, 4352), A("eio"), 0.0, C(10), OP.mult, OP.add)
@@ -321,7 +352,7 @@ def build(g, core, T, topo):
             dma(T.bd[:, 16 + j, a:b], T.bdg[13 + j:128:16, a:b], [("bdg", a, b)], [("bd", a, b)], twin=k)
 
     def window(t):
-        w, k = "bw%d" % (t % 2), None
+        w, k = "bw0", None
         for r in range(4, -1, -1):
             for d in range(2):
                 a = 512 * t + 256 * d
@@ -334,8 +365,6 @@ def build(g, core, T, topo):
                 k = z if k is None else k
 
     window(0)
-    dma(T.bw1[:], T.bw0[:], [("bw0", 0, 4352)], [("bw1", 0, 4352)], 8704)
-    window(1)
     ts(C(11), K(0), 174.0, 1.0, OP.mult, OP.add)
     ts(C(12), K(4), 126.0, C(11), OP.mult, OP.add)
     ts(C(13), K(8), 15.0, C(12), OP.mult, OP.add)
@@ -343,19 +372,10 @@ def build(g, core, T, topo):
         dma(T["dw%d" % h][:, 0:2048], T.bw0[:, 0:2048], [("bw0", 0, 2048)], [("dw%d" % h, 0, 2048)], 4096)
         ts(A("dw%d" % h, 2048, 2176), A("eio", 0, 128), 0.0, C(13), OP.mult, OP.add)
         ms(A("v2%d" % h, 2048, 2064), 0.0)
-    ts(A("ni8"), A("dif", 0, 8), 0.0, -1.0, OP.is_equal, OP.mult)
-    ts(A("rep"), A("t1", 0, 512), 0.0, None, OP.is_equal)
-    ts(A("selu"), A("t1", 512, 528), 0.0, None, OP.is_equal)
-    ms(A("one"), 1.0)
-    ms(A("nil"), 0.0)
-    ts(A("idf"), A("dif"), 0.0, None, OP.is_equal)
     for k in range(16):
-        ts(A("sel", 128 * k, 128 * k + 128), A("blk"), K(k), None, OP.mult)
-    ts(C(14), K(9), -160.0, None, OP.mult)
-    ts(A("t3", 0, 512, p1=32), A("t3", 0, 512, p1=32), A("km", 8, 9, p1=32), A("col", 14, 15, p1=32), OP.mult, OP.add)
-    ts(A("t3", 512, 1024, p1=32), A("t3", 512, 1024, p1=32), 0.0, 64.0, OP.is_equal, OP.mult)
-    tt(A("rx", p1=32), A("t3", 0, 512, p1=32), A("t3", 512, 1024, p1=32), OP.add)
-    ms(A("labx", p1=32), 1.0)
+        keep(A("sel", 128 * k, 128 * k + 128), A("one"), GR, OP.is_equal, 0.0, -k, 1)
+    iota(A("labx", p1=32), [[0, 512]], 1, 0)
+    dma(T.di[0:8, :], T.lab[:], [], [("di", 0, 512)])
     ts(A("labx", p1=8), A("di", p1=8), -1.0, 1.0, OP.mult, OP.add)
     dma(T.di[0:8, :], T.ask[:], [], [("di", 0, 512)])
     cp(A("askb", p1=8), A("di", p1=8))
@@ -368,7 +388,7 @@ def build(g, core, T, topo):
 
     def gather(nm, h, win, lst, a):
         for s in range(0, 2048, QG):
-            gat(A(nm, 2048 * h + s, 2048 * h + s + QG), A(win), A(lst, a + s // 16, a + (s + QG) // 16))
+            gat(A(nm, 2048 * h + s, 2048 * h + s + QG), A(win), A(lst, a + s // 16, a + (s + QG) // 16), GN)
 
     def strong(h, d, win, thr, lst, a):
         for s in range(0, 2048, QG):
@@ -383,11 +403,12 @@ def build(g, core, T, topo):
         tt(A(Y, 128, 256), c("ls"), A(Y, 128, 256), OP.mult)
         tt(c("ti"), c("uu"), A(Y, 128, 256), OP.add)
         ts(c("li"), c("ti"), 5, NW - 1, OP.arith_shift_right, OP.bitwise_and)
-        cp(c("lu", d, 2), c("li"))
+        lu = c("lu%d" % (t % 2), d, 2)
+        cp(lu, c("li"))
         if d == 0 or t < EP - 1:
-            ts(c("dh", d, 2), c("lu", d, 2), 1.0 / 128, 143.50390625, OP.mult, OP.add)
-            ts(c("di", d, 2), c("ti"), 5, 127, OP.arith_shift_right, OP.bitwise_and)
-            cp(c("dl", d, 2), c("di", d, 2))
+            ts(c("dh", d, 2), lu, 1.0 / 128, 143.50390625, OP.mult, OP.add)
+            ts(c("li"), c("ti"), 5, 127, OP.arith_shift_right, OP.bitwise_and)
+            cp(c("dl", d, 2), c("li"))
 
     def second(t, h):
         X, Y = "PX%d" % h, "PY%d" % h
@@ -401,7 +422,7 @@ def build(g, core, T, topo):
            + [(A("idn"), A("eo", 40 * h, 40 * h + 40))])
         o = A("o1", 128 * h, 128 * h + 40)
         cp(o, A(X, 0, 40))
-        gat(A("g1o", 2048 * h, 2048 * h + 640), A("bw%d" % (t % 2)), o)
+        gat(A("g1o", 2048 * h, 2048 * h + 640), A("bw0"), o)
         gp = lambda j: A("g1o", 2048 * h + 128 * j, 2048 * h + 128 * j + 128)
         mm(A(Y, 256, 384), [(MAT(3, j), cm(j)) for j in range(5)])
         ev(c("l2"), A(Y, 256, 384))
@@ -410,7 +431,7 @@ def build(g, core, T, topo):
         mm(A(Y, 128, 256), [(MAT(1, j), gp(j)) for j in range(5)])
         ev(c("ls"), A(Y, 0, 128), 1.0, 3232.0, relu=True)
         ts(c("uu"), A(Y, 0, 128), -4033.0, 2080.0, OP.max, OP.mult)
-        ts(c("par", 0, 2), c("ls"), -1184.0, None, OP.add)
+        ts(c("par%d" % (t % 2), 0, 2), c("ls"), -1184.0, None, OP.add)
         names(t, h, 0)
         w, k = "dw%d" % h, None
         for j, src in ((2, c("l2")), (0, c("dh", 0, 2)), (1, c("dl", 0, 2))):
@@ -438,9 +459,9 @@ def build(g, core, T, topo):
         mm(A(X, 128, 256), [(A("i256"), c("eq", j, 3)) for j in range(3)] + [(A("idn"), c("eio"))]
            + [(BIG(3, k), wide("g1o", h, k)) for k in range(16)])
         ts(c("o2"), A(X, 128, 256), 256.0, 4351.0, OP.add, OP.min)
-        gather("ge", h, "bw%d" % (t % 2), "o2", 128 * h)
+        gather("ge", h, "bw0", "o2", 128 * h)
         mm(A(Y, 384, 512), [(A("idn"), c("kb")), (A("idn"), A("e16"))])
-        ts(c("par", 1, 2), A(Y, 384, 512), -144.0, None, OP.add)
+        ts(c("par%d" % (t % 2), 1, 2), A(Y, 384, 512), -144.0, None, OP.add)
         mm(A(Y, 0, 128), [(BIG(2, k), wide("g1o", h, k)) for k in range(16)])
         ev(c("ls"), A(Y, 0, 128), 1.0, 3232.0)
         ev(c("uu"), A(Y, 0, 128), 2080.0)
@@ -451,50 +472,75 @@ def build(g, core, T, topo):
         Y, S = "PY%d" % h, "PS%d" % h
         mm(A(Y, 384, 400), [(lo, A("selu"))])
         a = 48 * h + 16 * d
-        ev(A("lot", a, a + 16), A(Y, 384, 400))
+        ev(A("lot", a, a + 16), A(Y, 384, 400), *((1.0, 0.0) if d else (-512.0, 256.0)))
         for j in range(16):
-            ts(A("ohw", 128 * (a + j), 128 * (a + j) + 128), A("eio", 0, 128), A("lot", a + j, a + j + 1), None, OP.is_equal)
+            o, col = A("ohw", 128 * (a + j), 128 * (a + j) + 128), A("lot", a + j, a + j + 1)
+            if d:
+                ts(o, A("eio", 0, 128), col, None, OP.is_equal)
+            else:
+                step(o, col, SIDE)
         e0, k = 256 * t + 128 * h, 10 if d else 9
         mm(A(S), [(hi, A("rep")), (A("labx", e0, e0 + 128, p1=k), A("rx", p1=k))])
         ev((T["xs%d" % h][:, d, :], ("xs%d" % h, 8 * d, 8 * d + 8)), A(S), lean=FAR)
 
-    def values12(t, h):
+    def total(src, a, h, r, left, narrow=False):
+        if narrow:
+            for k in range(0, 16, 4):
+                mm(A("PZ", 128 * h + r // 16, 128 * h + 64 + r // 16), [(A("idf"), A(src, a + z, a + 1024, 16)) for z in range(k, k + 4)],
+                   first=False, left=left)
+        elif r:
+            for k in range(0, 16, 2):
+                mm(A("PZ", 128 * h, 128 * h + 128), [(A("idf"), A(src, a - 1024 + z, a + 1024, 16)) for z in range(k, k + 2)],
+                   first=False, left=left)
+
+    def values12(t, h, left):
         for s in range(0, 2048, QV):
             a, b = s // 16, (s + QV) // 16
             l1 = A("l1u", 256 * t + 128 * h + a, 256 * t + 128 * h + b)
-            l2 = A("lu", 256 * h + a, 256 * h + b)
+            l2 = A("lu%d" % (t % 2), 256 * h + a, 256 * h + b)
             vp = A("v1p", s % 1024, s % 1024 + QV)
-            gat(vp, A("fa"), A("par", 256 * h + a, 256 * h + b), FAR)
+            gat(vp, A("fa"), A("par%d" % (t % 2), 256 * h + a, 256 * h + b), FAR)
             gmul(A("v2%d" % h, s, s + QV), A("fa"), l2, vp)
             gmul(A("t2", 2048 * h + s, 2048 * h + s + QV), A("w2%d" % (t % 2)), l2, A("v2%d" % h, s, s + QV))
-            gat(A("t1", s % 1024, s % 1024 + QV), A("fw1"), l1, FAR)
+            if ON2[t][h]:
+                x = A("t2", 2048 * h + s, 2048 * h + s + QV)
+                gmul(x, A("fw1"), l1, x, OP.add)
+            else:
+                gat(A("t1", s, s + QV), A("fw1"), l1, FAR)
             if (s + QV) % 1024 == 0:
-                plus(2048 * h + s + QV - 1024, "t1")
+                r = s + QV - 1024
+                if ON2[t][h]:
+                    pass
+                elif PE1[t]:
+                    total("t1", r, h, r, left)
+                else:
+                    plus(2048 * h + r, "t1", r)
+                if PE3[t]:
+                    total("t2", 2048 * h + r, h, r, left)
 
-    def plus(r, nm):
-        o, x = A("t2", r, r + 1024), A(nm)
+    def plus(r, nm, a):
+        o, x = A("t2", r, r + 1024), A(nm, a, a + 1024)
         k = add("G", lambda q, e: [q.dma_start(o[0], x[0], accum_op=OP.add)], [x[1], o[1]], [o[1]], 1000, DM + DB * 8192, kind="d", big=DB * 8192)
         ops[k]["sem"] = [sem(), 16]
 
-    def values3(t, h):
+    def values3(t, h, left):
         for s in range(0, 2048, QV):
             a, b = s // 16, (s + QV) // 16
-            l3 = A("lu", 256 * h + 128 + a, 256 * h + 128 + b)
-            x = A("t3", s % 1024, s % 1024 + QV)
-            gat(x, A("v2%d" % h), A("par", 256 * h + 128 + a, 256 * h + 128 + b), FAR)
+            l3 = A("lu%d" % (t % 2), 256 * h + 128 + a, 256 * h + 128 + b)
+            r = s - s % 1024
+            nm = "t1" if PE3[t] and h else "t3"
+            x = A(nm, s, s + QV)
+            gat(x, A("v2%d" % h), A("par%d" % (t % 2), 256 * h + 128 + a, 256 * h + 128 + b), FAR)
             gmul(x, A("fw3"), l3, x)
             if (s + QV) % 1024 == 0:
-                r = s + QV - 1024
-                sums = [(A("idf"), A("t2", 2048 * h + r + k, 2048 * h + r + 1024, 16)) for k in range(16)]
-                if t == EP - 1 and h == 1:
-                    sums += [(A("idf"), A("t3", k, 1024, 16)) for k in range(16)]
+                if PE3[t]:
+                    total(nm, r, h, r, left, h == 1)
                 else:
-                    plus(2048 * h + r, "t3")
-                for k in range(0, len(sums), 4):
-                    mm(A("PZ", 128 * h + r // 16, 128 * h + 64 + r // 16), sums[k:k + 4], k == 0, k + 4 == len(sums), wr=[("zt", 0, 1)])
-        e0, ys = 256 * t + 128 * h, A("ys", 128 * h, 128 * h + 128)
-        tt(ys, A("xvs", e0, e0 + 128), A("PZ", 128 * h, 128 * h + 128), OP.mult)
-        dma(T.y[:, e0:e0 + 128], ys[0], [ys[1]], [])
+                    plus(2048 * h + r, "t3", r)
+                    total("t2", 2048 * h + r, h, r, left)
+        if h == 1:
+            tt(A("ys"), A("xvs", 256 * t, 256 * t + 256), A("PZ", 0, 256), OP.mult)
+            dma(T.y[:, 256 * t:256 * t + 256], T.ys[:], [("ys", 0, 256)], [])
 
     def products(v):
         for j in range(8):
@@ -514,6 +560,7 @@ def build(g, core, T, topo):
     products(0)
     for t in range(EP):
         last = t == EP - 1
+        side[1] = t
         for h in range(2):
             strong(h, 0, "wu" if t else "w1", "th", "l1u", 256 * t + 128 * h)
         for h in range(2):
@@ -525,13 +572,13 @@ def build(g, core, T, topo):
             e0 = 256 * t + 128 * h
             if not last:
                 marks(t, h, 0, BD(t, 0, 128 * h, 128 * h + 128), BD(t, 1, 128 * h, 128 * h + 128))
-            strong(h, 1, "w2%d" % (t % 2), "th2", "lu", 256 * h)
+            strong(h, 1, "w2%d" % (t % 2), "th2", "lu%d" % (t % 2), 256 * h)
             if not last:
                 marks(t, h, 1, A("dh", 256 * h, 256 * h + 128), A("dl", 256 * h, 256 * h + 128))
             third(t, h)
             if not last:
                 marks(t, h, 2, A("dh", 256 * h + 128, 256 * h + 256), A("dl", 256 * h + 128, 256 * h + 256))
-            strong(h, 2, "w3", "th3", "lu", 256 * h + 128)
+            strong(h, 2, "w3", "th3", "lu%d" % (t % 2), 256 * h + 128)
             sts = [A("st", 384 * h + 128 * d, 384 * h + 128 * d + 128) for d in range(3)]
             if not last:
                 x = A("PX%d" % h, 128, 136)
@@ -551,24 +598,28 @@ def build(g, core, T, topo):
             ev(A("cvs", 128 * h, 128 * h + 128, p1=8), y8)
             if h == 1:
                 dma(T.cv[:, 256 * t:256 * t + 256], T.cvs[0:8, :], [("cvs", 0, 256)], [])
-            values12(t, h)
-            values3(t, h)
+            side[0] = 1
+            if h == 0:
+                lz = [1 + 16 * (1 + PE1[t] + PE3[t])]
+                mm(A("PZ", 0, 256), [(A("nil", p1=1), A("rep", 0, 256, p1=1))], left=lz)
+            values12(t, h, lz)
+            values3(t, h, lz)
+            side[0] = 0
         if last:
             break
-        if t == 0:
-            window(2)
-        o = 512 * t
-        ev(A("cs", o, o + 512), A("PT"))
+        window(t + 1)
+        o = 0
+        ev(A("cs"), A("PT"))
         for gr in range(8):
             mm(A("PS0", 32 * gr, 32 * gr + 32), [hot(h, 0, gr, u) for h in range(2) for u in range(2)])
         ev(A("c0"), A("PS0", 0, 256))
         send([(1, A("cs", o, o + 256), A("cin", o, o + 256)), (2, A("cs", o + 256, o + 512), A("cin", o + 256, o + 512))],
              0, wr=[("w2%d" % ((t + 1) % 2), 0, NW)])
         for b in range(2):
-            mm(A("PX0", 128 * b, 128 * b + 128),
-               [(A("one", p1=1), A("one", p1=1)), (A("c0", b, 256, 2), A("idn")),
-                (A("cin", o + b, o + 256, 2), A("idn")), (A("cin", o + 256 + b, o + 512, 2), A("idn"))])
-        ts(A("fct"), A("PX0", 0, 256), 0.5, 2.0, OP.max, OP.min)
+            x = A("PX%d" % b, 0, 128)
+            mm(x, [(A("one", p1=1), A("one", p1=1)), (A("c0", b, 256, 2), A("dff"))], final=False, wr=[A("PX%d" % b)[1]])
+            mm(x, [(A("cin", o + b, o + 256, 2), A("idn")), (A("cin", o + 256 + b, o + 512, 2), A("idn"))], first=False)
+            ts(A("fct", 128 * b, 128 * b + 128), x, 0.5, 2.0, OP.max, OP.min)
         for j in range(8):
             P = ("PY0", "PS0", "PY1", "PS1")[j % 4]
             for b in range(2):
@@ -583,15 +634,43 @@ def build(g, core, T, topo):
     return ops
 
 
-def place(ops, order, before, back, lean):
+def after(row, t):
+    a, b = 0, len(row)
+    while a < b:
+        m = (a + b) // 2
+        if row[m][1] > t:
+            b = m
+        else:
+            a = m + 1
+    return a
+
+
+def replay(ops, at, pred, pace):
+    free, end = {}, {}
+    for i in sorted(at, key=lambda i: (at[i][0], i)):
+        o, e = ops[i], at[i][1]
+        t = max([end[j] + HOP for j in pred[i]] + [free.get(e, 0.0)] + [free.get(b, 0.0) for b in o["banks"]])
+        occ = o["occ"][e] * (pace[0] if o["ga"] else pace[2] if e == "P" else pace[1])
+        end[i] = t + occ + o["lag"] * pace[3]
+        if o["big"] > 300:
+            end[i] = max(end[i], free.get("D", 0.0) + o["big"] * pace[3])
+            free["D"] = end[i]
+        if e != " ":
+            free[e] = t + occ
+        for b in o["banks"]:
+            free[b] = t + occ + HOP
+    return max(end.values()) / pace[4]
+
+
+def place(ops, order, before, back, f):
     busy, at = {}, {}
     for i in order:
         o = ops[i]
         best = None
         off = o["lag"] if back else 0.0
         t0 = max([at[j][2] + HOP for j in before[i]] + [0.0]) + off
-        for k, e in enumerate(o["eng"] or " "):
-            t, occ = t0, o["occ"][e]
+        for e in o["eng"] or " ":
+            t, occ = t0, o["occ"][e] * f[i]
             res = [] if e == " " else [(e, occ)] + [(b, occ + 60) for b in o["banks"]]
             if o["big"] > 300:
                 res.append(("D", o["big"]))
@@ -599,18 +678,19 @@ def place(ops, order, before, back, lean):
             while moved:
                 moved = False
                 for r, d in res:
-                    for a, b in busy.setdefault(r, []):
-                        if a >= t + d:
-                            break
-                        if b > t:
-                            t, moved = b, True
-            if best is None or t + occ + lean * o["lean"] < best[0] + best[3]:
+                    row = busy.setdefault(r, [])
+                    k = after(row, t)
+                    while k < len(row) and row[k][0] < t + d:
+                        t, moved, k = row[k][1], len(res) > 1, k + 1
+            if best is None or t + occ + o["lean"] < best[0] + best[3]:
                 best = (t, e, res, occ)
         at[i] = (best[0] - off, best[1], best[0] - off + best[3] + o["lag"])
         for r, d in best[2]:
-            busy[r].append((best[0], best[0] + d))
-            busy[r].sort()
-    return at, max(x[2] for x in at.values())
+            busy[r].insert(after(busy[r], best[0]), (best[0], best[0] + d))
+    return at
+
+
+KEPT = []
 
 
 def plan(ops):
@@ -623,15 +703,23 @@ def plan(ops):
         for j in pred[i]:
             up[j] = max(up[j], up[i] + HOP)
             succ[j].append(i)
-    best = None
-    for lean in LEANS:
-        at, end = place(ops, sorted(range(n), key=lambda i: (-up[i], i)), pred, False, lean)
-        for k in range(PASSES + 1):
-            if best is None or end < best[0]:
-                best = (end, at)
-            if k < PASSES:
-                bk, _ = place(ops, sorted(range(n), key=lambda i: (-at[i][2], -i)), succ, True, lean)
-                at, end = place(ops, sorted(range(n), key=lambda i: (-bk[i][2], i)), pred, False, lean)
+    best, x, even = None, 12345, [1.0] * n
+    at = place(ops, sorted(range(n), key=lambda i: (-up[i], i)), pred, False, even)
+    if KEPT:
+        best = KEPT[0]
+    for k in range(0 if KEPT else PASSES):
+        mark = sum(replay(ops, at, pred, pace) for pace in PACES)
+        if best is None or mark < best[0]:
+            best = (mark, at)
+        if k % 3 == 2:
+            at = best[1]
+        f = []
+        for i in range(n):
+            x = (x * 1103515245 + 12345) % 2147483648
+            f.append(1 + SHAKE * (x / 1073741824.0 - 1))
+        bk = place(ops, sorted(range(n), key=lambda i: (-at[i][2], -i)), succ, True, f)
+        at = place(ops, sorted(range(n), key=lambda i: (-bk[i][2], i)), pred, False, even)
+    KEPT[:] = [best]
     for i in range(n):
         ops[i]["t"], ops[i]["e"], ops[i]["end"] = best[1][i]
     order = sorted(range(n), key=lambda i: (ops[i]["t"], i))

@@ -14,14 +14,14 @@ SCRATCH = {
     "w1": _sb(NW, BF), "w20": _sb(NW, BF), "w21": _sb(NW, BF), "w3": _sb(NW, BF), "fa": _sb(NW, BF),
     "fw1": _sb(NW, F32), "fw3": _sb(NW, F32),
     "fd": ("dram", [6, 128, NW // 2], F32), "wd": ("dram", [6, 128, NW // 2], BF), "thd": ("dram", [128, 8], F32),
-    "bd": ("dram", [8, 19, 1536], BF),
+    "bd": ("dram", [8, 20, 1536], BF),
     "bni": _sb(256, I32), "bdg": _sb(1536, BF), "l1u": _sb(768, U16),
     "bw0": _sb(17 * 256, BF), "dw0": _sb(17 * H, BF), "dw1": _sb(17 * H, BF),
     "ge": _sb(4096, BF), "g1o": _sb(4096, BF), "ohw": _sb(12288, BF),
-    "v1p": _sb(1024, BF), "v20": _sb(2064, F32), "v21": _sb(2064, F32),
+    "v1p": _sb(2048, BF), "v20": _sb(2064, F32), "v21": _sb(2064, F32),
     "t1": _sb(2048, F32), "t2": _sb(4096, F32), "t3": _sb(2048, F32), "idf": _sb(128, F32),
     "xs0": ("sbuf", [128, 3, 512], BF), "xs1": ("sbuf", [128, 3, 512], BF),
-    "st": _sb(768, BF), "nb": _sb(256, BF), "endb": _sb(256, BF), "kb": _sb(256, BF), "eq": _sb(768, BF),
+    "st": _sb(768, BF), "nb": _sb(256, BF), "endb": _sb(256, BF), "kb": _sb(256, BF),
     "o1": _sb(256, U16), "o2": _sb(256, U16), "par0": _sb(512, U16), "par1": _sb(512, U16), "lu0": _sb(512, U16), "lu1": _sb(512, U16),
     "ls": _sb(256, F32), "uu": _sb(256, F32), "ti": _sb(256, I32), "li": _sb(256, I32),
     "di": _sb(512, I32), "dh": _sb(512, BF), "dl": _sb(512, BF), "l2": _sb(256, BF),
@@ -32,22 +32,25 @@ SCRATCH = {
     "cvs": _sb(256, F32), "taus": _sb(4, F32), "tw": _sb(16, F32), "tb": _sb(8, BF), "th": _sb(8, F32),
     "th2": _sb(8, F32), "th3": _sb(8, F32),
     "q144": _sb(144, F32), "pc": _sb(8, I32), "col": _sb(32, F32),
-    "km": _sb(16, F32), "idn": _sb(128, BF), "i256": _sb(128, BF), "blk": _sb(128, BF), "tri": _sb(256, BF),
-    "shf": _sb(384, BF), "big": _sb(5 * 144, BF), "sel": _sb(2048, BF), "g8": _sb(8, BF),
-    "ni8": _sb(8, BF), "selu": _sb(16, BF), "rep": _sb(512, BF), "one": _sb(128, BF), "nil": _sb(128, BF),
+    "km": _sb(16, F32), "idn": _sb(128, BF), "blk": _sb(128, BF), "tri": _sb(384, BF),
+    "big": _sb(5 * 144, BF), "sel": _sb(2048, BF), "g8": _sb(8, BF),
+    "ni8": _sb(8, BF), "selu": _sb(16, BF), "rep": _sb(512, BF), "one": _sb(128, BF), "nil": _sb(128, BF), "run": _sb(1024, BF),
     "eio": _sb(256, BF), "es2": _sb(128, BF), "e16": _sb(128, BF), "eo": _sb(80, BF),
-    "ma": ("sbuf", [128, 4, 144], BF), "mb": ("sbuf", [128, 4, 128], BF), "mc": ("sbuf", [128, 4, 128], BF),
-    "mw": ("sbuf", [128, 4, 8], F32),
+    "ma": ("sbuf", [128, 3, 144], BF), "mb": ("sbuf", [128, 3, 128], BF), "mc": ("sbuf", [128, 3, 128], BF),
+    "mw": ("sbuf", [128, 3, 8], F32),
 }
 for _b in ("X0", "Y0", "X1", "Y1", "Z", "T", "S0", "S1"):
     SCRATCH["P" + _b] = ("psum", [128, 512], F32)
 SEMAPHORES = ["cV", "cA", "cP", "cG"] + ["s%d" % i for i in range(146)]
 
-OV, CY, PCY, GA, HOP, DM, DB = 40.0, 0.9, 0.45, 1.4, 100.0, 2000.0, 0.24
-PASSES, SHAKE, NEAR, FAR, GN = 300, 0.4, 300.0, 4000.0, 1500.0
-POV = 20.0
+OV, CY, PCY, GA, HOP, DM, DB = 40.0, 0.9, 0.45, 1.35, 200.0, 2000.0, 0.28
+PASSES, SHAKE, NEAR, FAR, GN = 400, 0.5, 900.0, 4000.0, 1000.0
+POV, SCAN, SLACK = 20.0, 2048, 2000.0
+ROOM = (((0.0, 0.0), (0.0, 0.0)), ((20000.0, 20000.0), (20000.0, 20000.0)), ((10000.0, 4000.0), (6000.0, 0.0)))
 ON2 = ((0, 0), (0, 0), (1, 1))
-PACES = ((0.67, 0.92, 0.92, 1.0, 0.9), (1.0, 1.0, 1.0, 1.0, 1.05), (0.82, 1.0, 1.3, 1.0, 1.1), (1.32, 1.0, 1.0, 1.0, 1.25))
+PACES = ((0.67, 0.92, 0.92, 1.0, 0.9, 1.0), (1.0, 1.0, 1.0, 1.0, 1.05, 0.6), (1.15, 1.15, 1.2, 1.1, 1.2, 1.0),
+         (1.32, 1.0, 1.0, 1.0, 1.25, 0.6), (1.85, 1.39, 1.3, 1.3, 1.7, 1.0))
+BANK, OWN = 150.0, ("PZ", "PT")
 SIDE = "AV"
 TILT = (1.0, 1.0, 1.0)
 PE1, PE3 = (0, 0, 0), (0, 0, 1)
@@ -56,7 +59,7 @@ PE1, PE3 = (0, 0, 0), (0, 0, 1)
 def build(g, core, T, topo):
     rank = T.rank_of(core)
     n = len(T.cores)
-    ops, acc, nsem, side = [], {}, [0], [0, 0]
+    ops, acc, nsem, side = [], {}, [0], [0, 0, 0.0]
 
     def A(name, a=0, b=None, s=1, p0=0, p1=128, ps=1):
         if b is None:
@@ -65,7 +68,7 @@ def build(g, core, T, topo):
             name, a, b = "ohw", a + 8192, b + 8192
         return (T[name][p0:p1:ps, a:b:s], (name, a, b))
 
-    def add(eng, fn, rd, wr, occ, lag=0.0, kind="c", after=(), lean=NEAR, big=0.0, ga=False):
+    def add(eng, fn, rd, wr, occ, lag=0.0, kind="c", after=(), lean=NEAR, big=0.0, ga=False, soon=0.0):
         i = len(ops)
         deps = dict((j, True) for j in after)
         for regs, w in ((rd, False), (wr, True)):
@@ -74,13 +77,14 @@ def build(g, core, T, topo):
                     if j == i:
                         continue
                     if a < d and c < b and (w or w2):
-                        deps[j] = True
+                        near = eng == ops[j]["eng"] == "P" and (c, d) == (a, b) and (nm, a, b) in rd
+                        deps[j] = deps.get(j, False) or not near
                 if w:
                     acc[nm] = [x for x in acc[nm] if not (a <= x[1] and x[2] <= b)]
                 acc[nm].append((i, a, b, w))
         if not isinstance(occ, dict):
             occ = dict((e, occ) for e in eng or " ")
-        ops.append(dict(eng=eng, fn=fn, deps=deps, occ=occ, lag=lag, kind=kind, lean=lean * TILT[side[1]], big=big, side=side[0], ga=ga,
+        ops.append(dict(eng=eng, fn=fn, deps=deps, occ=occ, lag=lag, kind=kind, lean=lean * TILT[side[1]], big=big, side=side[0], ga=ga, soon=soon, room=side[2],
                         banks=sorted(set(x[0] for x in list(rd) + list(wr) if x[0][0] == "P"))))
         return i
 
@@ -102,6 +106,11 @@ def build(g, core, T, topo):
         return {"A": OV + CY * max(64, wid(o)), "V": cost(o, i)}
 
     def ts(o, i, s1, s2, op0, op1=None):
+        if len(o[0].shape) == 2 and all(SCRATCH[x[1][0]][2] in (BF, F32) for x in (o, i)):
+            if (op0, op1) == (OP.mult, OP.add):
+                return ev(o, i, s1, s2)
+            if op1 is None and op0 in (OP.mult, OP.add):
+                return ev(o, i, s1) if op0 == OP.mult else ev(o, i, 1.0, s1)
         rd = [i[1]] + [s[1] for s in (s1, s2) if isinstance(s, tuple)]
         v1 = s1[0] if isinstance(s1, tuple) else s1
         v2 = s2[0] if isinstance(s2, tuple) else s2
@@ -119,21 +128,23 @@ def build(g, core, T, topo):
         return add("V", lambda q, e: [q.tensor_copy(o[0], i[0])], [i[1]], [o[1]], cost(o, i))
 
     def ev(o, i, scale=1.0, bias=0.0, relu=False, lean=NEAR):
+        rd = [i[1]] + [s[1] for s in (scale, bias) if isinstance(s, tuple)]
+        scale, bias = [s[0] if isinstance(s, tuple) else s for s in (scale, bias)]
         def fn(q, e):
             if e == "A":
                 return [q.activation(o[0], i[0], AF.Relu if relu else AF.Identity, bias=bias, scale=scale)]
             if relu:
                 return [q.tensor_scalar(o[0], i[0], bias, 0.0, OP.add, OP.max)]
             return [q.tensor_scalar(o[0], i[0], scale, bias, OP.mult, OP.add)]
-        return add("AV", fn, [i[1]], [o[1]], both(o, i), lean=lean)
+        return add("AV", fn, rd, [o[1]], both(o, i), lean=lean, soon=200.0)
 
-    def gt(o, i, c, up=True, eng="VA"):
+    def gt(o, i, c, up=True, eng="VA", soon=0.0):
         k = 512.0 if up else -512.0
         def fn(q, e):
             if e == "A":
                 return [q.activation(o[0], i[0], AF.Sigmoid, bias=-k * c, scale=k)]
             return [q.tensor_scalar(o[0], i[0], c, None, OP.is_gt if up else OP.is_lt)]
-        return add(eng, fn, [i[1]], [o[1]], both(o, i), lean=50.0)
+        return add(eng, fn, [i[1]], [o[1]], both(o, i), lean=50.0, soon=max(soon, 200.0))
 
     def step(o, col, eng):
         i = A("e512")
@@ -177,7 +188,8 @@ def build(g, core, T, topo):
         def fn(q, e):
             src = win[0].indirect(off[0])
             return [q.activation(o[0], src, AF.Copy) if e == "A" else q.tensor_copy(o[0], src)]
-        return add("AV", fn, [win[1], off[1]], [o[1]], 60 + GA * wid(o), lean=lean, ga=True)
+        rd = [win[1], off[1]] + [("bws", 0, 1)] * (win[1][0] == "bw0") + [("dws" + win[1][0][2:], 0, 1)] * (win[1][0][:2] == "dw")
+        return add("AV", fn, rd, [o[1]], 60 + GA * wid(o), lean=lean, ga=True)
 
     def gge(o, win, off, thr, d):
         pos, neg = A(thr, d, d + 1), A(thr, 4 + d, 5 + d)
@@ -220,21 +232,22 @@ def build(g, core, T, topo):
                 400, DM + 2 * DB * nb, kind="r", big=2 * DB * nb)
         ops[i]["tok"] = (ls, sum(cnt))
         for k, p in enumerate(parts):
-            j = add("", None, [], [p[2][1]], 0, 300, kind="a", after=[i])
+            j = add("", None, [], [p[2][1]], 0, 300 + SLACK * (p[0] == -2 and nb > 0), kind="a", after=[i])
             ops[j]["tok"] = (rs[k], cnt[k])
 
-    for k in range(2):
-        dma(T.w1[:, k * 2048:(k + 1) * 2048], T.wt[:, k * 2048:(k + 1) * 2048], [], [("w1", k * 2048, (k + 1) * 2048)], 4096, "SA"[k])
     dma(T.bni[:, 0:256], T.bn[:, 0:256], [], [("bni", 0, 256)], 1024, "A")
-    dma(T.taus[:, 0:3], T.tau[:], [], [("taus", 0, 4)])
-    dma(T.di[:], T.bn[:, 256:768], [], [("di", 0, 512)], 2048)
-    dma(T.fa[:], T.ft[:], [], [("fa", 0, NW)], 8192)
-    dma(T.xvs[:], T.xv[:], [], [("xvs", 0, 768)], 1536)
+    dma(T.taus[:, 0:3], T.tau[:], [], [("taus", 0, 4)], 0, "A")
+    for k in range(2):
+        dma(T.w1[:, k * 2048:(k + 1) * 2048], T.wt[:, k * 2048:(k + 1) * 2048], [], [("w1", k * 2048, (k + 1) * 2048)], 4096)
+    for j in (dma(T.fa[:], T.ft[:], [], [("fa", 0, NW)], 8192), dma(T.di[:], T.bn[:, 256:768], [], [("di", 0, 512)], 2048),
+              dma(T.xvs[:], T.xv[:], [], [("xvs", 0, 768)], 1536)):
+        ops[j]["soon"] = 2200.0
 
     def send_w(v, k):
         half = A("w1", k * 2048, (k + 1) * 2048)
         slot = 2 * v + k
-        send([(-1, half, A("w2%d" % (v % 2), k * 2048, (k + 1) * 2048)), (-2, half, (T.wd[slot], ("wd", slot, slot + 1)))], 8192)
+        send([(-1, half, A("w2%d" % (v % 2), k * 2048, (k + 1) * 2048))], 4096)
+        send([(-2, half, (T.wd[slot], ("wd", slot, slot + 1)))], 4096)
         c = slice(k * 2048, (k + 1) * 2048)
         j = dma(T.w3[0:112, c], T.wd[slot, 16:128, :], [("wd", slot, slot + 1)], [("w3", k * 2048, (k + 1) * 2048)], 4096)
         dma(T.w3[112:128, c], T.wd[slot, 0:16, :], [("wd", slot, slot + 1)], [("w3", k * 2048, (k + 1) * 2048)], twin=j)
@@ -266,13 +279,12 @@ def build(g, core, T, topo):
     keep(A("blk"), A("one"), GR, OP.is_ge, 0.0, 0, 1)
     keep(A("blk"), A("blk"), [[16, 8], [0, 16]], OP.is_ge, 0.0, 15, -1)
     keep(A("tri", 128, 256), A("blk"), [[1, 128]], OP.is_ge, 0.0, 0, -1)
-    iota(A("shf"), [[0, 384]], 1, 0)
-    keep(A("shf"), A("shf"), [[0, 3], [1, 128]], OP.is_equal, 0.0, 0, -1)
-    keep(A("shf"), A("shf"), [[-1, 3], [1, 128]], OP.not_equal, -1.0, -1, -1)
-    keep(A("shf"), A("shf"), [[0, 3]] + GR, OP.is_ge, 0.0, 0, 1)
+    keep(A("tri", 256, 384), A("blk"), [[1, 128]], OP.is_gt, 0.0, 0, -1)
     iota(A("e16"), [[16, 128]], 0, 0)
     iota(A("e512"), [[512, 128]], 0, 0)
     iota(A("nil"), [[0, 128]], 0, 0)
+    iota(A("run"), [[0, 1024]], 1, 0)
+    keep(A("run"), A("run"), [[0, 64], [1, 16]], OP.not_equal, 0.0, 0, 0)
     iota(A("rep"), [[0, 512]], 1, 0)
     keep(A("rep"), A("rep"), [[16, 8], [1, 2], [0, 32]], OP.is_equal, 0.0, 0, -1)
     keep(A("selu"), A("one", 0, 16), [[16, 8], [1, 2]], OP.is_equal, 0.0, 0, -1)
@@ -298,34 +310,30 @@ def build(g, core, T, topo):
     ts(A("big", 0, 144), A("q144"), C(2), None, OP.is_equal)
     for j in range(1, 5):
         sc(A("big", 144 * j, 144 * j + 144), A("big", 0, 144), C(2 + j))
-    gt(A("tb", 4, 5), C(1), 11.5, False, "A")
+    gt(A("tb", 4, 5), C(1), 11.5, False, "A", 200.0)
     ev(C(8), A("tb", 4, 5), 1.0, 3.0)
     sc(A("tri", 0, 128), A("tri", 128, 256), C(8))
-    ms(A("tri", 15, 128, 16), 0.0)
-    ev(A("i256"), A("idn"), 256.0, lean=FAR)
+    ev(C(14), C(1), 256.0)
     ev(A("ni8"), A("idn", 0, 8), -1.0, lean=FAR)
     ev(A("es2"), A("eio", 0, 128), 1.0 / 128, lean=FAR)
     ts(A("eo"), A("eo"), C(1), None, OP.add)
     ts(A("g8"), A("q144", 0, 8), C(0), None, OP.is_equal)
     MW = lambda m, a, b: (T.mw[:, m, a:b], ("mw", 8 * m + a, 8 * m + b))
-    ts(MW(0, 0, 5), A("q144", 0, 5), 0.0, C(3), OP.mult, OP.add)
+    for c, row in enumerate((11, 3, 7, 8, 11)):
+        ts(MW(0, c, c + 1), K(row), -8192.0, C(3), OP.mult, OP.add)
     ts(A("col", 24, 28), A("km", 1, 16, 4), 128.0, None, OP.mult)
     tt(MW(1, 0, 4), A("col", 24, 28), A("km", 2, 16, 4), OP.add)
-    cp(MW(1, 4, 5), MW(1, 3, 4))
-    ts(A("col", 28, 32), A("q144", 0, 4), C(1), None, OP.add)
-    ts(MW(2, 0, 4), A("col", 28, 32), 14.0, -8192.0, OP.is_equal, OP.mult)
-    ts(MW(2, 4, 5), K(14), -8192.0, None, OP.mult)
-    ts(MW(3, 0, 4), A("q144", 0, 4), K(15), 1.0, OP.mult, OP.add)
-    tt(C(9), K(15), K(11), OP.subtract)
-    ts(MW(3, 4, 5), C(9), 3.0, 1.0, OP.mult, OP.add)
-    ms((T.ma[:], ("ma", 0, 144)), 0.0)
-    ms((T.mc[:], ("mc", 0, 8)), 0.0)
+    ts(MW(1, 4, 5), MW(1, 3, 4), 1.0, None, OP.mult)
+    ts(MW(2, 0, 4), A("q144", 1, 5), K(15), K(12), OP.mult, OP.add)
+    ts(MW(2, 4, 5), K(8), -3.0, MW(2, 3, 4), OP.mult, OP.add)
+    iota((T.ma[:], ("ma", 0, 144)), [[0, 432]], 0, 0)
+    iota((T.mc[:], ("mc", 0, 8)), [[0, 384]], 0, 0)
     for gr in range(8):
         ts((T.ma[:, :, 16 * gr + 12:16 * gr + 16], ("ma", 16 * gr + 12, 16 * gr + 16)), (T.mw[:, :, 0:4], ("mw", 0, 32)),
            A("g8", gr, gr + 1), None, OP.mult)
     cp((T.mb[:], ("mb", 0, 8)), (T.ma[:, :, 0:128], ("ma", 0, 144)))
     ms((T.mb[:, :, 15:128:16], ("mb", 0, 8)), 0.0)
-    for m in range(4):
+    for m in range(3):
         ts((T.mc[:, m, 15:128:16], ("mc", m, m + 1)), A("g8"), MW(m, 4, 5), None, OP.mult)
 
     def MAT(m, j):
@@ -335,12 +343,19 @@ def build(g, core, T, topo):
 
     cp(A("l1u", 0, 256), A("bni", 0, 256))
     cp(A("l1u", 256, 768), A("di"))
-    ms(A("bw0", 0, 4096), 1.0)
+    k = None
+    for j, (row, over) in enumerate(((3, 13.5), (7, 12.5), (8, 11.5), (11, 14.5), (12, None), (15, -0.5))):
+        x = A("g1o", 2560 + 256 * j, 2816 + 256 * j)
+        if over is not None:
+            gt(C(16 + j), C(1), over)
+        ev(x, A("eio"), 0.0, C(1) if over is None else C(16 + j))
+        z = dma(T.bw0[row:128:16, 0:4096], x[0], [x[1]], [("bws", 0, 1)], 800, twin=k)
+        k = z if k is None else k
     BD = lambda t, d, a=0, b=256: A("bdg", 512 * t + 256 * d + a, 512 * t + 256 * d + b)
     for t in range(EP):
-        x, y = (A("di", 256 * t - 256, 256 * t), A("bni")) if t else (A("bni"), A("ti"))
-        ts(y, x, 7, None, OP.arith_shift_right)
-        ts(BD(t, 0), y, -16.0, None, OP.add)
+        x = A("di", 256 * t - 256, 256 * t) if t else A("bni")
+        ts(BD(t, 0), A("l1u", 256 * t, 256 * t + 256), 1.0 / 128, 143.50390625, OP.mult, OP.add)
+        ts(BD(t, 0), BD(t, 0), -160.0, None, OP.add)
         ts(x, x, 127, None, OP.bitwise_and)
         cp(BD(t, 1), x)
     ts(C(10), K(0), -17.0, 1.0, OP.mult, OP.add)
@@ -348,8 +363,8 @@ def build(g, core, T, topo):
     ts(A("bw0", 4096, 4352), A("eio"), 0.0, C(10), OP.mult, OP.add)
     for a, b in ((0, 512), (512, 1536)):
         k = dma(T.bd[:, 0:16, a:b], T.bdg[:, a:b], [("bdg", a, b)], [("bd", a, b)])
-        for j in range(3):
-            dma(T.bd[:, 16 + j, a:b], T.bdg[13 + j:128:16, a:b], [("bdg", a, b)], [("bd", a, b)], twin=k)
+        for j in range(4):
+            dma(T.bd[:, 16 + j, a:b], T.bdg[min(13 + j, 15):128:16, a:b], [("bdg", a, b)], [("bd", a, b)], twin=k)
 
     def window(t):
         w, k = "bw0", None
@@ -359,8 +374,7 @@ def build(g, core, T, topo):
                 if r == 0:
                     o, i, rd = T[w][4 * d:128:16, 0:4096], T.bdg[:, a:a + 256], ("bdg", a, a + 256)
                 else:
-                    m = 15 if r == 4 else 16
-                    o, i, rd = T[w][4 * r - 3 + d:128:16, 0:256 * m], T.bd[:, r:r + m, a:a + 256], ("bd", a, a + 256)
+                    o, i, rd = T[w][4 * r - 3 + d:128:16, 0:4096], T.bd[:, r:r + 16, a:a + 256], ("bd", a, a + 256)
                 z = dma(o, i, [rd], [(w, 0, 4096)], 800, twin=k)
                 k = z if k is None else k
 
@@ -369,7 +383,7 @@ def build(g, core, T, topo):
     ts(C(12), K(4), 126.0, C(11), OP.mult, OP.add)
     ts(C(13), K(8), 15.0, C(12), OP.mult, OP.add)
     for h in range(2):
-        dma(T["dw%d" % h][:, 0:2048], T.bw0[:, 0:2048], [("bw0", 0, 2048)], [("dw%d" % h, 0, 2048)], 4096)
+        dma(T["dw%d" % h][:, 0:2048], T.bw0[:, 0:2048], [("bw0", 0, 2048), ("bws", 0, 1)], [("dw%d" % h, 0, 2048), ("dws%d" % h, 0, 1)], 4096)
         ts(A("dw%d" % h, 2048, 2176), A("eio", 0, 128), 0.0, C(13), OP.mult, OP.add)
         ms(A("v2%d" % h, 2048, 2064), 0.0)
     for k in range(16):
@@ -398,7 +412,7 @@ def build(g, core, T, topo):
         gt(A("st", 384 * h + 128 * d, 384 * h + 128 * d + 128), x, 0.5)
 
     def names(t, h, d):
-        Y = "PY%d" % h
+        Y = ("PY%d" if d else "PX%d") % h
         c = lambda nm, j=0, w=1: A(nm, 128 * (w * h + j), 128 * (w * h + j) + 128)
         tt(A(Y, 128, 256), c("ls"), A(Y, 128, 256), OP.mult)
         tt(c("ti"), c("uu"), A(Y, 128, 256), OP.add)
@@ -424,17 +438,16 @@ def build(g, core, T, topo):
         cp(o, A(X, 0, 40))
         gat(A("g1o", 2048 * h, 2048 * h + 640), A("bw0"), o)
         gp = lambda j: A("g1o", 2048 * h + 128 * j, 2048 * h + 128 * j + 128)
-        mm(A(Y, 256, 384), [(MAT(3, j), cm(j)) for j in range(5)])
+        for m in range(3):
+            mm(A(X if m == 1 else Y, 128 * m, 128 * m + 128), [(MAT(m, j), gp(j)) for j in range(5)])
         ev(c("l2"), A(Y, 256, 384))
         ts(A(Y, 256, 384), A(Y, 256, 384), -15.0, -4.0, OP.add, OP.max)
-        mm(A(Y, 0, 128), [(MAT(2, j), cm(j)) for j in range(5)] + [(MAT(0, j), gp(j)) for j in range(5)])
-        mm(A(Y, 128, 256), [(MAT(1, j), gp(j)) for j in range(5)])
         ev(c("ls"), A(Y, 0, 128), 1.0, 3232.0, relu=True)
         ts(c("uu"), A(Y, 0, 128), -4033.0, 2080.0, OP.max, OP.mult)
         ts(c("par%d" % (t % 2), 0, 2), c("ls"), -1184.0, None, OP.add)
         names(t, h, 0)
         w, k = "dw%d" % h, None
-        for j, src in ((2, c("l2")), (0, c("dh", 0, 2)), (1, c("dl", 0, 2))):
+        for j, src in ((0, c("dh", 0, 2)), (1, c("dl", 0, 2))):
             z = dma(T[w][4 * j:128:16, 0:2048], src[0], [src[1]], [(w, 0, 2048)], 400, twin=k)
             k = z if k is None else k
 
@@ -444,6 +457,9 @@ def build(g, core, T, topo):
         tt(c("nb"), c("st", 1, 3), A(Y, 256, 384), OP.mult)
         mm(A(X, 128, 256), [(A("tri", 128, 256), c("nb"))])
         ev(c("endb"), A(X, 128, 256))
+        mm(A(Y, 256, 384), [(A("tri", 256, 384), c("nb")), (A("idn"), c("l2"))])
+        ev(c("l2"), A(Y, 256, 384), 1.0, 1.0)
+        dma(T["dw%d" % h][8:128:16, 0:2048], c("l2")[0], [c("l2")[1]], [("dws%d" % h, 0, 1)], 400)
         cm = lambda m: A("ge", 2048 * h + 128 * m, 2048 * h + 128 * m + 128)
         for m in range(16):
             gt(cm(m), c("endb"), -m - 0.5)
@@ -453,12 +469,8 @@ def build(g, core, T, topo):
         ts(c("o1"), kp, 128.0, None, OP.mult)
         ev(c("kb"), kp, 1.0, 143.50390625)
         gather("g1o", h, "dw%d" % h, "o1", 128 * h)
-        for j in range(3):
-            mm(A(X, 128 * j + 128, 128 * j + 256), [(A("shf", 128 * j, 128 * j + 128), c("kb"))])
-        gt(A("eq", 384 * h, 384 * h + 384), A(X, 128, 512), 0.5, False, "AV")
-        mm(A(X, 128, 256), [(A("i256"), c("eq", j, 3)) for j in range(3)] + [(A("idn"), c("eio"))]
-           + [(BIG(3, k), wide("g1o", h, k)) for k in range(16)])
-        ts(c("o2"), A(X, 128, 256), 256.0, 4351.0, OP.add, OP.min)
+        mm(A(X, 128, 256), [(A("idn"), c("eio"))] + [(BIG(3, k), wide("g1o", h, k)) for k in range(16)])
+        ts(c("o2"), A(X, 128, 256), C(14), 4351.0, OP.add, OP.min)
         gather("ge", h, "bw0", "o2", 128 * h)
         mm(A(Y, 384, 512), [(A("idn"), c("kb")), (A("idn"), A("e16"))])
         ts(c("par%d" % (t % 2), 1, 2), A(Y, 384, 512), -144.0, None, OP.add)
@@ -498,7 +510,7 @@ def build(g, core, T, topo):
             a, b = s // 16, (s + QV) // 16
             l1 = A("l1u", 256 * t + 128 * h + a, 256 * t + 128 * h + b)
             l2 = A("lu%d" % (t % 2), 256 * h + a, 256 * h + b)
-            vp = A("v1p", s % 1024, s % 1024 + QV)
+            vp = A("v1p", s, s + QV)
             gat(vp, A("fa"), A("par%d" % (t % 2), 256 * h + a, 256 * h + b), FAR)
             gmul(A("v2%d" % h, s, s + QV), A("fa"), l2, vp)
             gmul(A("t2", 2048 * h + s, 2048 * h + s + QV), A("w2%d" % (t % 2)), l2, A("v2%d" % h, s, s + QV))
@@ -533,12 +545,19 @@ def build(g, core, T, topo):
             gat(x, A("v2%d" % h), A("par%d" % (t % 2), 256 * h + 128 + a, 256 * h + 128 + b), FAR)
             gmul(x, A("fw3"), l3, x)
             if (s + QV) % 1024 == 0:
-                if PE3[t]:
+                if PE3[t] and h and r >= 2048 - SCAN:
+                    o, x, m = A("t2", r, r + 1024), A(nm, r, r + 1024), A("run")
+                    add("V", lambda q, e, o=o, x=x, m=m: [q.tensor_tensor_scan(o[0], m[0], x[0], 0.0, OP.mult, OP.add)],
+                        [x[1], m[1]], [o[1]], cost(o, x))
+                elif PE3[t]:
                     total(nm, r, h, r, left, h == 1)
                 else:
                     plus(2048 * h + r, "t3", r)
                     total("t2", 2048 * h + r, h, r, left)
         if h == 1:
+            if PE3[t] and SCAN:
+                z = (A("PZ", 256 - SCAN // 16, 256)[0], ("PZ", 0, 256))
+                tt(z, A("t2", 2048 - SCAN + 15, 2048, 16), z, OP.add)
             tt(A("ys"), A("xvs", 256 * t, 256 * t + 256), A("PZ", 0, 256), OP.mult)
             dma(T.y[:, 256 * t:256 * t + 256], T.ys[:], [("ys", 0, 256)], [])
 
@@ -600,11 +619,13 @@ def build(g, core, T, topo):
                 dma(T.cv[:, 256 * t:256 * t + 256], T.cvs[0:8, :], [("cvs", 0, 256)], [])
             side[0] = 1
             if h == 0:
-                lz = [1 + 16 * (1 + PE1[t] + PE3[t])]
+                lz = [1 + 16 * (1 + PE1[t] + PE3[t]) - PE3[t] * SCAN // 256]
                 mm(A("PZ", 0, 256), [(A("nil", p1=1), A("rep", 0, 256, p1=1))], left=lz)
+            side[2] = ROOM[t][h][0]
             values12(t, h, lz)
+            side[2] = ROOM[t][h][1]
             values3(t, h, lz)
-            side[0] = 0
+            side[0], side[2] = 0, 0.0
         if last:
             break
         window(t + 1)
@@ -649,7 +670,8 @@ def replay(ops, at, pred, pace):
     free, end = {}, {}
     for i in sorted(at, key=lambda i: (at[i][0], i)):
         o, e = ops[i], at[i][1]
-        t = max([end[j] + HOP for j in pred[i]] + [free.get(e, 0.0)] + [free.get(b, 0.0) for b in o["banks"]])
+        t = max([end[j] + HOP * pace[5] for j, soft in pred[i] if not soft or at[j][1] != e] + [free.get(e, 0.0)]
+                + [free[b][0] for b in o["banks"] if b in free and free[b][1] != e])
         occ = o["occ"][e] * (pace[0] if o["ga"] else pace[2] if e == "P" else pace[1])
         end[i] = t + occ + o["lag"] * pace[3]
         if o["big"] > 300:
@@ -658,7 +680,7 @@ def replay(ops, at, pred, pace):
         if e != " ":
             free[e] = t + occ
         for b in o["banks"]:
-            free[b] = t + occ + HOP
+            free[b] = (end[i] + HOP * pace[5], e)
     return max(end.values()) / pace[4]
 
 
@@ -668,10 +690,11 @@ def place(ops, order, before, back, f):
         o = ops[i]
         best = None
         off = o["lag"] if back else 0.0
-        t0 = max([at[j][2] + HOP for j in before[i]] + [0.0]) + off
         for e in o["eng"] or " ":
-            t, occ = t0, o["occ"][e] * f[i]
-            res = [] if e == " " else [(e, occ)] + [(b, occ + 60) for b in o["banks"]]
+            t = max([at[j][2] + (-o["lag"] if soft and at[j][1] == e else HOP) for j, soft in before[i]]
+                    + [o["room"] if back else o["soon"]]) + off
+            occ = o["occ"][e] * f[i]
+            res = [] if e == " " else [(e, occ)] + [(b, occ + (0 if b in OWN else BANK)) for b in o["banks"]]
             if o["big"] > 300:
                 res.append(("D", o["big"]))
             moved = True
@@ -695,14 +718,14 @@ KEPT = []
 
 def plan(ops):
     n = len(ops)
-    pred = [list(o["deps"]) for o in ops]
+    pred = [[(j, not hard) for j, hard in o["deps"].items()] for o in ops]
     succ = [[] for _ in ops]
     up = [0.0] * n
     for i in range(n - 1, -1, -1):
         up[i] += min(ops[i]["occ"].values()) + ops[i]["lag"]
-        for j in pred[i]:
+        for j, soft in pred[i]:
             up[j] = max(up[j], up[i] + HOP)
-            succ[j].append(i)
+            succ[j].append((i, soft))
     best, x, even = None, 12345, [1.0] * n
     at = place(ops, sorted(range(n), key=lambda i: (-up[i], i)), pred, False, even)
     if KEPT:
@@ -711,7 +734,7 @@ def plan(ops):
         mark = sum(replay(ops, at, pred, pace) for pace in PACES)
         if best is None or mark < best[0]:
             best = (mark, at)
-        if k % 3 == 2:
+        if k % 8 == 7:
             at = best[1]
         f = []
         for i in range(n):
@@ -756,9 +779,8 @@ def rank_program(g, core, T, topo):
                     seen[e][s] = v
             ins = o["fn"](Q[e], e)
             if o["kind"] == "c":
-                for x in ins:
-                    x.then_inc(T.sem["c" + e], 1)
-                cnt[e] += len(ins)
+                ins[-1].then_inc(T.sem["c" + e], 1)
+                cnt[e] += 1
                 o["tok"] = ("c" + e, cnt[e])
             elif o["kind"] == "d":
                 ins[0].then_inc(T.sem[o["sem"][0]], 16)

@@ -1,9 +1,10 @@
+import numpy as np
 from concourse.bass import DstId, RemoteDMATransfer
 from concourse.mybir import AluOpType as OP, ActivationFunctionType as AF
 
 NW, E, EP, H = 4096, 256, 3, 128
 BF, F32, I32, U16 = "bfloat16", "float32", "int32", "uint16"
-QG, QV = 1024, 512
+QG, QV = 1024, 1024
 
 
 def _sb(cols, d):
@@ -14,59 +15,73 @@ SCRATCH = {
     "w1": _sb(NW, BF), "w20": _sb(NW, BF), "w21": _sb(NW, BF), "w3": _sb(NW, BF), "fa": _sb(NW, BF),
     "fw1": _sb(NW, F32), "fw3": _sb(NW, F32),
     "fd": ("dram", [6, 128, NW // 2], F32), "wd": ("dram", [6, 128, NW // 2], BF), "thd": ("dram", [128, 8], F32),
-    "bd": ("dram", [8, 20, 1536], BF),
-    "bni": _sb(256, I32), "bdg": _sb(1536, BF), "l1u": _sb(768, U16),
+    "bd": ("dram", [3, 8, 2, 20, 256], BF), "ld": ("dram", [8, 32, 256], BF),
+    "bdg": _sb(1024, BF), "l1u": _sb(768, U16), "lut": _sb(4104, BF),
+    "p5": _sb(128, BF), "pl": _sb(80, U16), "i128": _sb(128, BF), "in16": _sb(128, BF),
     "bw0": _sb(17 * 256, BF), "dw0": _sb(17 * H, BF), "dw1": _sb(17 * H, BF),
     "ge": _sb(4096, BF), "g1o": _sb(4096, BF), "ohw": _sb(12288, BF),
     "v1p": _sb(2048, BF), "v20": _sb(2064, F32), "v21": _sb(2064, F32),
     "t1": _sb(2048, F32), "t2": _sb(4096, F32), "t3": _sb(2048, F32), "idf": _sb(128, F32),
     "xs0": ("sbuf", [128, 3, 512], BF), "xs1": ("sbuf", [128, 3, 512], BF),
     "st": _sb(768, BF), "nb": _sb(256, BF), "endb": _sb(256, BF), "kb": _sb(256, BF),
-    "o1": _sb(256, U16), "o2": _sb(256, U16), "par0": _sb(512, U16), "par1": _sb(512, U16), "lu0": _sb(512, U16), "lu1": _sb(512, U16),
+    "o1": _sb(256, U16), "o2": _sb(256, U16), "par0": _sb(256, U16), "par1": _sb(256, U16), "lu0": _sb(512, U16), "lu1": _sb(512, U16),
     "ls": _sb(256, F32), "uu": _sb(256, F32), "ti": _sb(256, I32), "li": _sb(256, I32),
     "di": _sb(512, I32), "dh": _sb(512, BF), "dl": _sb(512, BF), "l2": _sb(256, BF),
     "lot": _sb(96, BF), "fl": _sb(16, BF), "fab": _sb(32, BF),
-    "labx": _sb(512, BF), "askb": _sb(512, BF), "rx": _sb(512, BF),
+    "labx": _sb(512, BF), "rx": _sb(512, BF),
     "cs": _sb(512, BF), "cin": _sb(512, BF), "c0": _sb(256, F32), "dff": _sb(128, F32), "e512": _sb(128, BF), "fct": _sb(256, BF),
-    "xvs": _sb(768, BF), "ys": _sb(256, F32),
+    "xvs": _sb(256, BF), "ys": _sb(256, F32),
     "cvs": _sb(256, F32), "taus": _sb(4, F32), "tw": _sb(16, F32), "tb": _sb(8, BF), "th": _sb(8, F32),
     "th2": _sb(8, F32), "th3": _sb(8, F32),
     "q144": _sb(144, F32), "pc": _sb(8, I32), "col": _sb(32, F32),
-    "km": _sb(16, F32), "idn": _sb(128, BF), "blk": _sb(128, BF), "tri": _sb(384, BF),
-    "big": _sb(5 * 144, BF), "sel": _sb(2048, BF), "g8": _sb(8, BF),
-    "ni8": _sb(8, BF), "selu": _sb(16, BF), "rep": _sb(512, BF), "one": _sb(128, BF), "nil": _sb(128, BF), "run": _sb(1024, BF),
-    "eio": _sb(256, BF), "es2": _sb(128, BF), "e16": _sb(128, BF), "eo": _sb(80, BF),
-    "ma": ("sbuf", [128, 3, 144], BF), "mb": ("sbuf", [128, 3, 128], BF), "mc": ("sbuf", [128, 3, 128], BF),
-    "mw": ("sbuf", [128, 3, 8], F32),
+    "km": _sb(16, F32), "idn": _sb(128, BF), "blk": _sb(128, BF), "tri": _sb(256, BF),
+    "big": _sb(4 * 144, BF), "sel": _sb(2048, BF), "g8": _sb(8, BF),
+    "ni8": _sb(8, BF), "selu": _sb(16, BF), "rep": _sb(512, BF), "one": _sb(128, BF), "nil": _sb(256, BF),
+    "eio": _sb(256, BF), "es2": _sb(256, BF), "e16": _sb(128, BF), "eo": _sb(80, BF),
+    "ma": ("sbuf", [128, 6, 144], BF), "mb": ("sbuf", [128, 3, 128], BF), "mc": ("sbuf", [128, 3, 128], BF),
+    "mw": ("sbuf", [128, 6, 8], F32),
 }
+PART = {"askb": "labx", "dia": "di", "vc": "v1p"}
 for _b in ("X0", "Y0", "X1", "Y1", "Z", "T", "S0", "S1"):
     SCRATCH["P" + _b] = ("psum", [128, 512], F32)
 SEMAPHORES = ["cV", "cA", "cP", "cG"] + ["s%d" % i for i in range(146)]
 
-OV, CY, PCY, GA, HOP, DM, DB = 40.0, 0.9, 0.45, 1.35, 200.0, 2000.0, 0.28
-PASSES, SHAKE, NEAR, FAR, GN = 400, 0.5, 900.0, 4000.0, 1000.0
+OV, CY, PCY, GA, HOP, DM = 40.0, 0.9, 0.45, 1.35, 200.0, 1900.0
+ROW, BW, FARB, FIRST = 10.0, 38.0, 1.3, 3000.0
+PASSES, SHAKE, NEAR, FAR, GN = 40, 0.5, 900.0, 8000.0, 2000.0
 POV, SCAN, SLACK = 20.0, 2048, 2000.0
 ROOM = (((0.0, 0.0), (0.0, 0.0)), ((20000.0, 20000.0), (20000.0, 20000.0)), ((10000.0, 4000.0), (6000.0, 0.0)))
-ON2 = ((0, 0), (0, 0), (1, 1))
-PACES = ((0.67, 0.92, 0.92, 1.0, 0.9, 1.0), (1.0, 1.0, 1.0, 1.0, 1.05, 0.6), (1.15, 1.15, 1.2, 1.1, 1.2, 1.0),
-         (1.32, 1.0, 1.0, 1.0, 1.25, 0.6), (1.85, 1.39, 1.3, 1.3, 1.7, 1.0))
+ONE = (("first", "first"), ("dma", "dma"), ("on", "on"))
+LATE = (5500.0, 8000.0, 20000.0)
+PW = 1024
+PACES = TRIED = ((0.65, 0.9, 0.82, 0.95, 0.76, 0.6, 1.0), (1.0, 1.25, 1.25, 1.25, 1.3, 1.2, 2.0),
+                 (0.9, 0.95, 0.9, 1.0, 0.93, 0.7, 1.0), (1.6, 1.2, 1.1, 1.1, 1.4, 1.0, 1.1))
+ROUNDS, WIDE, EARLY = 450, 64, 0.1
 BANK, OWN = 150.0, ("PZ", "PT")
+PLAIN = ("AV", "AV")
+ONV = ("", "", "")
+REST = "AV"
 SIDE = "AV"
 TILT = (1.0, 1.0, 1.0)
-PE1, PE3 = (0, 0, 0), (0, 0, 1)
+PE3 = ((0, 0), (0, 0), (1, 1))
 
 
 def build(g, core, T, topo):
     rank = T.rank_of(core)
     n = len(T.cores)
-    ops, acc, nsem, side = [], {}, [0], [0, 0, 0.0]
+    ops, acc, nsem, side = [], {}, [0], [0, 0, 0.0, 0]
 
-    def A(name, a=0, b=None, s=1, p0=0, p1=128, ps=1):
+    def A(name, a=0, b=None, s=1, p0=0, p1=128, ps=1, own=None):
         if b is None:
-            b = NW if name == "wu" else SCRATCH[name][1][1]
+            b = NW if name == "wu" else SCRATCH[PART.get(name, name)][1][1]
+        if name == "ys2":
+            name = "fw1"
         if name == "wu":
             name, a, b = "ohw", a + 8192, b + 8192
-        return (T[name][p0:p1:ps, a:b:s], (name, a, b))
+        return (T[PART.get(name, name)][p0:p1:ps, a:b:s], (name,) + (own or (a, b)))
+
+    def kind(x):
+        return SCRATCH[PART.get(x[1][0], x[1][0])][2]
 
     def add(eng, fn, rd, wr, occ, lag=0.0, kind="c", after=(), lean=NEAR, big=0.0, ga=False, soon=0.0):
         i = len(ops)
@@ -99,14 +114,14 @@ def build(g, core, T, topo):
         return k
 
     def cost(*xs):
-        two = all(SCRATCH[x[1][0]][2] in (BF, U16) for x in xs)
+        two = all(kind(x) in (BF, U16) for x in xs)
         return OV + CY * max(64, wid(xs[0]) * (0.5 if two else 1))
 
     def both(o, i):
         return {"A": OV + CY * max(64, wid(o)), "V": cost(o, i)}
 
     def ts(o, i, s1, s2, op0, op1=None):
-        if len(o[0].shape) == 2 and all(SCRATCH[x[1][0]][2] in (BF, F32) for x in (o, i)):
+        if len(o[0].shape) == 2 and all(kind(x) in (BF, F32) for x in (o, i)) and s1 is not None:
             if (op0, op1) == (OP.mult, OP.add):
                 return ev(o, i, s1, s2)
             if op1 is None and op0 in (OP.mult, OP.add):
@@ -136,7 +151,7 @@ def build(g, core, T, topo):
             if relu:
                 return [q.tensor_scalar(o[0], i[0], bias, 0.0, OP.add, OP.max)]
             return [q.tensor_scalar(o[0], i[0], scale, bias, OP.mult, OP.add)]
-        return add("AV", fn, rd, [o[1]], both(o, i), lean=lean, soon=200.0)
+        return add(PLAIN[side[3]], fn, rd, [o[1]], both(o, i), lean=lean, soon=200.0)
 
     def gt(o, i, c, up=True, eng="VA", soon=0.0):
         k = 512.0 if up else -512.0
@@ -165,7 +180,7 @@ def build(g, core, T, topo):
         return add("V", lambda q, e: [q.memset(o[0], v)], [], [o[1]], cost(o))
 
     def iota(o, pat, base, cm):
-        if SCRATCH[o[1][0]][2] == I32:
+        if kind(o) == I32:
             fn = lambda q, e: [q.iota(o[0], pat, base, cm)]
         else:
             fn = lambda q, e: [q.iota(o[0], pat, base, cm, allow_small_or_imprecise_dtypes=True)]
@@ -175,6 +190,8 @@ def build(g, core, T, topo):
         return add("G", lambda q, e: [q.affine_select(o[0], i[0], pat, op, fill, base, cm)], [i[1]], [o[1]], 190 + 2 * CY * wid(o))
 
     def mm(o, pairs, first=True, final=True, left=None, wr=()):
+        if left is not None:
+            left[0] += 1
         def fn(q, e):
             stop = final
             if left is not None:
@@ -182,35 +199,42 @@ def build(g, core, T, topo):
                 stop = left[0] == 0
             return [q.matmul(o[0], l[0], r[0], first and k == 0, stop and k == len(pairs) - 1) for k, (l, r) in enumerate(pairs)]
         return add("P", fn, [x[1] for pr in pairs for x in pr] + ([] if first else [o[1]]), [o[1]] + list(wr),
-                   sum(POV + PCY * max(64, wid(o)) * (4 if SCRATCH[l[1][0]][2] == F32 else 1) for l, r in pairs), 60)
+                   sum(POV + PCY * max(64, wid(o)) * (4 if kind(l) == F32 else 1) for l, r in pairs), 60)
 
-    def gat(o, win, off, lean=NEAR):
+    def gat(o, win, off, lean=NEAR, eng=None):
         def fn(q, e):
             src = win[0].indirect(off[0])
             return [q.activation(o[0], src, AF.Copy) if e == "A" else q.tensor_copy(o[0], src)]
         rd = [win[1], off[1]] + [("bws", 0, 1)] * (win[1][0] == "bw0") + [("dws" + win[1][0][2:], 0, 1)] * (win[1][0][:2] == "dw")
-        return add("AV", fn, rd, [o[1]], 60 + GA * wid(o), lean=lean, ga=True)
+        return add(eng or REST, fn, rd, [o[1]], 60 + GA * wid(o), lean=lean, ga=True)
 
-    def gge(o, win, off, thr, d):
+    def gge(o, win, off, thr, d, eng):
         pos, neg = A(thr, d, d + 1), A(thr, 4 + d, 5 + d)
         def fn(q, e):
             src = win[0].indirect(off[0])
             if e == "A":
                 return [q.activation(o[0], src, AF.Sign, bias=neg[0])]
             return [q.tensor_scalar(o[0], src, pos[0], 0.5, OP.is_ge, OP.subtract)]
-        return add("AV", fn, [win[1], off[1], (thr, 0, 8)], [o[1]], 60 + GA * wid(o), lean=GN, ga=True)
+        return add(eng, fn, [win[1], off[1], (thr, 0, 8)], [o[1]], 60 + GA * wid(o), lean=GN, ga=True)
 
-    def gmul(o, win, off, b, op=OP.mult):
+    def gmul(o, win, off, b, op=OP.mult, more=()):
         return add("V", lambda q, e: [q.tensor_tensor(o[0], win[0].indirect(off[0]), b[0], op)],
-                   [win[1], off[1], b[1]], [o[1]], 55 + GA * wid(o), ga=True)
+                   [win[1], off[1], b[1]] + list(more), [o[1]], 55 + GA * wid(o), ga=True)
 
-    def dma(o, i, rd, wr, nb=0, eng="S", twin=None):
+    def span(o, i, size, k=16):
+        m = 1
+        for z in o.shape:
+            m *= int(z)
+        return (ROW * m / min(int(o.shape[-1]), int(i.shape[-1])) + m * size / BW) / k
+
+    def dma(o, i, rd, wr, size=2, eng="S", twin=None, few=False):
         fn = lambda q, e: [q.dma_start(o, i)]
+        d = span(o, i, size, 8 if few else 16)
         if twin is None:
-            k = add(eng, fn, rd, wr, 80, DM + DB * nb, kind="d", big=DB * nb)
+            k = add(eng, fn, rd, wr, 80, DM + d * (1.6 if few else 1), kind="d", big=d)
             ops[k]["sem"] = [sem(), 16]
         else:
-            k = add(eng, fn, rd, [], 80, DM + DB * nb, kind="d", after=list(ops[twin]["deps"]), big=DB * nb)
+            k = add(eng, fn, rd, [], 80, DM + d * (1.6 if few else 1), kind="d", after=list(ops[twin]["deps"]), big=d)
             for nm, a, b in wr:
                 acc[nm].append((k, a, b, True))
             ops[k]["sem"] = ops[twin]["sem"]
@@ -228,20 +252,25 @@ def build(g, core, T, topo):
             trs.append(RemoteDMATransfer(dst_ids=[DstId(rid=rid, pnc=pid)], dma_engine_mask=sum(1 << x for x in en[k * m:(k + 1) * m]),
                                          remote_sem=T.sem[rs[k]], src=src[0], dst=dst[0]))
             cnt.append(m)
+        d = 128 * len(parts) * (ROW + FARB * nb / BW) / 16
+        first = FIRST * (not any(o["kind"] == "r" for o in ops))
         i = add("G", lambda q, e: [q.remote_dma_fused(trs, local_sem=T.sem[ls])], [p[1][1] for p in parts], list(wr),
-                400, DM + 2 * DB * nb, kind="r", big=2 * DB * nb)
+                400 + first, DM + d, kind="r", big=d)
         ops[i]["tok"] = (ls, sum(cnt))
+        for j in [j for j in range(i) if ops[j]["kind"] == "r"][:1]:
+            ops[i]["deps"].setdefault(j, False)
         for k, p in enumerate(parts):
-            j = add("", None, [], [p[2][1]], 0, 300 + SLACK * (p[0] == -2 and nb > 0), kind="a", after=[i])
+            j = add("", None, [], [p[2][1]], 0, 300 + SLACK * (p[0] == -2 and nb > 1024), kind="a", after=[i])
             ops[j]["tok"] = (rs[k], cnt[k])
 
-    dma(T.bni[:, 0:256], T.bn[:, 0:256], [], [("bni", 0, 256)], 1024, "A")
-    dma(T.taus[:, 0:3], T.tau[:], [], [("taus", 0, 4)], 0, "A")
-    for k in range(2):
-        dma(T.w1[:, k * 2048:(k + 1) * 2048], T.wt[:, k * 2048:(k + 1) * 2048], [], [("w1", k * 2048, (k + 1) * 2048)], 4096)
-    for j in (dma(T.fa[:], T.ft[:], [], [("fa", 0, NW)], 8192), dma(T.di[:], T.bn[:, 256:768], [], [("di", 0, 512)], 2048),
-              dma(T.xvs[:], T.xv[:], [], [("xvs", 0, 768)], 1536)):
-        ops[j]["soon"] = 2200.0
+    for k, j in enumerate((
+            dma(T.ti[:], T.bn[:, 0:256], [], [("ti", 0, 256)], 4, "A"),
+            dma(T.taus[:, 0:3], T.tau[:], [], [("taus", 0, 4)], 4, "A"),
+            dma(T.w1[:, 0:2048], T.wt[:, 0:2048], [], [("w1", 0, 2048)]),
+            dma(T.w1[:, 2048:NW], T.wt[:, 2048:NW], [], [("w1", 2048, NW)]))):
+        ops[j]["fix"] = 100.0 * k
+    ops[dma(T.fa[:], T.ft[:], [], [("fa", 0, NW)])]["soon"] = LATE[0]
+    ops[dma(T.di[:], T.bn[:, 256:768], [], [("di", 0, 512), ("dia", 0, 512)], 4)]["soon"] = LATE[1]
 
     def send_w(v, k):
         half = A("w1", k * 2048, (k + 1) * 2048)
@@ -249,7 +278,7 @@ def build(g, core, T, topo):
         send([(-1, half, A("w2%d" % (v % 2), k * 2048, (k + 1) * 2048))], 4096)
         send([(-2, half, (T.wd[slot], ("wd", slot, slot + 1)))], 4096)
         c = slice(k * 2048, (k + 1) * 2048)
-        j = dma(T.w3[0:112, c], T.wd[slot, 16:128, :], [("wd", slot, slot + 1)], [("w3", k * 2048, (k + 1) * 2048)], 4096)
+        j = dma(T.w3[0:112, c], T.wd[slot, 16:128, :], [("wd", slot, slot + 1)], [("w3", k * 2048, (k + 1) * 2048)])
         dma(T.w3[112:128, c], T.wd[slot, 0:16, :], [("wd", slot, slot + 1)], [("w3", k * 2048, (k + 1) * 2048)], twin=j)
 
     ta = A("taus", 0, 3)
@@ -264,28 +293,24 @@ def build(g, core, T, topo):
     ts(A("th", 4, 7), A("tw", 0, 3), -1.0, -0.01, OP.mult, OP.min)
     send_w(0, 0)
     send_w(0, 1)
-    send([(-1, A("th"), A("th2")), (-2, A("th"), (T.thd[:], ("thd", 0, 8)))], 0)
-    j = dma(T.th3[0:112, :], T.thd[16:128, :], [("thd", 0, 8)], [("th3", 0, 8)])
-    dma(T.th3[112:128, :], T.thd[0:16, :], [("thd", 0, 8)], [("th3", 0, 8)], twin=j)
+    send([(-1, A("th"), A("th2")), (-2, A("th"), (T.thd[:], ("thd", 0, 8)))], 32)
+    j = dma(T.th3[0:112, :], T.thd[16:128, :], [("thd", 0, 8)], [("th3", 0, 8)], 4)
+    dma(T.th3[112:128, :], T.thd[0:16, :], [("thd", 0, 8)], [("th3", 0, 8)], 4, twin=j)
 
     C = lambda j: A("col", j, j + 1)
     iota(A("pc", 0, 1), [[0, 1]], 0, 1)
     iota(A("q144"), [[1, 144]], 0, 0)
     iota(A("eio"), [[1, 256]], 0, 0)
-    iota(A("eo"), [[128, 2], [0, 5], [16, 8]], 0, 0)
-    iota(A("one"), [[0, 128]], 1, 0)
+    ms(A("one"), 1.0)
     GR = [[-16, 8], [0, 16]]
     keep(A("idn"), A("one"), [[1, 128]], OP.is_equal, 0.0, 0, -1)
     keep(A("blk"), A("one"), GR, OP.is_ge, 0.0, 0, 1)
     keep(A("blk"), A("blk"), [[16, 8], [0, 16]], OP.is_ge, 0.0, 15, -1)
     keep(A("tri", 128, 256), A("blk"), [[1, 128]], OP.is_ge, 0.0, 0, -1)
-    keep(A("tri", 256, 384), A("blk"), [[1, 128]], OP.is_gt, 0.0, 0, -1)
     iota(A("e16"), [[16, 128]], 0, 0)
     iota(A("e512"), [[512, 128]], 0, 0)
-    iota(A("nil"), [[0, 128]], 0, 0)
-    iota(A("run"), [[0, 1024]], 1, 0)
-    keep(A("run"), A("run"), [[0, 64], [1, 16]], OP.not_equal, 0.0, 0, 0)
-    iota(A("rep"), [[0, 512]], 1, 0)
+    ms(A("nil"), 0.0)
+    ms(A("rep"), 1.0)
     keep(A("rep"), A("rep"), [[16, 8], [1, 2], [0, 32]], OP.is_equal, 0.0, 0, -1)
     keep(A("selu"), A("one", 0, 16), [[16, 8], [1, 2]], OP.is_equal, 0.0, 0, -1)
     keep(A("idf"), A("one"), [[1, 128]], OP.is_equal, 0.0, 0, -1)
@@ -296,42 +321,53 @@ def build(g, core, T, topo):
     keep(rx, rx, [[0, 512]], OP.is_ge, 0.0, -8, 1)
     keep(rx, rx, [[1, 8], [0, 64]], OP.not_equal, 64.0, 0, -1)
     ts(A("pc", 2, 3), A("pc", 0, 1), 4, None, OP.arith_shift_right)
-    ts(A("pc", 4, 5), A("pc", 0, 1), 15, None, OP.bitwise_and)
-    cp(C(0), A("pc", 2, 3))
-    cp(C(1), A("pc", 4, 5))
+    ts(A("pc", 3, 4), A("pc", 0, 1), 15, None, OP.bitwise_and)
+    ts(A("pc", 4, 5), A("pc", 0, 1), 2, 3, OP.arith_shift_right, OP.bitwise_and)
+    ts(A("pc", 5, 6), A("pc", 0, 1), 3, None, OP.bitwise_and)
+    cp(A("col", 0, 2), A("pc", 2, 4))
+    ts(A("pc", 6, 7), A("pc", 0, 1), 7, None, OP.bitwise_and)
+    ts(A("pc", 7, 8), A("pc", 0, 1), 3, 1, OP.arith_shift_right, OP.bitwise_and)
+    cp(A("col", 28, 32), A("pc", 4, 8))
     ts(C(2), C(0), 16.0, 15.0, OP.mult, OP.add)
     ts(A("km"), A("q144", 0, 16), C(1), None, OP.is_equal)
     K = lambda j: A("km", j, j + 1)
     BIG = lambda j, m: A("big", 144 * j + 15 - m, 144 * j + 143 - m)
-    ts(C(3), K(0), 128.0, K(4), OP.mult, OP.add)
+    ts(C(3), K(0), 128.0, K(8), OP.mult, OP.add)
     ts(C(4), K(15), -20480.0, C(3), OP.mult, OP.add)
-    ts(C(5), K(8), 256.0, None, OP.mult)
-    ts(C(6), K(15), -256.0, 256.0, OP.mult, OP.add)
+    ts(C(5), K(15), -256.0, 256.0, OP.mult, OP.add)
     ts(A("big", 0, 144), A("q144"), C(2), None, OP.is_equal)
-    for j in range(1, 5):
+    for j in range(1, 4):
         sc(A("big", 144 * j, 144 * j + 144), A("big", 0, 144), C(2 + j))
     gt(A("tb", 4, 5), C(1), 11.5, False, "A", 200.0)
     ev(C(8), A("tb", 4, 5), 1.0, 3.0)
     sc(A("tri", 0, 128), A("tri", 128, 256), C(8))
-    ev(C(14), C(1), 256.0)
-    ev(A("ni8"), A("idn", 0, 8), -1.0, lean=FAR)
-    ev(A("es2"), A("eio", 0, 128), 1.0 / 128, lean=FAR)
-    ts(A("eo"), A("eo"), C(1), None, OP.add)
+    ev(A("ni8"), A("idn", 32, 40), -1.0, lean=FAR)
+    ev(A("es2"), A("eio"), 1.0 / 256, lean=FAR)
+    keep(A("i128"), A("nil", 0, 128), [[1, 128]], OP.not_equal, 128.0, 0, -1)
+    keep(A("in16"), A("nil", 0, 128), [[1, 128]], OP.not_equal, -16.0, 0, -1)
+    ts(A("eo", 0, 32), A("q144", 0, 128, 4), C(28), None, OP.add)
+    ts(A("eo", 32, 40), A("q144", 0, 128, 16), C(1), None, OP.add)
+    ts(A("eo", 40, 80), A("eo", 0, 40), 128.0, None, OP.add)
     ts(A("g8"), A("q144", 0, 8), C(0), None, OP.is_equal)
     MW = lambda m, a, b: (T.mw[:, m, a:b], ("mw", 8 * m + a, 8 * m + b))
-    for c, row in enumerate((11, 3, 7, 8, 11)):
+    for c, row in enumerate((14, 13, 5, 6, 14)):
         ts(MW(0, c, c + 1), K(row), -8192.0, C(3), OP.mult, OP.add)
-    ts(A("col", 24, 28), A("km", 1, 16, 4), 128.0, None, OP.mult)
-    tt(MW(1, 0, 4), A("col", 24, 28), A("km", 2, 16, 4), OP.add)
+    ts(A("col", 24, 28), A("km", 1, 5), 128.0, None, OP.mult)
+    tt(MW(1, 0, 4), A("col", 24, 28), A("km", 9, 13), OP.add)
     ts(MW(1, 4, 5), MW(1, 3, 4), 1.0, None, OP.mult)
-    ts(MW(2, 0, 4), A("q144", 1, 5), K(15), K(12), OP.mult, OP.add)
-    ts(MW(2, 4, 5), K(8), -3.0, MW(2, 3, 4), OP.mult, OP.add)
-    iota((T.ma[:], ("ma", 0, 144)), [[0, 432]], 0, 0)
-    iota((T.mc[:], ("mc", 0, 8)), [[0, 384]], 0, 0)
+    ts(MW(2, 0, 4), A("q144", 1, 5), K(15), K(7), OP.mult, OP.add)
+    ts(MW(2, 4, 5), K(6), -3.0, MW(2, 3, 4), OP.mult, OP.add)
+    ts(MW(3, 0, 4), A("q144", 0, 16, 4), C(1), -256.0, OP.is_gt, OP.mult)
+    ts(MW(4, 0, 4), A("km", 0, 16, 4), 16.0, None, OP.mult)
+    ts(C(6), C(29), 4.0, -4.0, OP.mult, OP.add)
+    ts(C(7), C(29), 1.0, C(6), OP.add, OP.max)
+    ts(MW(5, 0, 4), A("q144", 0, 4), C(28), C(7), OP.is_equal, OP.mult)
+    ms((T.ma[:], ("ma", 0, 144)), 0.0)
+    ms((T.mc[:], ("mc", 0, 8)), 0.0)
     for gr in range(8):
-        ts((T.ma[:, :, 16 * gr + 12:16 * gr + 16], ("ma", 16 * gr + 12, 16 * gr + 16)), (T.mw[:, :, 0:4], ("mw", 0, 32)),
+        ts((T.ma[:, :, 16 * gr + 12:16 * gr + 16], ("ma", 16 * gr + 12, 16 * gr + 16)), (T.mw[:, :, 0:4], ("mw", 0, 48)),
            A("g8", gr, gr + 1), None, OP.mult)
-    cp((T.mb[:], ("mb", 0, 8)), (T.ma[:, :, 0:128], ("ma", 0, 144)))
+    cp((T.mb[:], ("mb", 0, 8)), (T.ma[:, 0:3, 0:128], ("ma", 0, 144)))
     ms((T.mb[:, :, 15:128:16], ("mb", 0, 8)), 0.0)
     for m in range(3):
         ts((T.mc[:, m, 15:128:16], ("mc", m, m + 1)), A("g8"), MW(m, 4, 5), None, OP.mult)
@@ -341,58 +377,90 @@ def build(g, core, T, topo):
             return (T.ma[:, m, 12 - 4 * j:140 - 4 * j], ("ma", 0, 144))
         return (T.mb[:, m, :], ("mb", 0, 8)) if j == 3 else (T.mc[:, m, :], ("mc", m, m + 1))
 
-    cp(A("l1u", 0, 256), A("bni", 0, 256))
+    cp(A("l1u", 0, 256), A("ti"))
     cp(A("l1u", 256, 768), A("di"))
+    ts(C(14), C(30), 2.0, -12.5, OP.mult, OP.add)
+    ts(C(12), C(31), -1.0, C(14), OP.mult, OP.add)
+    ts(C(15), C(31), -3.0, C(14), OP.mult, OP.add)
+    ts(C(9), C(31), -1.0, 1.0, OP.mult, OP.add)
+    ts(A("col", 16, 18), A("q144", 0, 2), C(12), 0.0, OP.add, OP.is_gt)
+    ts(A("col", 18, 20), A("q144", 0, 2), C(15), -1.0, OP.add, OP.is_gt)
+    ts(A("col", 22, 24), A("q144", 0, 2), C(14), 12.5, OP.add, OP.add)
+    ts(A("col", 20, 22), A("col", 22, 24), C(9), C(31), OP.mult, OP.add)
+    for j in range(6):
+        ev(A("g1o", 2560 + 256 * j, 2816 + 256 * j), A("eio"), 0.0, C(16 + j))
     k = None
-    for j, (row, over) in enumerate(((3, 13.5), (7, 12.5), (8, 11.5), (11, 14.5), (12, None), (15, -0.5))):
-        x = A("g1o", 2560 + 256 * j, 2816 + 256 * j)
-        if over is not None:
-            gt(C(16 + j), C(1), over)
-        ev(x, A("eio"), 0.0, C(1) if over is None else C(16 + j))
-        z = dma(T.bw0[row:128:16, 0:4096], x[0], [x[1]], [("bws", 0, 1)], 800, twin=k)
+    for j in range(3):
+        x = A("g1o", 2560 + 512 * j, 3072 + 512 * j)
+        z = dma(T.bw0[5 + j:128:8, 0:4096], x[0], [x[1]], [("bws", 0, 1)], twin=k)
         k = z if k is None else k
-    BD = lambda t, d, a=0, b=256: A("bdg", 512 * t + 256 * d + a, 512 * t + 256 * d + b)
+    BD = lambda t, d, a=0, b=256: A("bdg", 512 * t + 256 * d + a, 512 * t + 256 * d + b) if t < 2 else A("v1p", 256 * d + a, 256 * d + b)
     for t in range(EP):
-        x = A("di", 256 * t - 256, 256 * t) if t else A("bni")
+        x = A("di", 256 * t - 256, 256 * t) if t else A("ti")
         ts(BD(t, 0), A("l1u", 256 * t, 256 * t + 256), 1.0 / 128, 143.50390625, OP.mult, OP.add)
         ts(BD(t, 0), BD(t, 0), -160.0, None, OP.add)
         ts(x, x, 127, None, OP.bitwise_and)
         cp(BD(t, 1), x)
     ts(C(10), K(0), -17.0, 1.0, OP.mult, OP.add)
-    tt(C(10), C(10), K(4), OP.subtract)
+    tt(C(10), C(10), K(8), OP.subtract)
     ts(A("bw0", 4096, 4352), A("eio"), 0.0, C(10), OP.mult, OP.add)
-    for a, b in ((0, 512), (512, 1536)):
-        k = dma(T.bd[:, 0:16, a:b], T.bdg[:, a:b], [("bdg", a, b)], [("bd", a, b)])
+    for t in range(EP):
+        nm, a, b = BD(t, 0, 0, 512)[1]
+        k = dma(T.bd[t, :, 0, 0:16, :], T[nm][:, a:a + 256], [(nm, a, b)], [("bd", t, t + 1)])
+        dma(T.bd[t, :, 1, 0:16, :], T[nm][:, a + 256:b], [(nm, a, b)], [("bd", t, t + 1)], twin=k)
         for j in range(4):
-            dma(T.bd[:, 16 + j, a:b], T.bdg[min(13 + j, 15):128:16, a:b], [("bdg", a, b)], [("bd", a, b)], twin=k)
+            dma(T.bd[t, :, :, 16 + j, :], T[nm][min(13 + j, 15):128:16, a:b], [(nm, a, b)], [("bd", t, t + 1)], twin=k, few=True)
 
     def window(t):
-        w, k = "bw0", None
-        for r in range(4, -1, -1):
-            for d in range(2):
-                a = 512 * t + 256 * d
-                if r == 0:
-                    o, i, rd = T[w][4 * d:128:16, 0:4096], T.bdg[:, a:a + 256], ("bdg", a, a + 256)
-                else:
-                    o, i, rd = T[w][4 * r - 3 + d:128:16, 0:4096], T.bd[:, r:r + 16, a:a + 256], ("bd", a, a + 256)
-                z = dma(o, i, [rd], [(w, 0, 4096)], 800, twin=k)
-                k = z if k is None else k
+        k = None
+        for r in range(5):
+            z = dma(T.bw0[r:128:8, 0:4096], T.bd[t, :, :, r:r + 16, :], [("bd", t, t + 1)], [("bw0", 0, 4096)], twin=k)
+            ops[z]["big"] = 300.0
+            k = z if k is None else k
 
     window(0)
-    ts(C(11), K(0), 174.0, 1.0, OP.mult, OP.add)
-    ts(C(12), K(4), 126.0, C(11), OP.mult, OP.add)
-    ts(C(13), K(8), 15.0, C(12), OP.mult, OP.add)
+    ts(C(11), K(0), 127.0, 1.0, OP.mult, OP.add)
+    ts(C(13), K(8), 62.0, C(11), OP.mult, OP.add)
     for h in range(2):
-        dma(T["dw%d" % h][:, 0:2048], T.bw0[:, 0:2048], [("bw0", 0, 2048), ("bws", 0, 1)], [("dw%d" % h, 0, 2048), ("dws%d" % h, 0, 1)], 4096)
+        dma(T["dw%d" % h][:, 0:2048], T.bw0[:, 0:2048], [("bw0", 0, 2048), ("bws", 0, 1)], [("dw%d" % h, 0, 2048)])
         ts(A("dw%d" % h, 2048, 2176), A("eio", 0, 128), 0.0, C(13), OP.mult, OP.add)
         ms(A("v2%d" % h, 2048, 2064), 0.0)
+
+    U = lambda j, w=1: A("ohw", 8192 + 256 * j, 8192 + 256 * (j + w))
+    iota(U(11), [[1, 16], [0, 16]], 2, 0)
+    for c in range(4):
+        ts(U(c), U(11), c + 1.0, 13.0, OP.add, OP.max)
+    ts(U(0, 4), U(0, 4), 17.0, None, OP.min)
+    ms(A("ohw", 8192 + 960, 8192 + 976), 16.0)
+    for c in range(4):
+        keep(U(c), U(c), [[0, 128 >> c], [1, 2], [0, 1 << c]], OP.is_gt, 17.0, 0, 0)
+    for c in range(4):
+        x = A(("PZ", "PT")[c // 2], 256 * (c % 2), 256 * (c % 2) + 256)
+        mm(x, [(A("idn"), U(z)) for z in range(c + 1)])
+        ts(U(4 + c), x, C(1), 17.0 * (c + 1), OP.add, OP.is_ge)
+    x = A("ohw", 8192 + 704, 8192 + 720)
+    ts(x, x, -2.0, None, OP.add)
+    mm(A("PZ"), [(A("idn"), U(0, 2))])
+    mm(A("PT", 0, 256), [(A("idn"), U(2))])
+    tt(U(8, 2), U(4, 2), A("PZ"), OP.mult)
+    tt(U(10), U(6), A("PT", 0, 256), OP.mult)
+    mm(A("PT", 256, 512), [(A("idn"), U(z)) for z in range(8, 12)] + [(A("i128"), U(7))])
+    ts(U(0), A("PT", 256, 512), C(1), 64.0, OP.add, OP.min)
+    ops[dma(T.ld[:, 0:16, :], T.nil[:], [("nil", 0, 256)], [("ld", 0, 1)])]["soon"] = LATE[1]
+    dma(T.ld[:, 16:32, :], U(0)[0], [U(0)[1]], [("ld", 1, 2)])
+    k = None
+    for s in range(16):
+        z = dma(T.lut[:, 256 * s:256 * s + 256], T.ld[:, 16 - s:32 - s, :], [("ld", 0, 2)], [("lut", 0, 4096)], twin=k)
+        k = z if k is None else k
+    ms(A("lut", 4096, 4104), 0.0)
+
     for k in range(16):
         keep(A("sel", 128 * k, 128 * k + 128), A("one"), GR, OP.is_equal, 0.0, -k, 1)
-    iota(A("labx", p1=32), [[0, 512]], 1, 0)
-    dma(T.di[0:8, :], T.lab[:], [], [("di", 0, 512)])
+    ms(A("labx", p1=32), 1.0)
+    k = dma(T.di[0:8, :], T.lab[:], [], [("di", 0, 512)], 4, few=True)
+    dma(T.di[32:40, :], T.ask[:], [], [("dia", 0, 512)], 4, twin=k, few=True)
     ts(A("labx", p1=8), A("di", p1=8), -1.0, 1.0, OP.mult, OP.add)
-    dma(T.di[0:8, :], T.ask[:], [], [("di", 0, 512)])
-    cp(A("askb", p1=8), A("di", p1=8))
+    cp(A("askb", p0=32, p1=40), A("dia", p0=32, p1=40))
     for j in range(4):
         mm(A("PS0", 8 * j, 8 * j + 8), [(A("labx", 128 * j, 128 * j + 128, p1=8), A("idn", 0, 8, p1=8))])
     ev(A("fab"), A("PS0", 0, 32), -2049.0, 2048.0)
@@ -400,16 +468,20 @@ def build(g, core, T, topo):
     def wide(nm, h, k):
         return A(nm, 2048 * h + k, 2048 * h + 2048, 16)
 
+    def who(nm, h, s):
+        return "V" if "%s%d%d" % (nm, h, s // QG) in ONV[side[1]].split() else REST
+
     def gather(nm, h, win, lst, a):
         for s in range(0, 2048, QG):
-            gat(A(nm, 2048 * h + s, 2048 * h + s + QG), A(win), A(lst, a + s // 16, a + (s + QG) // 16), GN)
+            gat(A(nm, 2048 * h + s, 2048 * h + s + QG), A(win), A(lst, a + s // 16, a + (s + QG) // 16), GN, who(nm, h, s))
 
     def strong(h, d, win, thr, lst, a):
         for s in range(0, 2048, QG):
-            gge(A("ge", 2048 * h + s, 2048 * h + s + QG), A(win), A(lst, a + s // 16, a + (s + QG) // 16), thr, d)
+            gge(A("ge", 2048 * h + s, 2048 * h + s + QG), A(win), A(lst, a + s // 16, a + (s + QG) // 16), thr, d,
+                who("s%d" % d, h, s))
         x = A("PX%d" % h, 0, 128)
         mm(x, [(BIG(0, k), wide("ge", h, k)) for k in range(16)])
-        gt(A("st", 384 * h + 128 * d, 384 * h + 128 * d + 128), x, 0.5)
+        gt(A("st", 384 * h + 128 * d, 384 * h + 128 * d + 128), x, 0.5, eng=PLAIN[1])
 
     def names(t, h, d):
         Y = ("PY%d" if d else "PX%d") % h
@@ -429,53 +501,55 @@ def build(g, core, T, topo):
         c = lambda nm, j=0, w=1: A(nm, 128 * (w * h + j), 128 * (w * h + j) + 128)
         mm(A(X, 128, 256), [(A("tri", 0, 128), c("st", 0, 3))])
         ev(c("endb"), A(X, 128, 256))
-        cm = lambda j: A("ge", 2048 * h + 128 * j, 2048 * h + 128 * j + 128)
-        for j, th in enumerate((0.5, 4.5, 8.5, 12.5, 15.5)):
-            gt(cm(j), c("endb"), th, False)
-        mm(A(X, 0, 40), [(BIG(4, b), A("ge", 2048 * h + b, 2048 * h + 640, 16)) for b in range(16)]
+        a = 2048 * h
+        for j, th in enumerate((0.5, 4.5, 8.5, 12.5)):
+            gt(A("ge", a + j, a + 512, 4, own=(a + 128 * j, a + 128 * j + 128)), c("endb"), th, False)
+        gt(A("ge", a + 512, a + 640), c("endb"), 15.5, False)
+        mm(A(X, 0, 40), [(BIG(3, b), A("ge", a + b, a + 640, 16, own=(a, a + 640))) for b in range(16)]
            + [(A("idn"), A("eo", 40 * h, 40 * h + 40))])
         o = A("o1", 128 * h, 128 * h + 40)
         cp(o, A(X, 0, 40))
-        gat(A("g1o", 2048 * h, 2048 * h + 640), A("bw0"), o)
-        gp = lambda j: A("g1o", 2048 * h + 128 * j, 2048 * h + 128 * j + 128)
+        gat(A("g1o", a, a + 640), A("bw0"), o)
+        gp = lambda j: A("g1o", a + j, a + 512, 4) if j < 4 else A("g1o", a + 512, a + 640)
         for m in range(3):
             mm(A(X if m == 1 else Y, 128 * m, 128 * m + 128), [(MAT(m, j), gp(j)) for j in range(5)])
         ev(c("l2"), A(Y, 256, 384))
         ts(A(Y, 256, 384), A(Y, 256, 384), -15.0, -4.0, OP.add, OP.max)
         ev(c("ls"), A(Y, 0, 128), 1.0, 3232.0, relu=True)
         ts(c("uu"), A(Y, 0, 128), -4033.0, 2080.0, OP.max, OP.mult)
-        ts(c("par%d" % (t % 2), 0, 2), c("ls"), -1184.0, None, OP.add)
         names(t, h, 0)
         w, k = "dw%d" % h, None
         for j, src in ((0, c("dh", 0, 2)), (1, c("dl", 0, 2))):
-            z = dma(T[w][4 * j:128:16, 0:2048], src[0], [src[1]], [(w, 0, 2048)], 400, twin=k)
+            z = dma(T[w][8 * j:128:16, 0:2048], src[0], [src[1]], [(w, 0, 2048)], twin=k, few=True)
             k = z if k is None else k
+        x = A("PS%d" % h, 0, 40)
+        mm(x, [(BIG(1, b), A("g1o", a + b, a + 640, 16)) for b in range(16)])
+        ts(A("pl", 40 * h, 40 * h + 40), x, 2048.0, None, OP.add)
 
     def third(t, h):
         X, Y = "PX%d" % h, "PY%d" % h
         c = lambda nm, j=0, w=1: A(nm, 128 * (w * h + j), 128 * (w * h + j) + 128)
         tt(c("nb"), c("st", 1, 3), A(Y, 256, 384), OP.mult)
-        mm(A(X, 128, 256), [(A("tri", 128, 256), c("nb"))])
-        ev(c("endb"), A(X, 128, 256))
-        mm(A(Y, 256, 384), [(A("tri", 256, 384), c("nb")), (A("idn"), c("l2"))])
-        ev(c("l2"), A(Y, 256, 384), 1.0, 1.0)
-        dma(T["dw%d" % h][8:128:16, 0:2048], c("l2")[0], [c("l2")[1]], [("dws%d" % h, 0, 1)], 400)
-        cm = lambda m: A("ge", 2048 * h + 128 * m, 2048 * h + 128 * m + 128)
-        for m in range(16):
-            gt(cm(m), c("endb"), -m - 0.5)
-        kp = A(X, 0, 128)
-        mm(kp, [(A("idn"), A("es2"))] + [(BIG(0, m), cm(m)) for m in range(8)], final=False)
-        mm(kp, [(BIG(0, m), cm(m)) for m in range(8, 16)], first=False)
-        ts(c("o1"), kp, 128.0, None, OP.mult)
-        ev(c("kb"), kp, 1.0, 143.50390625)
+        ts(c("endb"), c("nb"), -0.5, None, OP.is_lt)
+        mm(A(X, 0, 32), [((T.ma[:, 3 + m, 12 - 4 * q:140 - 4 * q], ("ma", 0, 144)), A(nm, 128 * h + q, 128 * h + 128, 4))
+                         for m, nm in ((1, "l2"), (0, "nb"), (2, "endb")) for q in range(4)])
+        o = A("o2", 128 * h, 128 * h + 32)
+        ts(o, A(X, 0, 32), -16.0, 4096.0, OP.add, OP.min)
+        a = 2048 * h
+        gat(A("ge", a, a + 512), A("lut"), o)
+        four = [(A("idn"), A("ge", a + j, a + 512, 4)) for j in range(4)]
+        mm(A(X, 128, 256), four)
+        ev(c("kb"), A(X, 128, 256), 1.0 / 16, 143.53125)
+        mm(A(X, 256, 384), [(A("idn"), A("eio", 0, 128)), (A("i128"), c("kb"))])
+        ts(c("o1"), A(X, 256, 384), -18432.0, None, OP.add)
         gather("g1o", h, "dw%d" % h, "o1", 128 * h)
-        mm(A(X, 128, 256), [(A("idn"), c("eio"))] + [(BIG(3, k), wide("g1o", h, k)) for k in range(16)])
-        ts(c("o2"), A(X, 128, 256), C(14), 4351.0, OP.add, OP.min)
+        mm(A(Y, 256, 384), four + [(A("idn"), c("es2")), (A("in16"), c("kb"))])
+        ts(c("o2"), A(Y, 256, 384), 2304.0, 256.0, OP.add, OP.mult)
         gather("ge", h, "bw0", "o2", 128 * h)
         mm(A(Y, 384, 512), [(A("idn"), c("kb")), (A("idn"), A("e16"))])
-        ts(c("par%d" % (t % 2), 1, 2), A(Y, 384, 512), -144.0, None, OP.add)
+        ts(c("par%d" % (t % 2)), A(Y, 384, 512), -144.0, None, OP.add)
         mm(A(Y, 0, 128), [(BIG(2, k), wide("g1o", h, k)) for k in range(16)])
-        ev(c("ls"), A(Y, 0, 128), 1.0, 3232.0)
+        ev(c("ls"), A(Y, 0, 128), 1.0, 3232.0, relu=True)
         ev(c("uu"), A(Y, 0, 128), 2080.0)
         mm(A(Y, 128, 256), [(BIG(1, k), wide("ge", h, k)) for k in range(16)])
         names(t, h, 1)
@@ -506,60 +580,65 @@ def build(g, core, T, topo):
                    first=False, left=left)
 
     def values12(t, h, left):
+        first = A("v1p", 0, 2048, 4)
+        gat(first, A("fa"), A("pl", 40 * h, 40 * h + 32), FAR)
+        gat(A("p5"), A("fa"), A("pl", 40 * h + 32, 40 * h + 40), FAR)
+        for k in range(1, 4):
+            keep(A("vc", k, 2048, 4, own=(k, k + 1)), first, [[0, 512]], OP.is_ge, 0.0, 0, 0)
+        keep(A("vc", 15, 2048, 16, own=(3, 4)), A("p5"), [[0, 128]], OP.is_ge, 0.0, 0, 0)
+        how = ONE[t][h]
         for s in range(0, 2048, QV):
             a, b = s // 16, (s + QV) // 16
             l1 = A("l1u", 256 * t + 128 * h + a, 256 * t + 128 * h + b)
             l2 = A("lu%d" % (t % 2), 256 * h + a, 256 * h + b)
-            vp = A("v1p", s, s + QV)
-            gat(vp, A("fa"), A("par%d" % (t % 2), 256 * h + a, 256 * h + b), FAR)
-            gmul(A("v2%d" % h, s, s + QV), A("fa"), l2, vp)
-            gmul(A("t2", 2048 * h + s, 2048 * h + s + QV), A("w2%d" % (t % 2)), l2, A("v2%d" % h, s, s + QV))
-            if ON2[t][h]:
-                x = A("t2", 2048 * h + s, 2048 * h + s + QV)
+            x = A("t2", 2048 * h + s, 2048 * h + s + QV)
+            gmul(A("v2%d" % h, s, s + QV), A("fa"), l2, A("v1p", s, s + QV), more=[("vc", 1, 4)])
+            if how == "first":
+                gat(x, A("fw1"), l1, FAR)
+            gmul(A("t1", s, s + QV) if how == "first" else x, A("w2%d" % (t % 2)), l2, A("v2%d" % h, s, s + QV))
+            if how == "on":
                 gmul(x, A("fw1"), l1, x, OP.add)
-            else:
+            elif how != "first":
                 gat(A("t1", s, s + QV), A("fw1"), l1, FAR)
-            if (s + QV) % 1024 == 0:
-                r = s + QV - 1024
-                if ON2[t][h]:
-                    pass
-                elif PE1[t]:
-                    total("t1", r, h, r, left)
-                else:
-                    plus(2048 * h + r, "t1", r)
-                if PE3[t]:
-                    total("t2", 2048 * h + r, h, r, left)
+            if (s + QV) % PW == 0 and how in ("first", "dma"):
+                plus(2048 * h + s + QV - PW, "t1", s + QV - PW)
+        if how == "pe":
+            total("t1", 1024, h, 1024, left)
+        if PE3[t][h]:
+            total("t2", 2048 * h + 1024, h, 1024, left)
 
     def plus(r, nm, a):
-        o, x = A("t2", r, r + 1024), A(nm, a, a + 1024)
-        k = add("G", lambda q, e: [q.dma_start(o[0], x[0], accum_op=OP.add)], [x[1], o[1]], [o[1]], 1000, DM + DB * 8192, kind="d", big=DB * 8192)
+        o, x = A("t2", r, r + PW), A(nm, a, a + PW)
+        k = add("G", lambda q, e: [q.dma_start(o[0], x[0], accum_op=OP.add)], [x[1], o[1]], [o[1]], 900,
+                DM + 300 + 2 * span(o[0], x[0], 4), kind="d", big=2 * span(o[0], x[0], 4))
         ops[k]["sem"] = [sem(), 16]
 
     def values3(t, h, left):
+        end = t == EP - 1 and h == 1
         for s in range(0, 2048, QV):
             a, b = s // 16, (s + QV) // 16
             l3 = A("lu%d" % (t % 2), 256 * h + 128 + a, 256 * h + 128 + b)
             r = s - s % 1024
-            nm = "t1" if PE3[t] and h else "t3"
+            nm = "t1" if h else "t3"
             x = A(nm, s, s + QV)
-            gat(x, A("v2%d" % h), A("par%d" % (t % 2), 256 * h + 128 + a, 256 * h + 128 + b), FAR)
+            gat(x, A("v2%d" % h), A("par%d" % (t % 2), 128 * h + a, 128 * h + b), FAR)
             gmul(x, A("fw3"), l3, x)
-            if (s + QV) % 1024 == 0:
-                if PE3[t] and h and r >= 2048 - SCAN:
-                    o, x, m = A("t2", r, r + 1024), A(nm, r, r + 1024), A("run")
-                    add("V", lambda q, e, o=o, x=x, m=m: [q.tensor_tensor_scan(o[0], m[0], x[0], 0.0, OP.mult, OP.add)],
-                        [x[1], m[1]], [o[1]], cost(o, x))
-                elif PE3[t]:
-                    total(nm, r, h, r, left, h == 1)
-                else:
-                    plus(2048 * h + r, "t3", r)
-                    total("t2", 2048 * h + r, h, r, left)
+            if (s + QV) % 1024 == 0 and end and r >= 2048 - SCAN:
+                o, x, m = A("ys2", r, r + 1024), A(nm, r, r + 1024), A("ohw", 0, 1024)
+                add("V", lambda q, e, o=o, x=x, m=m: [q.tensor_tensor_scan(o[0], m[0], x[0], 0.0, OP.mult, OP.add)],
+                    [x[1], m[1]], [o[1]], cost(o, x))
+            elif (s + QV) % 1024 == 0 and PE3[t][h]:
+                total(nm, r, h, r, left, end)
+            elif (s + QV) % PW == 0 and not PE3[t][h]:
+                plus(2048 * h + s + QV - PW, nm, s + QV - PW)
+        if not PE3[t][h]:
+            total("t2", 2048 * h + 1024, h, 1024, left)
         if h == 1:
-            if PE3[t] and SCAN:
+            if end and SCAN:
                 z = (A("PZ", 256 - SCAN // 16, 256)[0], ("PZ", 0, 256))
-                tt(z, A("t2", 2048 - SCAN + 15, 2048, 16), z, OP.add)
-            tt(A("ys"), A("xvs", 256 * t, 256 * t + 256), A("PZ", 0, 256), OP.mult)
-            dma(T.y[:, 256 * t:256 * t + 256], T.ys[:], [("ys", 0, 256)], [])
+                tt(z, A("ys2", 2048 - SCAN + 15, 2048, 16), z, OP.add)
+            tt(A("ys"), A("xvs"), A("PZ", 0, 256), OP.mult)
+            dma(T.y[:, 256 * t:256 * t + 256], T.ys[:], [("ys", 0, 256)], [], 4)
 
     def products(v):
         for j in range(8):
@@ -569,24 +648,29 @@ def build(g, core, T, topo):
         for k in range(2):
             a, slot = 2048 * k, 2 * v + k
             send([(-2, A("fw1", a, a + 2048), (T.fd[slot], ("fd", slot, slot + 1)))], 8192)
-            j = dma(T.fw3[0:112, a:a + 2048], T.fd[slot, 16:128, :], [("fd", slot, slot + 1)], [("fw3", a, a + 2048)], 8192)
-            dma(T.fw3[112:128, a:a + 2048], T.fd[slot, 0:16, :], [("fd", slot, slot + 1)], [("fw3", a, a + 2048)], twin=j)
+            j = dma(T.fw3[0:112, a:a + 2048], T.fd[slot, 16:128, :], [("fd", slot, slot + 1)], [("fw3", a, a + 2048)], 4)
+            dma(T.fw3[112:128, a:a + 2048], T.fd[slot, 0:16, :], [("fd", slot, slot + 1)], [("fw3", a, a + 2048)], 4, twin=j)
 
     def hot(h, d, gr, u):
         a = 128 * (48 * h + 16 * d + 2 * gr + u)
         return (A("ohw", a, a + 128), (T["xs%d" % h][:, d, 64 * gr + 32 * u:64 * gr + 32 * u + 32], ("xs%d" % h, 8 * d + gr, 8 * d + gr + 1)))
 
     products(0)
+    side[3] = 1
     for t in range(EP):
         last = t == EP - 1
         side[1] = t
+        ops[dma(T.xvs[:], T.xv[:, 256 * t:256 * t + 256], [], [("xvs", 0, 256)])]["soon"] = LATE[2]
+        if last:
+            iota(A("ohw", 0, 1024), [[0, 1024]], 1, 0)
+            keep(A("ohw", 0, 1024), A("ohw", 0, 1024), [[0, 64], [1, 16]], OP.not_equal, 0.0, 0, 0)
         for h in range(2):
             strong(h, 0, "wu" if t else "w1", "th", "l1u", 256 * t + 128 * h)
         for h in range(2):
             second(t, h)
         if not last:
-            left = [33]
-            mm(A("PT"), [(A("nil", p1=1), A("rep", p1=1))], left=left)
+            left = [0]
+            mm(A("PT"), [(A("nil", 0, 128, p1=1), A("rep", p1=1))], left=left)
         for h in range(2):
             e0 = 256 * t + 128 * h
             if not last:
@@ -601,7 +685,7 @@ def build(g, core, T, topo):
             sts = [A("st", 384 * h + 128 * d, 384 * h + 128 * d + 128) for d in range(3)]
             if not last:
                 x = A("PX%d" % h, 128, 136)
-                mm(x, [(s, A("g8")) for s in sts] + [(A("askb", e0, e0 + 128, p1=8), A("ni8", p1=8))])
+                mm(x, [(s, A("g8")) for s in sts] + [(A("askb", e0, e0 + 128, p0=32, p1=40), A("ni8", p0=32, p1=40))])
                 ts(A("fl", 8 * h, 8 * h + 8), x, -0.5, 64.0, OP.is_gt, OP.mult)
                 for gr in range(8):
                     x = (T["xs%d" % h][:, :, 64 * gr:64 * gr + 64], None)
@@ -616,11 +700,11 @@ def build(g, core, T, topo):
             mm(y8, [(A("g8"), s) for s in sts])
             ev(A("cvs", 128 * h, 128 * h + 128, p1=8), y8)
             if h == 1:
-                dma(T.cv[:, 256 * t:256 * t + 256], T.cvs[0:8, :], [("cvs", 0, 256)], [])
+                dma(T.cv[:, 256 * t:256 * t + 256], T.cvs[0:8, :], [("cvs", 0, 256)], [], 4, few=True)
             side[0] = 1
             if h == 0:
-                lz = [1 + 16 * (1 + PE1[t] + PE3[t]) - PE3[t] * SCAN // 256]
-                mm(A("PZ", 0, 256), [(A("nil", p1=1), A("rep", 0, 256, p1=1))], left=lz)
+                lz = [0]
+                mm(A("PZ", 0, 256), [(A("nil", 0, 128, p1=1), A("rep", 0, 256, p1=1))], left=lz)
             side[2] = ROOM[t][h][0]
             values12(t, h, lz)
             side[2] = ROOM[t][h][1]
@@ -635,7 +719,7 @@ def build(g, core, T, topo):
             mm(A("PS0", 32 * gr, 32 * gr + 32), [hot(h, 0, gr, u) for h in range(2) for u in range(2)])
         ev(A("c0"), A("PS0", 0, 256))
         send([(1, A("cs", o, o + 256), A("cin", o, o + 256)), (2, A("cs", o + 256, o + 512), A("cin", o + 256, o + 512))],
-             0, wr=[("w2%d" % ((t + 1) % 2), 0, NW)])
+             512, wr=[("w2%d" % ((t + 1) % 2), 0, NW)])
         for b in range(2):
             x = A("PX%d" % b, 0, 128)
             mm(x, [(A("one", p1=1), A("one", p1=1)), (A("c0", b, 256, 2), A("dff"))], final=False, wr=[A("PX%d" % b)[1]])
@@ -666,36 +750,76 @@ def after(row, t):
     return a
 
 
-def replay(ops, at, pred, pace):
-    free, end = {}, {}
-    for i in sorted(at, key=lambda i: (at[i][0], i)):
-        o, e = ops[i], at[i][1]
-        t = max([end[j] + HOP * pace[5] for j, soft in pred[i] if not soft or at[j][1] != e] + [free.get(e, 0.0)]
-                + [free[b][0] for b in o["banks"] if b in free and free[b][1] != e])
-        occ = o["occ"][e] * (pace[0] if o["ga"] else pace[2] if e == "P" else pace[1])
-        end[i] = t + occ + o["lag"] * pace[3]
-        if o["big"] > 300:
-            end[i] = max(end[i], free.get("D", 0.0) + o["big"] * pace[3])
-            free["D"] = end[i]
+def digest(ops, pred):
+    return [([j for j, s in pred[i] if not s], [j for j, s in pred[i] if s], o["banks"], o["occ"], o["ga"], o["lag"], o["big"])
+            for i, o in enumerate(ops)]
+
+
+def walk(seq, eng, steps, pace, why=None):
+    pg, po, pp, pd, div, ph, pb = pace
+    hop = HOP * ph
+    free, last, line = {}, {}, []
+    end = [0.0] * len(steps)
+    top = 0.0
+    for i in seq:
+        hard, soft, banks, occ, ga, lag, big = steps[i]
+        e = eng[i]
+        t, w = free.get(e, 0.0), -1
+        for j in hard:
+            if end[j] > t:
+                t, w = end[j], j
+        for j in soft:
+            if eng[j] != e and end[j] > t:
+                t, w = end[j], j
+        for b in banks:
+            j = last.get(b, i)
+            if eng[j] != e and end[j] > t:
+                t, w = end[j], -2 - j
+            last[b] = i
+        if why is not None:
+            why[i] = (w, last.get(e))
+            last[e] = i
+        c = t + occ[e] * (pg if ga else pp if e == "P" else po)
+        x = c + lag * pd
+        if big:
+            s, d = c + 1000.0 * pd, big * pb
+            k = after(line, s)
+            while k < len(line) and line[k][0] < s + d:
+                s, k = line[k][1], k + 1
+            line.insert(k, (s, s + d))
+            x = max(x, s + d + 700.0 * pd)
         if e != " ":
-            free[e] = t + occ
-        for b in o["banks"]:
-            free[b] = (end[i] + HOP * pace[5], e)
-    return max(end.values()) / pace[4]
+            free[e] = c
+        if x >= top:
+            top, tail = x, i
+        end[i] = x + hop
+    if why is not None:
+        why[-1] = tail
+    return top / div
+
+
+def replay(ops, at, pred, pace):
+    return walk(sorted(at, key=lambda i: (at[i][0], i)), [at[i][1] for i in range(len(ops))], digest(ops, pred), pace)
 
 
 def place(ops, order, before, back, f):
     busy, at = {}, {}
-    for i in order:
+    for i in order if back else sorted(order, key=lambda i: ops[i].get("fix", 1e9)):
         o = ops[i]
         best = None
+        if "fix" in o and not back:
+            row = busy.setdefault("D", [])
+            t = row[-1][1] if row else 0.0
+            row.append((t, t + o["big"]))
+            at[i] = (o["fix"], o["eng"], t + o["lag"])
+            continue
         off = o["lag"] if back else 0.0
         for e in o["eng"] or " ":
             t = max([at[j][2] + (-o["lag"] if soft and at[j][1] == e else HOP) for j, soft in before[i]]
                     + [o["room"] if back else o["soon"]]) + off
             occ = o["occ"][e] * f[i]
             res = [] if e == " " else [(e, occ)] + [(b, occ + (0 if b in OWN else BANK)) for b in o["banks"]]
-            if o["big"] > 300:
+            if o["big"] > 100:
                 res.append(("D", o["big"]))
             moved = True
             while moved:
@@ -713,11 +837,181 @@ def place(ops, order, before, back, f):
     return at
 
 
+def refine(ops, at, pred, succ):
+    n, Q, k = len(ops), "VAPGS ", len(TRIED)
+    steps = digest(ops, pred)
+    seq = sorted(range(n), key=lambda i: (at[i][0], i))
+    eng = [at[i][1] for i in range(n)]
+    hard = []
+    for i in range(n):
+        h = set(steps[i][0])
+        for j in list(h):
+            h -= set(steps[j][0])
+        hard.append(sorted(h))
+    cnt = np.array([len(h) for h in hard])
+    pre = np.full((n, int(cnt.max())), n)
+    names = sorted(set(b for o in ops for b in o["banks"]))
+    nb = len(names)
+    bank = np.full((n, 2), nb)
+    occ = np.zeros((k, n, 6))
+    for i, o in enumerate(ops):
+        pre[i, :len(hard[i])] = hard[i]
+        bank[i, :len(o["banks"])] = [names.index(b) for b in o["banks"]]
+        for e, c in o["occ"].items():
+            occ[:, i, Q.index(e)] = [c * (p[0] if o["ga"] else p[2] if e == "P" else p[1]) for p in TRIED]
+    lag, big = np.array([o["lag"] for o in ops]), np.array([o["big"] for o in ops])
+    x = [99]
+
+    def pick(z):
+        x[0] = (x[0] * 1103515245 + 12345) % 2147483648
+        return (x[0] >> 8) % z
+
+    def marks(cands):
+        B = len(cands) * k
+        S = np.repeat(np.array([s for s, e in cands]), k, 0).T.copy()
+        E = np.repeat(np.array([[Q.index(z) for z in e] for s, e in cands]), k, 0)
+        E = np.take_along_axis(E, S.T, 1).T.copy()
+        ar, pi = np.arange(B), np.tile(np.arange(k), len(cands))
+        pd, ph, pb, div = [np.array([p[z] for p in TRIED])[pi] for z in (3, 5, 6, 4)]
+        OCC, LAG, BIG = occ[pi[None, :], S, E], lag[S] * pd + HOP * ph, big[S] * pb
+        b0, b1 = bank[S, 0], bank[S, 1]
+        anyb, top, use0, use1 = BIG.max(1) > 0, cnt[S].max(1), b0.min(1) < nb, b1.min(1) < nb
+        end, free, line = np.zeros((n + 1) * B), np.zeros(6 * B), np.zeros(B)
+        bend, beng = np.zeros((nb + 1) * B), np.zeros((nb + 1) * B, int)
+        SI, EI, B0, B1 = S * B + ar, E * B + ar, b0 * B + ar, b1 * B + ar
+        d0, d1 = 1000.0 * pd, 700.0 * pd + HOP * ph
+        for p in range(n):
+            ei = EI[p]
+            t = free[ei]
+            if top[p]:
+                t = np.maximum(t, end[pre[S[p], :top[p]].T * B + ar].max(0))
+            if use0[p]:
+                t = np.maximum(t, bend[B0[p]] * (beng[B0[p]] != ei))
+            if use1[p]:
+                t = np.maximum(t, bend[B1[p]] * (beng[B1[p]] != ei))
+            t += OCC[p]
+            free[ei] = t
+            free[5 * B:] = 0.0
+            y = t + LAG[p]
+            if anyb[p]:
+                on = BIG[p] > 0
+                line = np.where(on, np.maximum(line, t + d0) + BIG[p], line)
+                y = np.where(on, np.maximum(y, line + d1), y)
+            end[SI[p]] = y
+            if use0[p]:
+                bend[B0[p]], beng[B0[p]] = y, ei
+                if use1[p]:
+                    bend[B1[p]], beng[B1[p]] = y, ei
+                bend[nb * B:] = 0.0
+        end = end.reshape(n + 1, B)[:n]
+        return ((end.max(0) + EARLY * end.mean(0)) / div).reshape(-1, k).sum(1), end - LAG[np.argsort(S, 0), ar]
+
+    def moved(s, e, mv):
+        i, to, q, a, grp = mv
+        if to < a:
+            s = s[:to] + list(grp) + [j for j in s[to:a + 1] if j not in grp] + s[a + 1:]
+        else:
+            s = s[:a] + [j for j in s[a:to + 1] if j not in grp] + list(grp) + s[to + 1:]
+        e = list(e)
+        e[i] = q
+        return s, e
+
+    def timed(s, e, st):
+        key, last = {}, {}
+        for z, i in enumerate(s):
+            on = [b for b in [e[i]] + ops[i]["banks"] if b != " "]
+            key[i] = (max([st[i]] + [key[j][0] for j, soft in pred[i]] + [last[b] for b in on if b in last]), z)
+            last.update((b, key[i][0]) for b in on)
+        return sorted(s, key=lambda i: key[i])
+
+    mark = marks([(seq, eng)])[0][0]
+    best, late = (mark, seq, eng), {}
+    for r in range(ROUNDS):
+        pos = [0] * n
+        for z, j in enumerate(seq):
+            pos[j] = z
+        runs = []
+        for p in TRIED:
+            why = {}
+            walk(seq, eng, steps, p, why)
+            u, i = [why[-1]], why[-1]
+            while why[i] != (-1, None):
+                w, q = why[i]
+                if w < 0:
+                    i = q if w == -1 else -2 - w
+                    u.append(i)
+                else:
+                    runs.append(u[::-1])
+                    i, u = w, [w]
+            runs.append(u[::-1])
+        runs = [u for u in runs if len(u) > 1 for z in range(1 + len(u) // 6)]
+        mvs = set()
+        for z in range(3 * WIDE):
+            u = runs[pick(len(runs))]
+            a = pick(len(u))
+            i, how = u[a], pick(6)
+            if how == 5:
+                i = seq[min(n - 1, max(0, pos[i] + pick(41) - 20))]
+            q = eng[i]
+            if how == 0 and len(ops[i]["eng"]) == 2:
+                q = ops[i]["eng"].replace(q, "")
+                to = pos[i] + pick(21) - 12
+            elif how < 3 and a > 0:
+                to = pos[u[max(0, a - 1 - pick(8))]]
+            elif how < 5 and a < len(u) - 1:
+                to = pos[u[min(len(u) - 1, a + 1 + pick(8))]]
+            else:
+                to = pos[i] + pick(61) - 30
+            if pick(3) == 0:
+                to += (to - pos[i]) * pick(4)
+            to, grp = min(n - 1, max(5, to)), [i]
+            for j in grp:
+                grp += [y for y, s in (pred if to < pos[i] else succ)[j] if min(to, pos[i]) <= pos[y] <= max(to, pos[i]) and y not in grp]
+                if len(grp) > 14:
+                    lo, hi = max([0] + [pos[y] + 1 for y, s in pred[i]]), min([n - 1] + [pos[y] - 1 for y, s in succ[i]])
+                    to, grp = min(hi, max(lo, to)), [i]
+                    break
+            if "fix" not in ops[i] and to > 4 and (to != pos[i] or q != eng[i]) and len(mvs) < WIDE:
+                mvs.add((i, to, q, pos[i], tuple(sorted(grp, key=lambda j: pos[j]))))
+        mvs = sorted(mvs)
+        got = marks([moved(seq, eng, mv) for mv in mvs])[0]
+        good = [mvs[z] for z in np.argsort(got) if got[z] < mark - 1.0]
+        if not good:
+            good = [mvs[z] for z in np.argsort(got) if r - late.get(mvs[z][0], -99) > 30][:1 + pick(3)]
+        late.update((mv[0], r) for mv in good[:3])
+        cands, cur, spans = [], (seq, eng), []
+        for mv in good:
+            a, b = min(pos[mv[0]], mv[1]), max(pos[mv[0]], mv[1])
+            if all(b < c - 1 or a > d + 1 for c, d in spans) and len(cands) < 16:
+                spans.append((a, b))
+                cur = moved(cur[0], cur[1], mv)
+                cands.append(cur)
+        if not cands:
+            continue
+        got, ends = marks(cands)
+        z = int(np.argmin(got)) if min(got) < mark else len(cands) - 1
+        (seq, eng), mark = cands[z], got[z]
+        if r % 4 == 3:
+            seq = timed(seq, eng, ends[:, z * k:z * k + k].sum(1))
+            mark = marks([(seq, eng)])[0][0]
+        if mark < best[0]:
+            best = (mark, seq, eng)
+    return best
+
+
 KEPT = []
 
 
 def plan(ops):
     n = len(ops)
+    twins = {}
+    for i, o in enumerate(ops):
+        if "sem" in o:
+            twins.setdefault(o["sem"][0], []).append(i)
+    for o in ops:
+        for j in list(o["deps"]):
+            if "sem" in ops[j]:
+                o["deps"].update((k, True) for k in twins[ops[j]["sem"][0]])
     pred = [[(j, not hard) for j, hard in o["deps"].items()] for o in ops]
     succ = [[] for _ in ops]
     up = [0.0] * n
@@ -742,6 +1036,9 @@ def plan(ops):
             f.append(1 + SHAKE * (x / 1073741824.0 - 1))
         bk = place(ops, sorted(range(n), key=lambda i: (-at[i][2], -i)), succ, True, f)
         at = place(ops, sorted(range(n), key=lambda i: (-bk[i][2], i)), pred, False, even)
+    if not KEPT and ROUNDS:
+        mark, seq, eng = refine(ops, best[1], pred, succ)
+        best = (mark, dict((i, (k, eng[i], k)) for k, i in enumerate(seq)))
     KEPT[:] = [best]
     for i in range(n):
         ops[i]["t"], ops[i]["e"], ops[i]["end"] = best[1][i]

import numpy as np
from concourse.bass import DstId, RemoteDMATransfer
from concourse.mybir import AluOpType as OP, ActivationFunctionType as AF

NW, E, EP, H = 4096, 256, 3, 128
BF, F32, I32, U16 = "bfloat16", "float32", "int32", "uint16"
QG, QV = 1024, 1024


def _sb(cols, d):
    return ("sbuf", [128, cols], d)


SCRATCH = {
    "w1": _sb(NW, BF), "w20": _sb(NW, BF), "w21": _sb(NW, BF), "w3": _sb(NW, BF), "fa": _sb(NW, BF),
    "fw1": _sb(NW, F32), "fw3": _sb(NW, F32),
    "fd": ("dram", [6, 128, NW // 2], F32), "wd": ("dram", [6, 128, NW // 2], BF), "thd": ("dram", [128, 8], F32),
    "bd": ("dram", [3, 8, 2, 20, 256], BF), "ld": ("dram", [8, 32, 256], BF),
    "bdg": _sb(1024, BF), "l1u": _sb(768, U16), "lut": _sb(4104, BF),
    "p5": _sb(128, BF), "pl": _sb(80, U16), "i128": _sb(128, BF), "in16": _sb(128, BF),
    "bw0": _sb(17 * 256, BF), "dw0": _sb(17 * H, BF), "dw1": _sb(17 * H, BF),
    "ge": _sb(4096, BF), "g1o": _sb(4096, BF), "ohw": _sb(12288, BF),
    "v1p": _sb(2048, BF), "v20": _sb(2064, F32), "v21": _sb(2064, F32),
    "t1": _sb(2048, F32), "t2": _sb(4096, F32), "t3": _sb(2048, F32), "idf": _sb(128, F32),
    "xs0": ("sbuf", [128, 3, 512], BF), "xs1": ("sbuf", [128, 3, 512], BF),
    "st": _sb(768, BF), "nb": _sb(256, BF), "endb": _sb(256, BF), "kb": _sb(256, BF),
    "o1": _sb(256, U16), "o2": _sb(256, U16), "par0": _sb(256, U16), "par1": _sb(256, U16), "lu0": _sb(512, U16), "lu1": _sb(512, U16),
    "ls": _sb(256, F32), "uu": _sb(256, F32), "ti": _sb(256, I32), "li": _sb(256, I32),
    "di": _sb(512, I32), "dh": _sb(512, BF), "dl": _sb(512, BF), "l2": _sb(256, BF),
    "lot": _sb(96, BF), "fl": _sb(16, BF), "fab": _sb(32, BF),
    "labx": _sb(512, BF), "rx": _sb(512, BF),
    "cs": _sb(512, BF), "cin": _sb(512, BF), "c0": _sb(256, F32), "dff": _sb(128, F32), "e512": _sb(128, BF), "fct": _sb(256, BF),
    "xvs": _sb(256, BF), "ys": _sb(256, F32),
    "cvs": _sb(256, F32), "taus": _sb(4, F32), "tw": _sb(16, F32), "tb": _sb(8, BF), "th": _sb(8, F32),
    "th2": _sb(8, F32), "th3": _sb(8, F32),
    "q144": _sb(144, F32), "pc": _sb(8, I32), "col": _sb(32, F32),
    "km": _sb(16, F32), "idn": _sb(128, BF), "blk": _sb(128, BF), "tri": _sb(256, BF),
    "big": _sb(4 * 144, BF), "sel": _sb(2048, BF), "g8": _sb(8, BF),
    "ni8": _sb(8, BF), "selu": _sb(16, BF), "rep": _sb(512, BF), "one": _sb(128, BF), "nil": _sb(256, BF),
    "eio": _sb(256, BF), "es2": _sb(256, BF), "e16": _sb(128, BF), "eo": _sb(80, BF),
    "ma": ("sbuf", [128, 6, 144], BF), "mb": ("sbuf", [128, 3, 128], BF), "mc": ("sbuf", [128, 3, 128], BF),
    "mw": ("sbuf", [128, 6, 8], F32),
}
PART = {"askb": "labx", "dia": "di", "vc": "v1p"}
for _b in ("X0", "Y0", "X1", "Y1", "Z", "T", "S0", "S1"):
    SCRATCH["P" + _b] = ("psum", [128, 512], F32)
SEMAPHORES = ["cV", "cA", "cP", "cG"] + ["s%d" % i for i in range(146)]

OV, CY, PCY, GA, HOP, DM = 40.0, 0.9, 0.45, 1.35, 200.0, 1900.0
ROW, BW, FARB, FIRST = 10.0, 38.0, 1.3, 3000.0
PASSES, SHAKE, NEAR, FAR, GN = 40, 0.5, 900.0, 8000.0, 2000.0
POV, SCAN, SLACK = 20.0, 2048, 2000.0
ROOM = (((0.0, 0.0), (0.0, 0.0)), ((20000.0, 20000.0), (20000.0, 20000.0)), ((10000.0, 4000.0), (6000.0, 0.0)))
ONE = (("first", "first"), ("dma", "dma"), ("on", "on"))
LATE = (5500.0, 8000.0, 20000.0)
PW = 1024
PACES = TRIED = ((0.65, 0.9, 0.82, 0.95, 0.76, 0.6, 1.0), (1.0, 1.25, 1.25, 1.25, 1.3, 1.2, 2.0),
                 (0.9, 0.95, 0.9, 1.0, 0.93, 0.7, 1.0), (1.6, 1.2, 1.1, 1.1, 1.4, 1.0, 1.1))
ROUNDS, WIDE, EARLY = 450, 64, 0.1
BANK, OWN = 150.0, ("PZ", "PT")
PLAIN = ("AV", "AV")
ONV = ("", "", "")
REST = "AV"
SIDE = "AV"
TILT = (1.0, 1.0, 1.0)
PE3 = ((0, 0), (0, 0), (1, 1))


def build(g, core, T, topo):
    rank = T.rank_of(core)
    n = len(T.cores)
    ops, acc, nsem, side = [], {}, [0], [0, 0, 0.0, 0]

    def A(name, a=0, b=None, s=1, p0=0, p1=128, ps=1, own=None):
        if b is None:
            b = NW if name == "wu" else SCRATCH[PART.get(name, name)][1][1]
        if name == "ys2":
            name = "fw1"
        if name == "wu":
            name, a, b = "ohw", a + 8192, b + 8192
        return (T[PART.get(name, name)][p0:p1:ps, a:b:s], (name,) + (own or (a, b)))

    def kind(x):
        return SCRATCH[PART.get(x[1][0], x[1][0])][2]

    def add(eng, fn, rd, wr, occ, lag=0.0, kind="c", after=(), lean=NEAR, big=0.0, ga=False, soon=0.0):
        i = len(ops)
        deps = dict((j, True) for j in after)
        for regs, w in ((rd, False), (wr, True)):
            for nm, a, b in regs:
                for j, c, d, w2 in acc.setdefault(nm, []):
                    if j == i:
                        continue
                    if a < d and c < b and (w or w2):
                        near = eng == ops[j]["eng"] == "P" and (c, d) == (a, b) and (nm, a, b) in rd
                        deps[j] = deps.get(j, False) or not near
                if w:
                    acc[nm] = [x for x in acc[nm] if not (a <= x[1] and x[2] <= b)]
                acc[nm].append((i, a, b, w))
        if not isinstance(occ, dict):
            occ = dict((e, occ) for e in eng or " ")
        ops.append(dict(eng=eng, fn=fn, deps=deps, occ=occ, lag=lag, kind=kind, lean=lean * TILT[side[1]], big=big, side=side[0], ga=ga, soon=soon, room=side[2],
                        banks=sorted(set(x[0] for x in list(rd) + list(wr) if x[0][0] == "P"))))
        return i

    def sem():
        nsem[0] += 1
        return "s%d" % (nsem[0] - 1)

    def wid(x):
        k = 1
        for z in x[0].shape[1:]:
            k *= int(z)
        return k

    def cost(*xs):
        two = all(kind(x) in (BF, U16) for x in xs)
        return OV + CY * max(64, wid(xs[0]) * (0.5 if two else 1))

    def both(o, i):
        return {"A": OV + CY * max(64, wid(o)), "V": cost(o, i)}

    def ts(o, i, s1, s2, op0, op1=None):
        if len(o[0].shape) == 2 and all(kind(x) in (BF, F32) for x in (o, i)) and s1 is not None:
            if (op0, op1) == (OP.mult, OP.add):
                return ev(o, i, s1, s2)
            if op1 is None and op0 in (OP.mult, OP.add):
                return ev(o, i, s1) if op0 == OP.mult else ev(o, i, 1.0, s1)
        rd = [i[1]] + [s[1] for s in (s1, s2) if isinstance(s, tuple)]
        v1 = s1[0] if isinstance(s1, tuple) else s1
        v2 = s2[0] if isinstance(s2, tuple) else s2
        if op1 is None:
            fn = lambda q, e: [q.tensor_scalar(o[0], i[0], v1, None, op0)]
        else:
            fn = lambda q, e: [q.tensor_scalar(o[0], i[0], v1, v2, op0, op1)]
        return add("V", fn, rd, [o[1]], cost(o, i))

    def tt(o, a, b, op):
        k = 1 if "P" in (a[1][0][0], b[1][0][0]) else 2
        return add("V", lambda q, e: [q.tensor_tensor(o[0], a[0], b[0], op)], [a[1], b[1]], [o[1]], OV + CY * max(64, k * wid(o)))

    def cp(o, i):
        return add("V", lambda q, e: [q.tensor_copy(o[0], i[0])], [i[1]], [o[1]], cost(o, i))

    def ev(o, i, scale=1.0, bias=0.0, relu=False, lean=NEAR):
        rd = [i[1]] + [s[1] for s in (scale, bias) if isinstance(s, tuple)]
        scale, bias = [s[0] if isinstance(s, tuple) else s for s in (scale, bias)]
        def fn(q, e):
            if e == "A":
                return [q.activation(o[0], i[0], AF.Relu if relu else AF.Identity, bias=bias, scale=scale)]
            if relu:
                return [q.tensor_scalar(o[0], i[0], bias, 0.0, OP.add, OP.max)]
            return [q.tensor_scalar(o[0], i[0], scale, bias, OP.mult, OP.add)]
        return add(PLAIN[side[3]], fn, rd, [o[1]], both(o, i), lean=lean, soon=200.0)

    def gt(o, i, c, up=True, eng="VA", soon=0.0):
        k = 512.0 if up else -512.0
        def fn(q, e):
            if e == "A":
                return [q.activation(o[0], i[0], AF.Sigmoid, bias=-k * c, scale=k)]
            return [q.tensor_scalar(o[0], i[0], c, None, OP.is_gt if up else OP.is_lt)]
        return add(eng, fn, [i[1]], [o[1]], both(o, i), lean=50.0, soon=max(soon, 200.0))

    def step(o, col, eng):
        i = A("e512")
        def fn(q, e):
            if e == "A":
                return [q.activation(o[0], i[0], AF.Sigmoid, bias=col[0])]
            return [q.tensor_scalar(o[0], i[0], col[0], 0.0, OP.add, OP.is_gt)]
        return add(eng, fn, [i[1], col[1]], [o[1]], both(o, i))

    def sc(o, i, col):
        def fn(q, e):
            if e == "A":
                return [q.activation(o[0], i[0], AF.Identity, scale=col[0])]
            return [q.tensor_scalar(o[0], i[0], col[0], None, OP.mult)]
        return add("AV", fn, [i[1], col[1]], [o[1]], both(o, i), lean=FAR)

    def ms(o, v):
        return add("V", lambda q, e: [q.memset(o[0], v)], [], [o[1]], cost(o))

    def iota(o, pat, base, cm):
        if kind(o) == I32:
            fn = lambda q, e: [q.iota(o[0], pat, base, cm)]
        else:
            fn = lambda q, e: [q.iota(o[0], pat, base, cm, allow_small_or_imprecise_dtypes=True)]
        return add("G", fn, [], [o[1]], 150 + 2 * CY * wid(o))

    def keep(o, i, pat, op, fill, base, cm):
        return add("G", lambda q, e: [q.affine_select(o[0], i[0], pat, op, fill, base, cm)], [i[1]], [o[1]], 190 + 2 * CY * wid(o))

    def mm(o, pairs, first=True, final=True, left=None, wr=()):
        if left is not None:
            left[0] += 1
        def fn(q, e):
            stop = final
            if left is not None:
                left[0] -= 1
                stop = left[0] == 0
            return [q.matmul(o[0], l[0], r[0], first and k == 0, stop and k == len(pairs) - 1) for k, (l, r) in enumerate(pairs)]
        return add("P", fn, [x[1] for pr in pairs for x in pr] + ([] if first else [o[1]]), [o[1]] + list(wr),
                   sum(POV + PCY * max(64, wid(o)) * (4 if kind(l) == F32 else 1) for l, r in pairs), 60)

    def gat(o, win, off, lean=NEAR, eng=None):
        def fn(q, e):
            src = win[0].indirect(off[0])
            return [q.activation(o[0], src, AF.Copy) if e == "A" else q.tensor_copy(o[0], src)]
        rd = [win[1], off[1]] + [("bws", 0, 1)] * (win[1][0] == "bw0") + [("dws" + win[1][0][2:], 0, 1)] * (win[1][0][:2] == "dw")
        return add(eng or REST, fn, rd, [o[1]], 60 + GA * wid(o), lean=lean, ga=True)

    def gge(o, win, off, thr, d, eng):
        pos, neg = A(thr, d, d + 1), A(thr, 4 + d, 5 + d)
        def fn(q, e):
            src = win[0].indirect(off[0])
            if e == "A":
                return [q.activation(o[0], src, AF.Sign, bias=neg[0])]
            return [q.tensor_scalar(o[0], src, pos[0], 0.5, OP.is_ge, OP.subtract)]
        return add(eng, fn, [win[1], off[1], (thr, 0, 8)], [o[1]], 60 + GA * wid(o), lean=GN, ga=True)

    def gmul(o, win, off, b, op=OP.mult, more=()):
        return add("V", lambda q, e: [q.tensor_tensor(o[0], win[0].indirect(off[0]), b[0], op)],
                   [win[1], off[1], b[1]] + list(more), [o[1]], 55 + GA * wid(o), ga=True)

    def span(o, i, size, k=16):
        m = 1
        for z in o.shape:
            m *= int(z)
        return (ROW * m / min(int(o.shape[-1]), int(i.shape[-1])) + m * size / BW) / k

    def dma(o, i, rd, wr, size=2, eng="S", twin=None, few=False):
        fn = lambda q, e: [q.dma_start(o, i)]
        d = span(o, i, size, 8 if few else 16)
        if twin is None:
            k = add(eng, fn, rd, wr, 80, DM + d * (1.6 if few else 1), kind="d", big=d)
            ops[k]["sem"] = [sem(), 16]
        else:
            k = add(eng, fn, rd, [], 80, DM + d * (1.6 if few else 1), kind="d", after=list(ops[twin]["deps"]), big=d)
            for nm, a, b in wr:
                acc[nm].append((k, a, b, True))
            ops[k]["sem"] = ops[twin]["sem"]
            ops[k]["sem"][1] += 16
        return k

    def send(parts, nb, wr=()):
        ls, rs = sem(), [sem() for _ in parts]
        trs, cnt = [], []
        for k, (ahead, src, dst) in enumerate(parts):
            to = T.cores[(rank + ahead) % n]
            en = topo.engines(core, to)
            m = len(en) // len(parts)
            rid, pid = topo.addr(to)[:2]
            trs.append(RemoteDMATransfer(dst_ids=[DstId(rid=rid, pnc=pid)], dma_engine_mask=sum(1 << x for x in en[k * m:(k + 1) * m]),
                                         remote_sem=T.sem[rs[k]], src=src[0], dst=dst[0]))
            cnt.append(m)
        d = 128 * len(parts) * (ROW + FARB * nb / BW) / 16
        first = FIRST * (not any(o["kind"] == "r" for o in ops))
        i = add("G", lambda q, e: [q.remote_dma_fused(trs, local_sem=T.sem[ls])], [p[1][1] for p in parts], list(wr),
                400 + first, DM + d, kind="r", big=d)
        ops[i]["tok"] = (ls, sum(cnt))
        for j in [j for j in range(i) if ops[j]["kind"] == "r"][:1]:
            ops[i]["deps"].setdefault(j, False)
        for k, p in enumerate(parts):
            j = add("", None, [], [p[2][1]], 0, 300 + SLACK * (p[0] == -2 and nb > 1024), kind="a", after=[i])
            ops[j]["tok"] = (rs[k], cnt[k])

    for k, j in enumerate((
            dma(T.ti[:], T.bn[:, 0:256], [], [("ti", 0, 256)], 4, "A"),
            dma(T.taus[:, 0:3], T.tau[:], [], [("taus", 0, 4)], 4, "A"),
            dma(T.w1[:, 0:2048], T.wt[:, 0:2048], [], [("w1", 0, 2048)]),
            dma(T.w1[:, 2048:NW], T.wt[:, 2048:NW], [], [("w1", 2048, NW)]))):
        ops[j]["fix"] = 100.0 * k
    ops[dma(T.fa[:], T.ft[:], [], [("fa", 0, NW)])]["soon"] = LATE[0]
    ops[dma(T.di[:], T.bn[:, 256:768], [], [("di", 0, 512), ("dia", 0, 512)], 4)]["soon"] = LATE[1]

    def send_w(v, k):
        half = A("w1", k * 2048, (k + 1) * 2048)
        slot = 2 * v + k
        send([(-1, half, A("w2%d" % (v % 2), k * 2048, (k + 1) * 2048))], 4096)
        send([(-2, half, (T.wd[slot], ("wd", slot, slot + 1)))], 4096)
        c = slice(k * 2048, (k + 1) * 2048)
        j = dma(T.w3[0:112, c], T.wd[slot, 16:128, :], [("wd", slot, slot + 1)], [("w3", k * 2048, (k + 1) * 2048)])
        dma(T.w3[112:128, c], T.wd[slot, 0:16, :], [("wd", slot, slot + 1)], [("w3", k * 2048, (k + 1) * 2048)], twin=j)

    ta = A("taus", 0, 3)
    cp(A("tb", 0, 3), ta)
    tt(A("tw", 0, 3), A("tb", 0, 3), ta, OP.is_ge)
    ts(A("tw", 4, 7), A("tw", 0, 3), -2.0 ** -9, 1 + 2.0 ** -10, OP.mult, OP.add)
    tt(A("tw", 8, 11), A("tw", 4, 7), A("tb", 0, 3), OP.mult)
    ts(A("tw", 12, 15), ta, 0.25, None, OP.is_gt)
    ms(A("th"), 0.0)
    tt(A("tw", 0, 3), A("tw", 8, 11), A("tw", 12, 15), OP.mult)
    ts(A("th", 0, 3), A("tw", 0, 3), 0.01, None, OP.max)
    ts(A("th", 4, 7), A("tw", 0, 3), -1.0, -0.01, OP.mult, OP.min)
    send_w(0, 0)
    send_w(0, 1)
    send([(-1, A("th"), A("th2")), (-2, A("th"), (T.thd[:], ("thd", 0, 8)))], 32)
    j = dma(T.th3[0:112, :], T.thd[16:128, :], [("thd", 0, 8)], [("th3", 0, 8)], 4)
    dma(T.th3[112:128, :], T.thd[0:16, :], [("thd", 0, 8)], [("th3", 0, 8)], 4, twin=j)

    C = lambda j: A("col", j, j + 1)
    iota(A("pc", 0, 1), [[0, 1]], 0, 1)
    iota(A("q144"), [[1, 144]], 0, 0)
    iota(A("eio"), [[1, 256]], 0, 0)
    ms(A("one"), 1.0)
    GR = [[-16, 8], [0, 16]]
    keep(A("idn"), A("one"), [[1, 128]], OP.is_equal, 0.0, 0, -1)
    keep(A("blk"), A("one"), GR, OP.is_ge, 0.0, 0, 1)
    keep(A("blk"), A("blk"), [[16, 8], [0, 16]], OP.is_ge, 0.0, 15, -1)
    keep(A("tri", 128, 256), A("blk"), [[1, 128]], OP.is_ge, 0.0, 0, -1)
    iota(A("e16"), [[16, 128]], 0, 0)
    iota(A("e512"), [[512, 128]], 0, 0)
    ms(A("nil"), 0.0)
    ms(A("rep"), 1.0)
    keep(A("rep"), A("rep"), [[16, 8], [1, 2], [0, 32]], OP.is_equal, 0.0, 0, -1)
    keep(A("selu"), A("one", 0, 16), [[16, 8], [1, 2]], OP.is_equal, 0.0, 0, -1)
    keep(A("idf"), A("one"), [[1, 128]], OP.is_equal, 0.0, 0, -1)
    keep(A("dff"), A("idf"), [[1, 128]], OP.not_equal, -1.0, -1, -1)
    rx = A("rx", p1=32)
    iota(rx, [[0, 16], [-1, 32]], 16, 0)
    keep(rx, rx, [[0, 512]], OP.not_equal, -160.0, -9, 1)
    keep(rx, rx, [[0, 512]], OP.is_ge, 0.0, -8, 1)
    keep(rx, rx, [[1, 8], [0, 64]], OP.not_equal, 64.0, 0, -1)
    ts(A("pc", 2, 3), A("pc", 0, 1), 4, None, OP.arith_shift_right)
    ts(A("pc", 3, 4), A("pc", 0, 1), 15, None, OP.bitwise_and)
    ts(A("pc", 4, 5), A("pc", 0, 1), 2, 3, OP.arith_shift_right, OP.bitwise_and)
    ts(A("pc", 5, 6), A("pc", 0, 1), 3, None, OP.bitwise_and)
    cp(A("col", 0, 2), A("pc", 2, 4))
    ts(A("pc", 6, 7), A("pc", 0, 1), 7, None, OP.bitwise_and)
    ts(A("pc", 7, 8), A("pc", 0, 1), 3, 1, OP.arith_shift_right, OP.bitwise_and)
    cp(A("col", 28, 32), A("pc", 4, 8))
    ts(C(2), C(0), 16.0, 15.0, OP.mult, OP.add)
    ts(A("km"), A("q144", 0, 16), C(1), None, OP.is_equal)
    K = lambda j: A("km", j, j + 1)
    BIG = lambda j, m: A("big", 144 * j + 15 - m, 144 * j + 143 - m)
    ts(C(3), K(0), 128.0, K(8), OP.mult, OP.add)
    ts(C(4), K(15), -20480.0, C(3), OP.mult, OP.add)
    ts(C(5), K(15), -256.0, 256.0, OP.mult, OP.add)
    ts(A("big", 0, 144), A("q144"), C(2), None, OP.is_equal)
    for j in range(1, 4):
        sc(A("big", 144 * j, 144 * j + 144), A("big", 0, 144), C(2 + j))
    gt(A("tb", 4, 5), C(1), 11.5, False, "A", 200.0)
    ev(C(8), A("tb", 4, 5), 1.0, 3.0)
    sc(A("tri", 0, 128), A("tri", 128, 256), C(8))
    ev(A("ni8"), A("idn", 32, 40), -1.0, lean=FAR)
    ev(A("es2"), A("eio"), 1.0 / 256, lean=FAR)
    keep(A("i128"), A("nil", 0, 128), [[1, 128]], OP.not_equal, 128.0, 0, -1)
    keep(A("in16"), A("nil", 0, 128), [[1, 128]], OP.not_equal, -16.0, 0, -1)
    ts(A("eo", 0, 32), A("q144", 0, 128, 4), C(28), None, OP.add)
    ts(A("eo", 32, 40), A("q144", 0, 128, 16), C(1), None, OP.add)
    ts(A("eo", 40, 80), A("eo", 0, 40), 128.0, None, OP.add)
    ts(A("g8"), A("q144", 0, 8), C(0), None, OP.is_equal)
    MW = lambda m, a, b: (T.mw[:, m, a:b], ("mw", 8 * m + a, 8 * m + b))
    for c, row in enumerate((14, 13, 5, 6, 14)):
        ts(MW(0, c, c + 1), K(row), -8192.0, C(3), OP.mult, OP.add)
    ts(A("col", 24, 28), A("km", 1, 5), 128.0, None, OP.mult)
    tt(MW(1, 0, 4), A("col", 24, 28), A("km", 9, 13), OP.add)
    ts(MW(1, 4, 5), MW(1, 3, 4), 1.0, None, OP.mult)
    ts(MW(2, 0, 4), A("q144", 1, 5), K(15), K(7), OP.mult, OP.add)
    ts(MW(2, 4, 5), K(6), -3.0, MW(2, 3, 4), OP.mult, OP.add)
    ts(MW(3, 0, 4), A("q144", 0, 16, 4), C(1), -256.0, OP.is_gt, OP.mult)
    ts(MW(4, 0, 4), A("km", 0, 16, 4), 16.0, None, OP.mult)
    ts(C(6), C(29), 4.0, -4.0, OP.mult, OP.add)
    ts(C(7), C(29), 1.0, C(6), OP.add, OP.max)
    ts(MW(5, 0, 4), A("q144", 0, 4), C(28), C(7), OP.is_equal, OP.mult)
    ms((T.ma[:], ("ma", 0, 144)), 0.0)
    ms((T.mc[:], ("mc", 0, 8)), 0.0)
    for gr in range(8):
        ts((T.ma[:, :, 16 * gr + 12:16 * gr + 16], ("ma", 16 * gr + 12, 16 * gr + 16)), (T.mw[:, :, 0:4], ("mw", 0, 48)),
           A("g8", gr, gr + 1), None, OP.mult)
    cp((T.mb[:], ("mb", 0, 8)), (T.ma[:, 0:3, 0:128], ("ma", 0, 144)))
    ms((T.mb[:, :, 15:128:16], ("mb", 0, 8)), 0.0)
    for m in range(3):
        ts((T.mc[:, m, 15:128:16], ("mc", m, m + 1)), A("g8"), MW(m, 4, 5), None, OP.mult)

    def MAT(m, j):
        if j < 3:
            return (T.ma[:, m, 12 - 4 * j:140 - 4 * j], ("ma", 0, 144))
        return (T.mb[:, m, :], ("mb", 0, 8)) if j == 3 else (T.mc[:, m, :], ("mc", m, m + 1))

    cp(A("l1u", 0, 256), A("ti"))
    cp(A("l1u", 256, 768), A("di"))
    ts(C(14), C(30), 2.0, -12.5, OP.mult, OP.add)
    ts(C(12), C(31), -1.0, C(14), OP.mult, OP.add)
    ts(C(15), C(31), -3.0, C(14), OP.mult, OP.add)
    ts(C(9), C(31), -1.0, 1.0, OP.mult, OP.add)
    ts(A("col", 16, 18), A("q144", 0, 2), C(12), 0.0, OP.add, OP.is_gt)
    ts(A("col", 18, 20), A("q144", 0, 2), C(15), -1.0, OP.add, OP.is_gt)
    ts(A("col", 22, 24), A("q144", 0, 2), C(14), 12.5, OP.add, OP.add)
    ts(A("col", 20, 22), A("col", 22, 24), C(9), C(31), OP.mult, OP.add)
    for j in range(6):
        ev(A("g1o", 2560 + 256 * j, 2816 + 256 * j), A("eio"), 0.0, C(16 + j))
    k = None
    for j in range(3):
        x = A("g1o", 2560 + 512 * j, 3072 + 512 * j)
        z = dma(T.bw0[5 + j:128:8, 0:4096], x[0], [x[1]], [("bws", 0, 1)], twin=k)
        k = z if k is None else k
    BD = lambda t, d, a=0, b=256: A("bdg", 512 * t + 256 * d + a, 512 * t + 256 * d + b) if t < 2 else A("v1p", 256 * d + a, 256 * d + b)
    for t in range(EP):
        x = A("di", 256 * t - 256, 256 * t) if t else A("ti")
        ts(BD(t, 0), A("l1u", 256 * t, 256 * t + 256), 1.0 / 128, 143.50390625, OP.mult, OP.add)
        ts(BD(t, 0), BD(t, 0), -160.0, None, OP.add)
        ts(x, x, 127, None, OP.bitwise_and)
        cp(BD(t, 1), x)
    ts(C(10), K(0), -17.0, 1.0, OP.mult, OP.add)
    tt(C(10), C(10), K(8), OP.subtract)
    ts(A("bw0", 4096, 4352), A("eio"), 0.0, C(10), OP.mult, OP.add)
    for t in range(EP):
        nm, a, b = BD(t, 0, 0, 512)[1]
        k = dma(T.bd[t, :, 0, 0:16, :], T[nm][:, a:a + 256], [(nm, a, b)], [("bd", t, t + 1)])
        dma(T.bd[t, :, 1, 0:16, :], T[nm][:, a + 256:b], [(nm, a, b)], [("bd", t, t + 1)], twin=k)
        for j in range(4):
            dma(T.bd[t, :, :, 16 + j, :], T[nm][min(13 + j, 15):128:16, a:b], [(nm, a, b)], [("bd", t, t + 1)], twin=k, few=True)

    def window(t):
        k = None
        for r in range(5):
            z = dma(T.bw0[r:128:8, 0:4096], T.bd[t, :, :, r:r + 16, :], [("bd", t, t + 1)], [("bw0", 0, 4096)], twin=k)
            ops[z]["big"] = 300.0
            k = z if k is None else k

    window(0)
    ts(C(11), K(0), 127.0, 1.0, OP.mult, OP.add)
    ts(C(13), K(8), 62.0, C(11), OP.mult, OP.add)
    for h in range(2):
        dma(T["dw%d" % h][:, 0:2048], T.bw0[:, 0:2048], [("bw0", 0, 2048), ("bws", 0, 1)], [("dw%d" % h, 0, 2048)])
        ts(A("dw%d" % h, 2048, 2176), A("eio", 0, 128), 0.0, C(13), OP.mult, OP.add)
        ms(A("v2%d" % h, 2048, 2064), 0.0)

    U = lambda j, w=1: A("ohw", 8192 + 256 * j, 8192 + 256 * (j + w))
    iota(U(11), [[1, 16], [0, 16]], 2, 0)
    for c in range(4):
        ts(U(c), U(11), c + 1.0, 13.0, OP.add, OP.max)
    ts(U(0, 4), U(0, 4), 17.0, None, OP.min)
    ms(A("ohw", 8192 + 960, 8192 + 976), 16.0)
    for c in range(4):
        keep(U(c), U(c), [[0, 128 >> c], [1, 2], [0, 1 << c]], OP.is_gt, 17.0, 0, 0)
    for c in range(4):
        x = A(("PZ", "PT")[c // 2], 256 * (c % 2), 256 * (c % 2) + 256)
        mm(x, [(A("idn"), U(z)) for z in range(c + 1)])
        ts(U(4 + c), x, C(1), 17.0 * (c + 1), OP.add, OP.is_ge)
    x = A("ohw", 8192 + 704, 8192 + 720)
    ts(x, x, -2.0, None, OP.add)
    mm(A("PZ"), [(A("idn"), U(0, 2))])
    mm(A("PT", 0, 256), [(A("idn"), U(2))])
    tt(U(8, 2), U(4, 2), A("PZ"), OP.mult)
    tt(U(10), U(6), A("PT", 0, 256), OP.mult)
    mm(A("PT", 256, 512), [(A("idn"), U(z)) for z in range(8, 12)] + [(A("i128"), U(7))])
    ts(U(0), A("PT", 256, 512), C(1), 64.0, OP.add, OP.min)
    ops[dma(T.ld[:, 0:16, :], T.nil[:], [("nil", 0, 256)], [("ld", 0, 1)])]["soon"] = LATE[1]
    dma(T.ld[:, 16:32, :], U(0)[0], [U(0)[1]], [("ld", 1, 2)])
    k = None
    for s in range(16):
        z = dma(T.lut[:, 256 * s:256 * s + 256], T.ld[:, 16 - s:32 - s, :], [("ld", 0, 2)], [("lut", 0, 4096)], twin=k)
        k = z if k is None else k
    ms(A("lut", 4096, 4104), 0.0)

    for k in range(16):
        keep(A("sel", 128 * k, 128 * k + 128), A("one"), GR, OP.is_equal, 0.0, -k, 1)
    ms(A("labx", p1=32), 1.0)
    k = dma(T.di[0:8, :], T.lab[:], [], [("di", 0, 512)], 4, few=True)
    dma(T.di[32:40, :], T.ask[:], [], [("dia", 0, 512)], 4, twin=k, few=True)
    ts(A("labx", p1=8), A("di", p1=8), -1.0, 1.0, OP.mult, OP.add)
    cp(A("askb", p0=32, p1=40), A("dia", p0=32, p1=40))
    for j in range(4):
        mm(A("PS0", 8 * j, 8 * j + 8), [(A("labx", 128 * j, 128 * j + 128, p1=8), A("idn", 0, 8, p1=8))])
    ev(A("fab"), A("PS0", 0, 32), -2049.0, 2048.0)

    def wide(nm, h, k):
        return A(nm, 2048 * h + k, 2048 * h + 2048, 16)

    def who(nm, h, s):
        return "V" if "%s%d%d" % (nm, h, s // QG) in ONV[side[1]].split() else REST

    def gather(nm, h, win, lst, a):
        for s in range(0, 2048, QG):
            gat(A(nm, 2048 * h + s, 2048 * h + s + QG), A(win), A(lst, a + s // 16, a + (s + QG) // 16), GN, who(nm, h, s))

    def strong(h, d, win, thr, lst, a):
        for s in range(0, 2048, QG):
            gge(A("ge", 2048 * h + s, 2048 * h + s + QG), A(win), A(lst, a + s // 16, a + (s + QG) // 16), thr, d,
                who("s%d" % d, h, s))
        x = A("PX%d" % h, 0, 128)
        mm(x, [(BIG(0, k), wide("ge", h, k)) for k in range(16)])
        gt(A("st", 384 * h + 128 * d, 384 * h + 128 * d + 128), x, 0.5, eng=PLAIN[1])

    def names(t, h, d):
        Y = ("PY%d" if d else "PX%d") % h
        c = lambda nm, j=0, w=1: A(nm, 128 * (w * h + j), 128 * (w * h + j) + 128)
        tt(A(Y, 128, 256), c("ls"), A(Y, 128, 256), OP.mult)
        tt(c("ti"), c("uu"), A(Y, 128, 256), OP.add)
        ts(c("li"), c("ti"), 5, NW - 1, OP.arith_shift_right, OP.bitwise_and)
        lu = c("lu%d" % (t % 2), d, 2)
        cp(lu, c("li"))
        if d == 0 or t < EP - 1:
            ts(c("dh", d, 2), lu, 1.0 / 128, 143.50390625, OP.mult, OP.add)
            ts(c("li"), c("ti"), 5, 127, OP.arith_shift_right, OP.bitwise_and)
            cp(c("dl", d, 2), c("li"))

    def second(t, h):
        X, Y = "PX%d" % h, "PY%d" % h
        c = lambda nm, j=0, w=1: A(nm, 128 * (w * h + j), 128 * (w * h + j) + 128)
        mm(A(X, 128, 256), [(A("tri", 0, 128), c("st", 0, 3))])
        ev(c("endb"), A(X, 128, 256))
        a = 2048 * h
        for j, th in enumerate((0.5, 4.5, 8.5, 12.5)):
            gt(A("ge", a + j, a + 512, 4, own=(a + 128 * j, a + 128 * j + 128)), c("endb"), th, False)
        gt(A("ge", a + 512, a + 640), c("endb"), 15.5, False)
        mm(A(X, 0, 40), [(BIG(3, b), A("ge", a + b, a + 640, 16, own=(a, a + 640))) for b in range(16)]
           + [(A("idn"), A("eo", 40 * h, 40 * h + 40))])
        o = A("o1", 128 * h, 128 * h + 40)
        cp(o, A(X, 0, 40))
        gat(A("g1o", a, a + 640), A("bw0"), o)
        gp = lambda j: A("g1o", a + j, a + 512, 4) if j < 4 else A("g1o", a + 512, a + 640)
        for m in range(3):
            mm(A(X if m == 1 else Y, 128 * m, 128 * m + 128), [(MAT(m, j), gp(j)) for j in range(5)])
        ev(c("l2"), A(Y, 256, 384))
        ts(A(Y, 256, 384), A(Y, 256, 384), -15.0, -4.0, OP.add, OP.max)
        ev(c("ls"), A(Y, 0, 128), 1.0, 3232.0, relu=True)
        ts(c("uu"), A(Y, 0, 128), -4033.0, 2080.0, OP.max, OP.mult)
        names(t, h, 0)
        w, k = "dw%d" % h, None
        for j, src in ((0, c("dh", 0, 2)), (1, c("dl", 0, 2))):
            z = dma(T[w][8 * j:128:16, 0:2048], src[0], [src[1]], [(w, 0, 2048)], twin=k, few=True)
            k = z if k is None else k
        x = A("PS%d" % h, 0, 40)
        mm(x, [(BIG(1, b), A("g1o", a + b, a + 640, 16)) for b in range(16)])
        ts(A("pl", 40 * h, 40 * h + 40), x, 2048.0, None, OP.add)

    def third(t, h):
        X, Y = "PX%d" % h, "PY%d" % h
        c = lambda nm, j=0, w=1: A(nm, 128 * (w * h + j), 128 * (w * h + j) + 128)
        tt(c("nb"), c("st", 1, 3), A(Y, 256, 384), OP.mult)
        ts(c("endb"), c("nb"), -0.5, None, OP.is_lt)
        mm(A(X, 0, 32), [((T.ma[:, 3 + m, 12 - 4 * q:140 - 4 * q], ("ma", 0, 144)), A(nm, 128 * h + q, 128 * h + 128, 4))
                         for m, nm in ((1, "l2"), (0, "nb"), (2, "endb")) for q in range(4)])
        o = A("o2", 128 * h, 128 * h + 32)
        ts(o, A(X, 0, 32), -16.0, 4096.0, OP.add, OP.min)
        a = 2048 * h
        gat(A("ge", a, a + 512), A("lut"), o)
        four = [(A("idn"), A("ge", a + j, a + 512, 4)) for j in range(4)]
        mm(A(X, 128, 256), four)
        ev(c("kb"), A(X, 128, 256), 1.0 / 16, 143.53125)
        mm(A(X, 256, 384), [(A("idn"), A("eio", 0, 128)), (A("i128"), c("kb"))])
        ts(c("o1"), A(X, 256, 384), -18432.0, None, OP.add)
        gather("g1o", h, "dw%d" % h, "o1", 128 * h)
        mm(A(Y, 256, 384), four + [(A("idn"), c("es2")), (A("in16"), c("kb"))])
        ts(c("o2"), A(Y, 256, 384), 2304.0, 256.0, OP.add, OP.mult)
        gather("ge", h, "bw0", "o2", 128 * h)
        mm(A(Y, 384, 512), [(A("idn"), c("kb")), (A("idn"), A("e16"))])
        ts(c("par%d" % (t % 2)), A(Y, 384, 512), -144.0, None, OP.add)
        mm(A(Y, 0, 128), [(BIG(2, k), wide("g1o", h, k)) for k in range(16)])
        ev(c("ls"), A(Y, 0, 128), 1.0, 3232.0, relu=True)
        ev(c("uu"), A(Y, 0, 128), 2080.0)
        mm(A(Y, 128, 256), [(BIG(1, k), wide("ge", h, k)) for k in range(16)])
        names(t, h, 1)

    def marks(t, h, d, hi, lo):
        Y, S = "PY%d" % h, "PS%d" % h
        mm(A(Y, 384, 400), [(lo, A("selu"))])
        a = 48 * h + 16 * d
        ev(A("lot", a, a + 16), A(Y, 384, 400), *((1.0, 0.0) if d else (-512.0, 256.0)))
        for j in range(16):
            o, col = A("ohw", 128 * (a + j), 128 * (a + j) + 128), A("lot", a + j, a + j + 1)
            if d:
                ts(o, A("eio", 0, 128), col, None, OP.is_equal)
            else:
                step(o, col, SIDE)
        e0, k = 256 * t + 128 * h, 10 if d else 9
        mm(A(S), [(hi, A("rep")), (A("labx", e0, e0 + 128, p1=k), A("rx", p1=k))])
        ev((T["xs%d" % h][:, d, :], ("xs%d" % h, 8 * d, 8 * d + 8)), A(S), lean=FAR)

    def total(src, a, h, r, left, narrow=False):
        if narrow:
            for k in range(0, 16, 4):
                mm(A("PZ", 128 * h + r // 16, 128 * h + 64 + r // 16), [(A("idf"), A(src, a + z, a + 1024, 16)) for z in range(k, k + 4)],
                   first=False, left=left)
        elif r:
            for k in range(0, 16, 2):
                mm(A("PZ", 128 * h, 128 * h + 128), [(A("idf"), A(src, a - 1024 + z, a + 1024, 16)) for z in range(k, k + 2)],
                   first=False, left=left)

    def values12(t, h, left):
        first = A("v1p", 0, 2048, 4)
        gat(first, A("fa"), A("pl", 40 * h, 40 * h + 32), FAR)
        gat(A("p5"), A("fa"), A("pl", 40 * h + 32, 40 * h + 40), FAR)
        for k in range(1, 4):
            keep(A("vc", k, 2048, 4, own=(k, k + 1)), first, [[0, 512]], OP.is_ge, 0.0, 0, 0)
        keep(A("vc", 15, 2048, 16, own=(3, 4)), A("p5"), [[0, 128]], OP.is_ge, 0.0, 0, 0)
        how = ONE[t][h]
        for s in range(0, 2048, QV):
            a, b = s // 16, (s + QV) // 16
            l1 = A("l1u", 256 * t + 128 * h + a, 256 * t + 128 * h + b)
            l2 = A("lu%d" % (t % 2), 256 * h + a, 256 * h + b)
            x = A("t2", 2048 * h + s, 2048 * h + s + QV)
            gmul(A("v2%d" % h, s, s + QV), A("fa"), l2, A("v1p", s, s + QV), more=[("vc", 1, 4)])
            if how == "first":
                gat(x, A("fw1"), l1, FAR)
            gmul(A("t1", s, s + QV) if how == "first" else x, A("w2%d" % (t % 2)), l2, A("v2%d" % h, s, s + QV))
            if how == "on":
                gmul(x, A("fw1"), l1, x, OP.add)
            elif how != "first":
                gat(A("t1", s, s + QV), A("fw1"), l1, FAR)
            if (s + QV) % PW == 0 and how in ("first", "dma"):
                plus(2048 * h + s + QV - PW, "t1", s + QV - PW)
        if how == "pe":
            total("t1", 1024, h, 1024, left)
        if PE3[t][h]:
            total("t2", 2048 * h + 1024, h, 1024, left)

    def plus(r, nm, a):
        o, x = A("t2", r, r + PW), A(nm, a, a + PW)
        k = add("G", lambda q, e: [q.dma_start(o[0], x[0], accum_op=OP.add)], [x[1], o[1]], [o[1]], 900,
                DM + 300 + 2 * span(o[0], x[0], 4), kind="d", big=2 * span(o[0], x[0], 4))
        ops[k]["sem"] = [sem(), 16]

    def values3(t, h, left):
        end = t == EP - 1 and h == 1
        for s in range(0, 2048, QV):
            a, b = s // 16, (s + QV) // 16
            l3 = A("lu%d" % (t % 2), 256 * h + 128 + a, 256 * h + 128 + b)
            r = s - s % 1024
            nm = "t1" if h else "t3"
            x = A(nm, s, s + QV)
            gat(x, A("v2%d" % h), A("par%d" % (t % 2), 128 * h + a, 128 * h + b), FAR)
            gmul(x, A("fw3"), l3, x)
            if (s + QV) % 1024 == 0 and end and r >= 2048 - SCAN:
                o, x, m = A("ys2", r, r + 1024), A(nm, r, r + 1024), A("ohw", 0, 1024)
                add("V", lambda q, e, o=o, x=x, m=m: [q.tensor_tensor_scan(o[0], m[0], x[0], 0.0, OP.mult, OP.add)],
                    [x[1], m[1]], [o[1]], cost(o, x))
            elif (s + QV) % 1024 == 0 and PE3[t][h]:
                total(nm, r, h, r, left, end)
            elif (s + QV) % PW == 0 and not PE3[t][h]:
                plus(2048 * h + s + QV - PW, nm, s + QV - PW)
        if not PE3[t][h]:
            total("t2", 2048 * h + 1024, h, 1024, left)
        if h == 1:
            if end and SCAN:
                z = (A("PZ", 256 - SCAN // 16, 256)[0], ("PZ", 0, 256))
                tt(z, A("ys2", 2048 - SCAN + 15, 2048, 16), z, OP.add)
            tt(A("ys"), A("xvs"), A("PZ", 0, 256), OP.mult)
            dma(T.y[:, 256 * t:256 * t + 256], T.ys[:], [("ys", 0, 256)], [], 4)

    def products(v):
        for j in range(8):
            P, c = ("PS0", "PS1")[j % 2], (512 * j, 512 * j + 512)
            mm(A(P), [(A("idn"), A("fa", *c))])
            tt(A("fw1", *c), A("w1", *c), A(P), OP.mult)
        for k in range(2):
            a, slot = 2048 * k, 2 * v + k
            send([(-2, A("fw1", a, a + 2048), (T.fd[slot], ("fd", slot, slot + 1)))], 8192)
            j = dma(T.fw3[0:112, a:a + 2048], T.fd[slot, 16:128, :], [("fd", slot, slot + 1)], [("fw3", a, a + 2048)], 4)
            dma(T.fw3[112:128, a:a + 2048], T.fd[slot, 0:16, :], [("fd", slot, slot + 1)], [("fw3", a, a + 2048)], 4, twin=j)

    def hot(h, d, gr, u):
        a = 128 * (48 * h + 16 * d + 2 * gr + u)
        return (A("ohw", a, a + 128), (T["xs%d" % h][:, d, 64 * gr + 32 * u:64 * gr + 32 * u + 32], ("xs%d" % h, 8 * d + gr, 8 * d + gr + 1)))

    products(0)
    side[3] = 1
    for t in range(EP):
        last = t == EP - 1
        side[1] = t
        ops[dma(T.xvs[:], T.xv[:, 256 * t:256 * t + 256], [], [("xvs", 0, 256)])]["soon"] = LATE[2]
        if last:
            iota(A("ohw", 0, 1024), [[0, 1024]], 1, 0)
            keep(A("ohw", 0, 1024), A("ohw", 0, 1024), [[0, 64], [1, 16]], OP.not_equal, 0.0, 0, 0)
        for h in range(2):
            strong(h, 0, "wu" if t else "w1", "th", "l1u", 256 * t + 128 * h)
        for h in range(2):
            second(t, h)
        if not last:
            left = [0]
            mm(A("PT"), [(A("nil", 0, 128, p1=1), A("rep", p1=1))], left=left)
        for h in range(2):
            e0 = 256 * t + 128 * h
            if not last:
                marks(t, h, 0, BD(t, 0, 128 * h, 128 * h + 128), BD(t, 1, 128 * h, 128 * h + 128))
            strong(h, 1, "w2%d" % (t % 2), "th2", "lu%d" % (t % 2), 256 * h)
            if not last:
                marks(t, h, 1, A("dh", 256 * h, 256 * h + 128), A("dl", 256 * h, 256 * h + 128))
            third(t, h)
            if not last:
                marks(t, h, 2, A("dh", 256 * h + 128, 256 * h + 256), A("dl", 256 * h + 128, 256 * h + 256))
            strong(h, 2, "w3", "th3", "lu%d" % (t % 2), 256 * h + 128)
            sts = [A("st", 384 * h + 128 * d, 384 * h + 128 * d + 128) for d in range(3)]
            if not last:
                x = A("PX%d" % h, 128, 136)
                mm(x, [(s, A("g8")) for s in sts] + [(A("askb", e0, e0 + 128, p0=32, p1=40), A("ni8", p0=32, p1=40))])
                ts(A("fl", 8 * h, 8 * h + 8), x, -0.5, 64.0, OP.is_gt, OP.mult)
                for gr in range(8):
                    x = (T["xs%d" % h][:, :, 64 * gr:64 * gr + 64], None)
                    fg, wt = A("fl", 8 * h + gr, 8 * h + gr + 1), A("fab", 16 * t + 8 * h + gr, 16 * t + 8 * h + gr + 1)
                    reg = [("xs%d" % h, 8 * d + gr, 8 * d + gr + 1) for d in range(3)]
                    add("V", lambda q, e, x=x, fg=fg, wt=wt: [q.tensor_scalar(x[0], x[0], fg[0], wt[0], OP.is_equal, OP.mult)],
                        reg + [fg[1], wt[1]], reg, OV + 96 * CY)
                    for d in (1, 2):
                        b = 256 * (d - 1) + 32 * ((gr + (d == 2)) % 8)
                        mm(A("PT", b, b + 32), [hot(h, d, gr, u) for u in range(2)], first=False, left=left)
            y8 = A("PX%d" % h, 256, 384, p1=8)
            mm(y8, [(A("g8"), s) for s in sts])
            ev(A("cvs", 128 * h, 128 * h + 128, p1=8), y8)
            if h == 1:
                dma(T.cv[:, 256 * t:256 * t + 256], T.cvs[0:8, :], [("cvs", 0, 256)], [], 4, few=True)
            side[0] = 1
            if h == 0:
                lz = [0]
                mm(A("PZ", 0, 256), [(A("nil", 0, 128, p1=1), A("rep", 0, 256, p1=1))], left=lz)
            side[2] = ROOM[t][h][0]
            values12(t, h, lz)
            side[2] = ROOM[t][h][1]
            values3(t, h, lz)
            side[0], side[2] = 0, 0.0
        if last:
            break
        window(t + 1)
        o = 0
        ev(A("cs"), A("PT"))
        for gr in range(8):
            mm(A("PS0", 32 * gr, 32 * gr + 32), [hot(h, 0, gr, u) for h in range(2) for u in range(2)])
        ev(A("c0"), A("PS0", 0, 256))
        send([(1, A("cs", o, o + 256), A("cin", o, o + 256)), (2, A("cs", o + 256, o + 512), A("cin", o + 256, o + 512))],
             512, wr=[("w2%d" % ((t + 1) % 2), 0, NW)])
        for b in range(2):
            x = A("PX%d" % b, 0, 128)
            mm(x, [(A("one", p1=1), A("one", p1=1)), (A("c0", b, 256, 2), A("dff"))], final=False, wr=[A("PX%d" % b)[1]])
            mm(x, [(A("cin", o + b, o + 256, 2), A("idn")), (A("cin", o + 256 + b, o + 512, 2), A("idn"))], first=False)
            ts(A("fct", 128 * b, 128 * b + 128), x, 0.5, 2.0, OP.max, OP.min)
        for j in range(8):
            P = ("PY0", "PS0", "PY1", "PS1")[j % 4]
            for b in range(2):
                mm(A(P, 256 * b, 256 * b + 256), [(A("sel", 128 * (2 * j + b), 128 * (2 * j + b + 1)), A("fct"))])
            tt(A("wu", 512 * j, 512 * j + 512), A("w1", 512 * j, 512 * j + 512), A(P), OP.mult)
            if j % 2 == 1:
                z = (512 * j - 512, min(512 * j + 512, NW - 1))
                ts(A("w1", *z), A("wu", *z), 0.25, 4.0, OP.max, OP.min)
            if j % 4 == 3:
                send_w(t + 1, j // 4)
        products(t + 1)
    return ops


def after(row, t):
    a, b = 0, len(row)
    while a < b:
        m = (a + b) // 2
        if row[m][1] > t:
            b = m
        else:
            a = m + 1
    return a


def digest(ops, pred):
    return [([j for j, s in pred[i] if not s], [j for j, s in pred[i] if s], o["banks"], o["occ"], o["ga"], o["lag"], o["big"])
            for i, o in enumerate(ops)]


def walk(seq, eng, steps, pace, why=None):
    pg, po, pp, pd, div, ph, pb = pace
    hop = HOP * ph
    free, last, line = {}, {}, []
    end = [0.0] * len(steps)
    top = 0.0
    for i in seq:
        hard, soft, banks, occ, ga, lag, big = steps[i]
        e = eng[i]
        t, w = free.get(e, 0.0), -1
        for j in hard:
            if end[j] > t:
                t, w = end[j], j
        for j in soft:
            if eng[j] != e and end[j] > t:
                t, w = end[j], j
        for b in banks:
            j = last.get(b, i)
            if eng[j] != e and end[j] > t:
                t, w = end[j], -2 - j
            last[b] = i
        if why is not None:
            why[i] = (w, last.get(e))
            last[e] = i
        c = t + occ[e] * (pg if ga else pp if e == "P" else po)
        x = c + lag * pd
        if big:
            s, d = c + 1000.0 * pd, big * pb
            k = after(line, s)
            while k < len(line) and line[k][0] < s + d:
                s, k = line[k][1], k + 1
            line.insert(k, (s, s + d))
            x = max(x, s + d + 700.0 * pd)
        if e != " ":
            free[e] = c
        if x >= top:
            top, tail = x, i
        end[i] = x + hop
    if why is not None:
        why[-1] = tail
    return top / div


def replay(ops, at, pred, pace):
    return walk(sorted(at, key=lambda i: (at[i][0], i)), [at[i][1] for i in range(len(ops))], digest(ops, pred), pace)


def place(ops, order, before, back, f):
    busy, at = {}, {}
    for i in order if back else sorted(order, key=lambda i: ops[i].get("fix", 1e9)):
        o = ops[i]
        best = None
        if "fix" in o and not back:
            row = busy.setdefault("D", [])
            t = row[-1][1] if row else 0.0
            row.append((t, t + o["big"]))
            at[i] = (o["fix"], o["eng"], t + o["lag"])
            continue
        off = o["lag"] if back else 0.0
        for e in o["eng"] or " ":
            t = max([at[j][2] + (-o["lag"] if soft and at[j][1] == e else HOP) for j, soft in before[i]]
                    + [o["room"] if back else o["soon"]]) + off
            occ = o["occ"][e] * f[i]
            res = [] if e == " " else [(e, occ)] + [(b, occ + (0 if b in OWN else BANK)) for b in o["banks"]]
            if o["big"] > 100:
                res.append(("D", o["big"]))
            moved = True
            while moved:
                moved = False
                for r, d in res:
                    row = busy.setdefault(r, [])
                    k = after(row, t)
                    while k < len(row) and row[k][0] < t + d:
                        t, moved, k = row[k][1], len(res) > 1, k + 1
            if best is None or t + occ + o["lean"] < best[0] + best[3]:
                best = (t, e, res, occ)
        at[i] = (best[0] - off, best[1], best[0] - off + best[3] + o["lag"])
        for r, d in best[2]:
            busy[r].insert(after(busy[r], best[0]), (best[0], best[0] + d))
    return at


def refine(ops, at, pred, succ):
    n, Q, k = len(ops), "VAPGS ", len(TRIED)
    steps = digest(ops, pred)
    seq = sorted(range(n), key=lambda i: (at[i][0], i))
    eng = [at[i][1] for i in range(n)]
    hard = []
    for i in range(n):
        h = set(steps[i][0])
        for j in list(h):
            h -= set(steps[j][0])
        hard.append(sorted(h))
    cnt = np.array([len(h) for h in hard])
    pre = np.full((n, int(cnt.max())), n)
    names = sorted(set(b for o in ops for b in o["banks"]))
    nb = len(names)
    bank = np.full((n, 2), nb)
    occ = np.zeros((k, n, 6))
    for i, o in enumerate(ops):
        pre[i, :len(hard[i])] = hard[i]
        bank[i, :len(o["banks"])] = [names.index(b) for b in o["banks"]]
        for e, c in o["occ"].items():
            occ[:, i, Q.index(e)] = [c * (p[0] if o["ga"] else p[2] if e == "P" else p[1]) for p in TRIED]
    lag, big = np.array([o["lag"] for o in ops]), np.array([o["big"] for o in ops])
    x = [99]

    def pick(z):
        x[0] = (x[0] * 1103515245 + 12345) % 2147483648
        return (x[0] >> 8) % z

    def marks(cands):
        B = len(cands) * k
        S = np.repeat(np.array([s for s, e in cands]), k, 0).T.copy()
        E = np.repeat(np.array([[Q.index(z) for z in e] for s, e in cands]), k, 0)
        E = np.take_along_axis(E, S.T, 1).T.copy()
        ar, pi = np.arange(B), np.tile(np.arange(k), len(cands))
        pd, ph, pb, div = [np.array([p[z] for p in TRIED])[pi] for z in (3, 5, 6, 4)]
        OCC, LAG, BIG = occ[pi[None, :], S, E], lag[S] * pd + HOP * ph, big[S] * pb
        b0, b1 = bank[S, 0], bank[S, 1]
        anyb, top, use0, use1 = BIG.max(1) > 0, cnt[S].max(1), b0.min(1) < nb, b1.min(1) < nb
        end, free, line = np.zeros((n + 1) * B), np.zeros(6 * B), np.zeros(B)
        bend, beng = np.zeros((nb + 1) * B), np.zeros((nb + 1) * B, int)
        SI, EI, B0, B1 = S * B + ar, E * B + ar, b0 * B + ar, b1 * B + ar
        d0, d1 = 1000.0 * pd, 700.0 * pd + HOP * ph
        for p in range(n):
            ei = EI[p]
            t = free[ei]
            if top[p]:
                t = np.maximum(t, end[pre[S[p], :top[p]].T * B + ar].max(0))
            if use0[p]:
                t = np.maximum(t, bend[B0[p]] * (beng[B0[p]] != ei))
            if use1[p]:
                t = np.maximum(t, bend[B1[p]] * (beng[B1[p]] != ei))
            t += OCC[p]
            free[ei] = t
            free[5 * B:] = 0.0
            y = t + LAG[p]
            if anyb[p]:
                on = BIG[p] > 0
                line = np.where(on, np.maximum(line, t + d0) + BIG[p], line)
                y = np.where(on, np.maximum(y, line + d1), y)
            end[SI[p]] = y
            if use0[p]:
                bend[B0[p]], beng[B0[p]] = y, ei
                if use1[p]:
                    bend[B1[p]], beng[B1[p]] = y, ei
                bend[nb * B:] = 0.0
        end = end.reshape(n + 1, B)[:n]
        return ((end.max(0) + EARLY * end.mean(0)) / div).reshape(-1, k).sum(1), end - LAG[np.argsort(S, 0), ar]

    def moved(s, e, mv):
        i, to, q, a, grp = mv
        if to < a:
            s = s[:to] + list(grp) + [j for j in s[to:a + 1] if j not in grp] + s[a + 1:]
        else:
            s = s[:a] + [j for j in s[a:to + 1] if j not in grp] + list(grp) + s[to + 1:]
        e = list(e)
        e[i] = q
        return s, e

    def timed(s, e, st):
        key, last = {}, {}
        for z, i in enumerate(s):
            on = [b for b in [e[i]] + ops[i]["banks"] if b != " "]
            key[i] = (max([st[i]] + [key[j][0] for j, soft in pred[i]] + [last[b] for b in on if b in last]), z)
            last.update((b, key[i][0]) for b in on)
        return sorted(s, key=lambda i: key[i])

    mark = marks([(seq, eng)])[0][0]
    best, late = (mark, seq, eng), {}
    for r in range(ROUNDS):
        pos = [0] * n
        for z, j in enumerate(seq):
            pos[j] = z
        runs = []
        for p in TRIED:
            why = {}
            walk(seq, eng, steps, p, why)
            u, i = [why[-1]], why[-1]
            while why[i] != (-1, None):
                w, q = why[i]
                if w < 0:
                    i = q if w == -1 else -2 - w
                    u.append(i)
                else:
                    runs.append(u[::-1])
                    i, u = w, [w]
            runs.append(u[::-1])
        runs = [u for u in runs if len(u) > 1 for z in range(1 + len(u) // 6)]
        mvs = set()
        for z in range(3 * WIDE):
            u = runs[pick(len(runs))]
            a = pick(len(u))
            i, how = u[a], pick(6)
            if how == 5:
                i = seq[min(n - 1, max(0, pos[i] + pick(41) - 20))]
            q = eng[i]
            if how == 0 and len(ops[i]["eng"]) == 2:
                q = ops[i]["eng"].replace(q, "")
                to = pos[i] + pick(21) - 12
            elif how < 3 and a > 0:
                to = pos[u[max(0, a - 1 - pick(8))]]
            elif how < 5 and a < len(u) - 1:
                to = pos[u[min(len(u) - 1, a + 1 + pick(8))]]
            else:
                to = pos[i] + pick(61) - 30
            if pick(3) == 0:
                to += (to - pos[i]) * pick(4)
            to, grp = min(n - 1, max(5, to)), [i]
            for j in grp:
                grp += [y for y, s in (pred if to < pos[i] else succ)[j] if min(to, pos[i]) <= pos[y] <= max(to, pos[i]) and y not in grp]
                if len(grp) > 14:
                    lo, hi = max([0] + [pos[y] + 1 for y, s in pred[i]]), min([n - 1] + [pos[y] - 1 for y, s in succ[i]])
                    to, grp = min(hi, max(lo, to)), [i]
                    break
            if "fix" not in ops[i] and to > 4 and (to != pos[i] or q != eng[i]) and len(mvs) < WIDE:
                mvs.add((i, to, q, pos[i], tuple(sorted(grp, key=lambda j: pos[j]))))
        mvs = sorted(mvs)
        got = marks([moved(seq, eng, mv) for mv in mvs])[0]
        good = [mvs[z] for z in np.argsort(got) if got[z] < mark - 1.0]
        if not good:
            good = [mvs[z] for z in np.argsort(got) if r - late.get(mvs[z][0], -99) > 30][:1 + pick(3)]
        late.update((mv[0], r) for mv in good[:3])
        cands, cur, spans = [], (seq, eng), []
        for mv in good:
            a, b = min(pos[mv[0]], mv[1]), max(pos[mv[0]], mv[1])
            if all(b < c - 1 or a > d + 1 for c, d in spans) and len(cands) < 16:
                spans.append((a, b))
                cur = moved(cur[0], cur[1], mv)
                cands.append(cur)
        if not cands:
            continue
        got, ends = marks(cands)
        z = int(np.argmin(got)) if min(got) < mark else len(cands) - 1
        (seq, eng), mark = cands[z], got[z]
        if r % 4 == 3:
            seq = timed(seq, eng, ends[:, z * k:z * k + k].sum(1))
            mark = marks([(seq, eng)])[0][0]
        if mark < best[0]:
            best = (mark, seq, eng)
    return best


KEPT = []


def plan(ops):
    n = len(ops)
    twins = {}
    for i, o in enumerate(ops):
        if "sem" in o:
            twins.setdefault(o["sem"][0], []).append(i)
    for o in ops:
        for j in list(o["deps"]):
            if "sem" in ops[j]:
                o["deps"].update((k, True) for k in twins[ops[j]["sem"][0]])
    pred = [[(j, not hard) for j, hard in o["deps"].items()] for o in ops]
    succ = [[] for _ in ops]
    up = [0.0] * n
    for i in range(n - 1, -1, -1):
        up[i] += min(ops[i]["occ"].values()) + ops[i]["lag"]
        for j, soft in pred[i]:
            up[j] = max(up[j], up[i] + HOP)
            succ[j].append((i, soft))
    best, x, even = None, 12345, [1.0] * n
    at = place(ops, sorted(range(n), key=lambda i: (-up[i], i)), pred, False, even)
    if KEPT:
        best = KEPT[0]
    for k in range(0 if KEPT else PASSES):
        mark = sum(replay(ops, at, pred, pace) for pace in PACES)
        if best is None or mark < best[0]:
            best = (mark, at)
        if k % 8 == 7:
            at = best[1]
        f = []
        for i in range(n):
            x = (x * 1103515245 + 12345) % 2147483648
            f.append(1 + SHAKE * (x / 1073741824.0 - 1))
        bk = place(ops, sorted(range(n), key=lambda i: (-at[i][2], -i)), succ, True, f)
        at = place(ops, sorted(range(n), key=lambda i: (-bk[i][2], i)), pred, False, even)
    if not KEPT and ROUNDS:
        mark, seq, eng = refine(ops, best[1], pred, succ)
        best = (mark, dict((i, (k, eng[i], k)) for k, i in enumerate(seq)))
    KEPT[:] = [best]
    for i in range(n):
        ops[i]["t"], ops[i]["e"], ops[i]["end"] = best[1][i]
    order = sorted(range(n), key=lambda i: (ops[i]["t"], i))
    prev = {}
    for i in order:
        for b in ops[i]["banks"]:
            if b in prev:
                ops[i]["deps"].setdefault(prev[b], False)
            prev[b] = i
    return order


def rank_program(g, core, T, topo):
    if T.rank_of(core) is None:
        return
    ops = build(g, core, T, topo)
    order = plan(ops)
    Q = {"V": g.vector, "A": g.scalar, "P": g.tensor, "G": g, "S": g.sync}
    cnt = dict((e, 0) for e in "VAPG")
    seen = dict((e, {}) for e in Q)
    total = {}
    for i in order:
        o = ops[i]
        e = o["e"]
        if o["kind"] != "a":
            need = {}
            for j, hard in o["deps"].items():
                if hard or ops[j]["e"] != e:
                    s, v = ops[j]["tok"]
                    need[s] = max(need.get(s, 0), v)
            for s, v in need.items():
                if seen[e].get(s, 0) < v:
                    Q[e].wait_ge(T.sem[s], v)
                    seen[e][s] = v
            ins = o["fn"](Q[e], e)
            if o["kind"] == "c":
                ins[-1].then_inc(T.sem["c" + e], 1)
                cnt[e] += 1
                o["tok"] = ("c" + e, cnt[e])
            elif o["kind"] == "d":
                ins[0].then_inc(T.sem[o["sem"][0]], 16)
                o["tok"] = tuple(o["sem"])
        s, v = o["tok"]
        total[s] = max(total.get(s, 0), v)
    for s, v in total.items():
        if not any(seen[e].get(s, 0) >= v for e in seen):
            g.sync.wait_ge(T.sem[s], v)
